import numpy as np
import ml_dtypes


def mxq(x, axis, fmt="e4m3"):
    dtype, down = {"e4m3": (ml_dtypes.float8_e4m3fn, 7), "e5m2": (ml_dtypes.float8_e5m2, 14)}[fmt]
    v = np.moveaxis(np.asarray(x, np.float32).astype(ml_dtypes.bfloat16).astype(np.float64), axis, -1)
    blocks = v.reshape(v.shape[:-1] + (-1, 32))
    amax = np.abs(blocks).max(-1, keepdims=True)
    byte = np.maximum(np.where(amax > 0, np.frexp(amax)[1] - 1 + 127, 0) - down, 1)
    scale = np.exp2(byte - 127.0)
    codes = (blocks / scale).astype(np.float32).astype(dtype).astype(np.float64)
    return np.moveaxis((codes * scale).reshape(v.shape), -1, axis)


WIDE = False


def mx_kscale(k):
    if not WIDE:
        return np.ones(k)
    levels = np.array([30, -30])
    if k % 512:
        return np.exp2(np.random.permutation(np.resize(levels, k // 32))).repeat(32)
    a = np.empty((k // 512, 16))
    for p in range(k // 512):
        a[p, :8] = np.random.permutation(np.resize(levels, 8))
        for g in range(8):
            far = levels[np.abs(levels - a[p, g]) >= 10]
            a[p, g + 8] = far[np.random.randint(len(far))]
    return np.exp2(a.ravel()).repeat(32)


def f64(x):
    return np.asarray(x).astype(np.float64)


def striped(idx):
    return np.tile(idx.reshape(-1, 16).T, (8, 1)).astype(np.uint16)


def unstriped(offs):
    return offs[:16].T.reshape(-1).astype(np.int64)


E2M1 = np.array([0.0, 0.5, 1.0, 1.5, 2.0, 3.0, 4.0, 6.0, -0.0, -0.5, -1.0, -1.5, -2.0, -3.0, -4.0, -6.0])


def pack_weight(w, fmt):
    k, n = w.shape
    w = f64(np.asarray(w, np.float32).astype(ml_dtypes.bfloat16)).reshape(k // 32, 32, n)
    amax = np.abs(w).max(1)
    if fmt == "e4m3":
        byte = np.frexp(amax)[1] - 1 + 127 - 7
    else:
        mant, ex = np.frexp(amax / 6.0)
        byte = np.where(mant > 0.5, ex, ex - 1) + 127
    byte = np.clip(np.where(amax > 0, byte, 1), 1, 254)
    scaled = (w * np.exp2(127.0 - byte)[:, None, :]).reshape(k, n).astype(np.float32)
    by_word = np.ascontiguousarray(scaled.reshape(k // 512, 128, 4, n).transpose(0, 1, 3, 2))
    if fmt == "e4m3":
        words = by_word.astype(ml_dtypes.float8_e4m3fn).view(np.uint8)
    else:
        c = by_word.astype(ml_dtypes.float4_e2m1fn).view(np.uint8) & 0xF
        words = (c[..., 0::2] | (c[..., 1::2] << 4)).reshape(k // 512, 128, 2 * n)
    return np.ascontiguousarray(words), np.ascontiguousarray(byte.astype(np.uint8).reshape(k // 512, 16, n))


def unpack_weight(words, scales, fmt):
    g, _, n = scales.shape
    words = np.ascontiguousarray(words).reshape(g, 128, n, -1)
    if fmt == "e4m3":
        vals = words.view(ml_dtypes.float8_e4m3fn).astype(np.float64)
    else:
        nib = np.empty((g, 128, n, 4), np.uint8)
        nib[..., 0::2] = words & 0xF
        nib[..., 1::2] = words >> 4
        vals = E2M1[nib]
    vals = vals * np.repeat(np.exp2(scales.astype(np.float64) - 127.0), 8, axis=1)[..., None]
    return vals.transpose(0, 1, 3, 2).reshape(g * 512, n)


def d_relu2(v):
    return 2.0 * np.maximum(v, 0.0)


K, T, E, C, H, N = 256, 1024, 2, 512, 1024, 1024


def by_expert(wq, xq):
    return np.concatenate([wq[e].T @ xq[:, e * C:(e + 1) * C] for e in range(E)], axis=1)


def setup_inputs():
    n = np.random.standard_normal
    s = mx_kscale(N)[:, None]
    u = mx_kscale(H)
    w2 = [pack_weight(m, "e2m1") for m in n((E, N, H)) / np.sqrt(N) / s[None] * u[None, None, :]]
    w1 = [pack_weight(m, "e2m1") for m in n((E, H, K)) / np.sqrt(H) / u[None, :, None]]
    return {
        "dyT": (n((N, T)) * s).astype(np.float32),
        "a": n((H, E * C)).astype(np.float32),
        "w2_words": np.stack([m[0] for m in w2]),
        "w2_scales": np.stack([m[1] for m in w2]),
        "w1_words": np.stack([m[0] for m in w1]),
        "w1_scales": np.stack([m[1] for m in w1]),
        "gate": np.tile(np.random.uniform(0.2, 1.0, E * C), (N, 1)).astype(np.float32),
        "offs": striped(np.random.permutation(T)[:E * C]),
    }


def reference(dyT, a, w2_words, w2_scales, w1_words, w1_scales, gate, offs):
    idx = unstriped(offs)
    w2 = np.stack([unpack_weight(w2_words[e], w2_scales[e], "e2m1") for e in range(E)])
    w1 = np.stack([unpack_weight(w1_words[e], w1_scales[e], "e2m1") for e in range(E)])
    gq = mxq(f64(gate) * f64(dyT)[:, idx], 0, "e5m2")
    dh = by_expert(w2, gq)
    da = dh * d_relu2(f64(a))
    dx = by_expert(w1, mxq(da, 0, "e5m2"))
    out = np.zeros((K, T))
    out[:, idx] = dx
    return out

@@ -1,0 +1,208 @@
+from contextlib import ExitStack
+
+import concourse.mybir as mybir
+
+K, T, E, C, H, N = 256, 1024, 2, 512, 1024, 1024
+P = 128
+PACK = 4
+PASS = P * PACK
+FLOPS = 2 * E * C * H * (N + K)
+BYTES = 4 * (N * T + H * E * C + K * T + E * C) + E * N * H // 2 + E * H * K // 2 + E * N * H // 32 + E * H * K // 32 + 2 * E * C
+
+F32 = mybir.dt.float32
+BF16 = mybir.dt.bfloat16
+I32 = mybir.dt.int32
+U32 = mybir.dt.uint32
+U16 = mybir.dt.uint16
+U8 = mybir.dt.uint8
+E5M2 = mybir.dt.float8_e5m2_x4
+E2M1 = mybir.dt.float4_e2m1fn_x4
+ALU = mybir.AluOpType
+COPY = mybir.ActivationFunctionType.Copy
+
+
+def tile_moe_bdx_mlp_relu2_kernel(
+    tc, dyT, a, w2_words, w2_scales, w1_words, w1_scales, gate, offs, out
+):
+    nc = tc.nc
+    SN, SI, KT = N // PASS, H // PASS, K // P
+
+
+    with ExitStack() as ctx:
+        held = ctx.enter_context(tc.tile_pool(name="held", bufs=1))
+        psum = ctx.enter_context(tc.psum_pool(name="psum", bufs=1))
+
+        offsets = held.tile([P, E * C // 16], U16, name="offsets")
+        dy_t = [[held.tile([P, T], F32, name=f"dy{s}{t}") for t in range(PACK)] for s in range(SN)]
+        gate_t = [held.tile([P, C], F32, name=f"gate{e}") for e in range(E)]
+        a_t = [[held.tile([P, PACK, C], F32, name=f"a{e}{s}") for s in range(SI)] for e in range(E)]
+        w2_raw = [held.tile([P, SN, 2 * H], U8, name=f"w2r{e}", align_bytes=64) for e in range(E)]
+        w2_p = [held.tile([P, SN, 2 * H], U8, name=f"w2p{e}", align_bytes=64) for e in range(E)]
+        w2s_raw = held.tile([P, H], U8, name="w2sr", align_bytes=64)
+        w2s_p = [held.tile([P, H], U8, name=f"w2sp{j}", align_bytes=64) for j in range(E * SN)]
+        w1_t = held.tile([P, E * SI, 2 * K], U8, name="w1t", align_bytes=64)
+        w1s_t = held.tile([P, E * SI, K], U8, name="w1s", align_bytes=64)
+        win = [held.tile([P, T], F32, name=f"win{k}") for k in range(KT)]
+
+        dy_v = dyT.rearrange("(s p t) c -> s t p c", p=P, t=PACK)
+        a_v = a.rearrange("(s p t) (e c) -> e s p t c", p=P, t=PACK, e=E)
+        w2_v = w2_words.bitcast(I32).rearrange("e s p b -> e p s b")
+        w2s_v = w2_scales.bitcast(I32).rearrange("e s f i -> (e s) f i")
+        w1_v = w1_words.bitcast(I32).rearrange("e s p b -> p (e s) b")
+        w1s_v = w1_scales.bitcast(I32).rearrange("e s f i -> f (e s) i")
+
+        nc.sync.dma_start(offsets[:], offs)
+        nc.vector.memset(w2s_raw[:].bitcast(I32), 0)
+        nc.vector.memset(w1s_t[:].bitcast(I32), 0)
+        for j in range(1, E * SN):
+            nc.gpsimd.memset(w2s_p[j][:].bitcast(I32), 0)
+
+        def load_w2(e):
+            nc.sync.dma_start(w2_raw[e][:].bitcast(I32), w2_v[e])
+
+        load_w2(0)
+        nc.sync.dma_start(gate_t[0][:], gate[0:P, 0:C])
+        for t in range(PACK):
+            nc.sync.dma_start(dy_t[0][t][:], dy_v[0, t])
+        for t in range(PACK):
+            nc.sync.dma_start(dy_t[1][t][:], dy_v[1, t])
+        for q in range(4):
+            nc.sync.dma_start(w2s_raw[32 * q : 32 * q + 16, :].bitcast(I32), w2s_v[:, 4 * q : 4 * q + 4])
+        nc.sync.dma_start(gate_t[1][:], gate[0:P, C : 2 * C])
+        nc.sync.dma_start(w1_t[:].bitcast(I32), w1_v)
+        for q in range(4):
+            nc.sync.dma_start(w1s_t[32 * q : 32 * q + 4, :, :].bitcast(I32), w1s_v[4 * q : 4 * q + 4])
+        for s in range(SI):
+            nc.sync.dma_start(a_t[0][s][:], a_v[0, s])
+        load_w2(1)
+        for s in range(SI):
+            nc.sync.dma_start(a_t[1][s][:], a_v[1, s])
+
+        def permute_w2_words(e):
+            nc.vector.tensor_copy(
+                out=w2_p[e][:].bitcast(U16).rearrange("p n (s t m) -> p (n s) t m", s=SI, t=PACK),
+                in_=w2_raw[e][:].bitcast(U16).rearrange("p n (s m t) -> p (n s) t m", s=SI, t=PACK),
+            )
+
+        def permute_w2_scales():
+            nc.vector.tensor_copy(
+                out=w2s_p[0][:].rearrange("p (s t m) -> p s t m", s=SI, t=PACK),
+                in_=w2s_raw[:].rearrange("p (s m t) -> p s t m", s=SI, t=PACK),
+            )
+            for j in range(1, E * SN):
+                for r in range(4):
+                    nc.sync.dma_start(w2s_p[j][r:P:32, :].bitcast(I32), w2s_p[0][4 * j + r : P : 32, :].bitcast(I32))
+
+        def interleave(dst, src):
+            nc.scalar.copy(
+                out=dst[:].rearrange("p (c i) t -> p c t i", i=4),
+                in_=src[:].rearrange("p t (c i) -> p c t i", i=4),
+            )
+
+        def quantize(codes, scales, src):
+            nc.vector.quantize_mx(out=codes[:].bitcast(E5M2), scales=scales[:], in_=src[:].rearrange("p c t -> p (c t)"))
+
+        pairs = [(e, s) for e in range(E) for s in range(2)]
+        g = {x: held.tile([P, PACK, C], F32, name=f"g{x[0]}{x[1]}") for x in pairs}
+        gi = {x: held.tile([P, C, PACK], BF16, name=f"gi{x[0]}{x[1]}", align_bytes=64) for x in pairs}
+        g_codes = {x: held.tile([P, C], U32, name=f"gc{x[0]}{x[1]}", align_bytes=64) for x in pairs}
+        g_scales = {x: held.tile([P, C], U8, name=f"gs{x[0]}{x[1]}", align_bytes=64) for x in pairs}
+        da = {x: held.tile([P, PACK, C], BF16, name=f"da{x[0]}{x[1]}") for x in pairs}
+        dai = {x: held.tile([P, C, PACK], BF16, name=f"dai{x[0]}{x[1]}", align_bytes=64) for x in pairs}
+        da_codes = {x: held.tile([P, C], U32, name=f"dc{x[0]}{x[1]}", align_bytes=64) for x in pairs}
+        da_scales = {x: held.tile([P, C], U8, name=f"ds{x[0]}{x[1]}", align_bytes=64) for x in pairs}
+        dx = {(e, k): held.tile([P, C], F32, name=f"dx{e}{k}") for e in range(E) for k in range(KT)}
+        banks = {}
+
+        def gather(e, s, t):
+            o = offsets[:, e * C // 16 : (e + 1) * C // 16]
+            nc.vector.tensor_tensor(g[e, s][:, t, :], dy_t[s][t][:].indirect(o), gate_t[e][:], ALU.mult)
+            if t == PACK - 1:
+                interleave(gi[e, s], g[e, s])
+
+        def quantize_g(e, s):
+            quantize(g_codes[e, s], g_scales[e, s], gi[e, s])
+
+        def first(e, j, s):
+            if s == 0:
+                banks[e, j] = psum.tile([P, C], F32, name=f"dh{(e * SI * PACK + j) % 6}")
+            nc.tensor.matmul_mx(
+                out=banks[e, j][:],
+                lhsT=w2_p[e][:, s, 2 * j * P : 2 * (j + 1) * P].bitcast(E2M1),
+                lhsT_scale=w2s_p[e * SN + s][:, j * P : (j + 1) * P],
+                rhs=g_codes[e, s][:].bitcast(E5M2),
+                rhs_scale=g_scales[e, s][:],
+                start=(s == 0),
+                stop=(s == SN - 1),
+            )
+
+        def derive(e, j):
+            si, t = divmod(j, PACK)
+            if (e, j) not in banks:
+                first(e, j, 0)
+            first(e, j, 1)
+            nc.vector.scalar_tensor_tensor(
+                out=da[e, si][:, t, :], in0=a_t[e][si][:, t, :], scalar=0.0, in1=banks[e, j][:], op0=ALU.max, op1=ALU.mult
+            )
+            if t == PACK - 1:
+                interleave(dai[e, si], da[e, si])
+
+        def second(e, si):
+            quantize(da_codes[e, si], da_scales[e, si], dai[e, si])
+            for k in range(KT):
+                if si == 0:
+                    banks[e, "x", k] = psum.tile([P, C], F32, name=f"acc{k}")
+                nc.tensor.matmul_mx(
+                    out=banks[e, "x", k][:],
+                    lhsT=w1_t[:, e * SI + si, 2 * k * P : 2 * (k + 1) * P].bitcast(E2M1),
+                    lhsT_scale=w1s_t[:, e * SI + si, k * P : (k + 1) * P],
+                    rhs=da_codes[e, si][:].bitcast(E5M2),
+                    rhs_scale=da_scales[e, si][:],
+                    start=(si == 0),
+                    stop=(si == SI - 1),
+                )
+                if si == SI - 1:
+                    nc.scalar.activation(out=dx[e, k][:], in_=banks[e, "x", k][:], func=COPY, scale=2.0)
+
+        def scatter(e, k):
+            nc.vector.tensor_copy(win[k][:].indirect(offsets[:, e * C // 16 : (e + 1) * C // 16]), dx[e, k][:])
+
+        permute_w2_words(0)
+        for s in range(SN):
+            for t in range(PACK):
+                gather(0, s, t)
+        permute_w2_scales()
+        quantize_g(0, 0)
+        for j in range(6):
+            first(0, j, 0)
+        for t in range(3):
+            gather(1, 0, t)
+        quantize_g(0, 1)
+        gather(1, 0, 3)
+        for j in range(4):
+            derive(0, j)
+        for t in range(3):
+            gather(1, 1, t)
+        quantize_g(1, 0)
+        gather(1, 1, 3)
+        second(0, 0)
+        permute_w2_words(1)
+        for j in range(4, 6):
+            derive(0, j)
+        quantize_g(1, 1)
+        for j in range(6, 8):
+            derive(0, j)
+        for j in range(6):
+            first(1, j, 0)
+        for j in range(5):
+            derive(1, j)
+        second(0, 1)
+        for j in range(5, 8):
+            derive(1, j)
+        second(1, 0)
+        scatter(0, 0)
+        second(1, 1)
+        scatter(0, 1)
+        for k in range(KT):
+            scatter(1, k)
+            nc.sync.dma_start(out[k * P : (k + 1) * P, :], win[k][:])

@@ -1,6 +1,7 @@
 from contextlib import ExitStack
 
 import concourse.mybir as mybir
+from concourse.masks import make_identity
 
 K, T, E, C, H, N = 256, 1024, 2, 512, 1024, 1024
 P = 128
@@ -18,190 +19,242 @@ U8 = mybir.dt.uint8
 E5M2 = mybir.dt.float8_e5m2_x4
 E2M1 = mybir.dt.float4_e2m1fn_x4
 ALU = mybir.AluOpType
-COPY = mybir.ActivationFunctionType.Copy
+RELU = mybir.ActivationFunctionType.Relu
 
 
 def tile_moe_bdx_mlp_relu2_kernel(
     tc, dyT, a, w2_words, w2_scales, w1_words, w1_scales, gate, offs, out
 ):
     nc = tc.nc
-    SN, SI, KT = N // PASS, H // PASS, K // P
-
+    SN, SI, KT, Q = N // PASS, H // PASS, K // P, C // P
 
     with ExitStack() as ctx:
         held = ctx.enter_context(tc.tile_pool(name="held", bufs=1))
         psum = ctx.enter_context(tc.psum_pool(name="psum", bufs=1))
 
+        pairs = [(e, s) for e in range(E) for s in range(2)]
         offsets = held.tile([P, E * C // 16], U16, name="offsets")
         dy_t = [[held.tile([P, T], F32, name=f"dy{s}{t}") for t in range(PACK)] for s in range(SN)]
-        gate_t = [held.tile([P, C], F32, name=f"gate{e}") for e in range(E)]
-        a_t = [[held.tile([P, PACK, C], F32, name=f"a{e}{s}") for s in range(SI)] for e in range(E)]
-        w2_raw = [held.tile([P, SN, 2 * H], U8, name=f"w2r{e}", align_bytes=64) for e in range(E)]
-        w2_p = [held.tile([P, SN, 2 * H], U8, name=f"w2p{e}", align_bytes=64) for e in range(E)]
-        w2s_raw = held.tile([P, H], U8, name="w2sr", align_bytes=64)
-        w2s_p = [held.tile([P, H], U8, name=f"w2sp{j}", align_bytes=64) for j in range(E * SN)]
+        g = {x: held.tile([P, PACK * C], F32, name=f"g{x[0]}{x[1]}", align_bytes=64) for x in pairs}
+        gate_t = [g[1, 1][:, C // 2 : C // 2 + C], held.tile([P, C], F32, name="gate1")[:]]
+        a_t = {(e, s, h): held.tile([P, 2, C], F32, name=f"a{e}{s}{h}", align_bytes=64) for e, s in pairs for h in range(2)}
+        w2_t = [held.tile([P, SN, 2 * H], U8, name=f"w2{e}", align_bytes=64) for e in range(E)]
+        w2s_t = held.tile([P, E * SN, H], U8, name="w2s", align_bytes=64)
         w1_t = held.tile([P, E * SI, 2 * K], U8, name="w1t", align_bytes=64)
         w1s_t = held.tile([P, E * SI, K], U8, name="w1s", align_bytes=64)
-        win = [held.tile([P, T], F32, name=f"win{k}") for k in range(KT)]
+        ident = held.tile([P, P], F32, name="ident")
 
         dy_v = dyT.rearrange("(s p t) c -> s t p c", p=P, t=PACK)
-        a_v = a.rearrange("(s p t) (e c) -> e s p t c", p=P, t=PACK, e=E)
+        a_v = a.rearrange("(s h j p) (e c) -> e s h p j c", p=P, j=2, e=E, h=2)
         w2_v = w2_words.bitcast(I32).rearrange("e s p b -> e p s b")
-        w2s_v = w2_scales.bitcast(I32).rearrange("e s f i -> (e s) f i")
+        w2s_v = w2_scales.bitcast(I32).rearrange("e s f i -> f (e s) i")
         w1_v = w1_words.bitcast(I32).rearrange("e s p b -> p (e s) b")
         w1s_v = w1_scales.bitcast(I32).rearrange("e s f i -> f (e s) i")
 
         nc.sync.dma_start(offsets[:], offs)
-        nc.vector.memset(w2s_raw[:].bitcast(I32), 0)
+        nc.vector.memset(w2s_t[:].bitcast(I32), 0)
         nc.vector.memset(w1s_t[:].bitcast(I32), 0)
-        for j in range(1, E * SN):
-            nc.gpsimd.memset(w2s_p[j][:].bitcast(I32), 0)
+        make_identity(nc, ident[:])
 
-        def load_w2(e):
-            nc.sync.dma_start(w2_raw[e][:].bitcast(I32), w2_v[e])
+        def load_dy(s, t):
+            nc.sync.dma_start(dy_t[s][t][:], dy_v[s, t])
 
-        load_w2(0)
-        nc.sync.dma_start(gate_t[0][:], gate[0:P, 0:C])
+        def load_a(e, s, h):
+            nc.sync.dma_start(a_t[e, s, h][:], a_v[e, s, h])
+
+        nc.sync.dma_start(gate_t[0], gate[0:P, 0:C])
+        load_dy(0, 0)
+        nc.sync.dma_start(gate_t[1], gate[0:P, C : 2 * C])
+        load_dy(0, 1)
+        load_a(0, 0, 0)
+        load_dy(0, 2)
+        load_a(0, 0, 1)
+        load_a(0, 1, 0)
+        load_dy(0, 3)
+        load_a(0, 1, 1)
         for t in range(PACK):
-            nc.sync.dma_start(dy_t[0][t][:], dy_v[0, t])
-        for t in range(PACK):
-            nc.sync.dma_start(dy_t[1][t][:], dy_v[1, t])
+            load_dy(1, t)
+        nc.sync.dma_start(w2_t[0][:].bitcast(I32), w2_v[0])
         for q in range(4):
-            nc.sync.dma_start(w2s_raw[32 * q : 32 * q + 16, :].bitcast(I32), w2s_v[:, 4 * q : 4 * q + 4])
-        nc.sync.dma_start(gate_t[1][:], gate[0:P, C : 2 * C])
+            nc.sync.dma_start(w2s_t[32 * q : 32 * q + 4, :, :].bitcast(I32), w2s_v[4 * q : 4 * q + 4])
+        for s in range(SI):
+            for h in range(2):
+                load_a(1, s, h)
+        nc.sync.dma_start(w2_t[1][:].bitcast(I32), w2_v[1])
         nc.sync.dma_start(w1_t[:].bitcast(I32), w1_v)
         for q in range(4):
             nc.sync.dma_start(w1s_t[32 * q : 32 * q + 4, :, :].bitcast(I32), w1s_v[4 * q : 4 * q + 4])
-        for s in range(SI):
-            nc.sync.dma_start(a_t[0][s][:], a_v[0, s])
-        load_w2(1)
-        for s in range(SI):
-            nc.sync.dma_start(a_t[1][s][:], a_v[1, s])
 
-        def permute_w2_words(e):
-            nc.vector.tensor_copy(
-                out=w2_p[e][:].bitcast(U16).rearrange("p n (s t m) -> p (n s) t m", s=SI, t=PACK),
-                in_=w2_raw[e][:].bitcast(U16).rearrange("p n (s m t) -> p (n s) t m", s=SI, t=PACK),
-            )
-
-        def permute_w2_scales():
-            nc.vector.tensor_copy(
-                out=w2s_p[0][:].rearrange("p (s t m) -> p s t m", s=SI, t=PACK),
-                in_=w2s_raw[:].rearrange("p (s m t) -> p s t m", s=SI, t=PACK),
-            )
-            for j in range(1, E * SN):
-                for r in range(4):
-                    nc.sync.dma_start(w2s_p[j][r:P:32, :].bitcast(I32), w2s_p[0][4 * j + r : P : 32, :].bitcast(I32))
-
-        def interleave(dst, src):
-            nc.scalar.copy(
-                out=dst[:].rearrange("p (c i) t -> p c t i", i=4),
-                in_=src[:].rearrange("p t (c i) -> p c t i", i=4),
-            )
-
-        def quantize(codes, scales, src):
-            nc.vector.quantize_mx(out=codes[:].bitcast(E5M2), scales=scales[:], in_=src[:].rearrange("p c t -> p (c t)"))
-
-        pairs = [(e, s) for e in range(E) for s in range(2)]
-        g = {x: held.tile([P, PACK, C], F32, name=f"g{x[0]}{x[1]}") for x in pairs}
-        gi = {x: held.tile([P, C, PACK], BF16, name=f"gi{x[0]}{x[1]}", align_bytes=64) for x in pairs}
+        gi = {}
+        gi_name = {(0, 0): "a011", (1, 0): "g00", (1, 1): "a110"}
         g_codes = {x: held.tile([P, C], U32, name=f"gc{x[0]}{x[1]}", align_bytes=64) for x in pairs}
         g_scales = {x: held.tile([P, C], U8, name=f"gs{x[0]}{x[1]}", align_bytes=64) for x in pairs}
-        da = {x: held.tile([P, PACK, C], BF16, name=f"da{x[0]}{x[1]}") for x in pairs}
-        dai = {x: held.tile([P, C, PACK], BF16, name=f"dai{x[0]}{x[1]}", align_bytes=64) for x in pairs}
+        slope = {
+            (e, s, r): held.tile([P, 2, PASS], F32, name=f"slope{e}{s}{r}", align_bytes=64) for e, s in pairs for r in range(2)
+        }
+        gi[0, 1] = g[1, 1][:, 2 * C : 4 * C].bitcast(BF16)
+        da_t = {(e, s, q): held.tile([P, PASS], BF16, name=f"da{e}{s}{q}") for e, s in pairs for q in range(Q)}
+        dai = {x: held.tile([P, C * PACK], BF16, name=f"dai{x[0]}{x[1]}", align_bytes=64) for x in pairs}
         da_codes = {x: held.tile([P, C], U32, name=f"dc{x[0]}{x[1]}", align_bytes=64) for x in pairs}
         da_scales = {x: held.tile([P, C], U8, name=f"ds{x[0]}{x[1]}", align_bytes=64) for x in pairs}
         dx = {(e, k): held.tile([P, C], F32, name=f"dx{e}{k}") for e in range(E) for k in range(KT)}
-        banks = {}
+        win_name = ["slope111", "dai11"]
+        win, banks = {}, {}
 
-        def gather(e, s, t):
-            o = offsets[:, e * C // 16 : (e + 1) * C // 16]
-            nc.vector.tensor_tensor(g[e, s][:, t, :], dy_t[s][t][:].indirect(o), gate_t[e][:], ALU.mult)
-            if t == PACK - 1:
-                interleave(gi[e, s], g[e, s])
+        def quantize(codes, scales, src):
+            nc.vector.quantize_mx(out=codes[:].bitcast(E5M2), scales=scales[:], in_=src)
+
+        def gather(e, s, t, c0=0, c1=C):
+            o = offsets[:, (e * C + c0) // 16 : (e * C + c1) // 16]
+            nc.vector.tensor_tensor(g[e, s][:, t * C + c0 : t * C + c1], dy_t[s][t][:].indirect(o), gate_t[e][:, c0:c1], ALU.mult)
+
+        def weave_g(e, s):
+            if (e, s) in gi_name:
+                gi[e, s] = held.tile([P, C * PACK], BF16, name=gi_name[e, s], align_bytes=64)[:]
+            nc.scalar.copy(
+                out=gi[e, s].rearrange("p (c i t) -> p c t i", i=4, t=PACK),
+                in_=g[e, s][:].rearrange("p (t c i) -> p c t i", i=4, t=PACK),
+            )
 
         def quantize_g(e, s):
             quantize(g_codes[e, s], g_scales[e, s], gi[e, s])
 
-        def first(e, j, s):
+        def turn_a(e, si, h, r, name):
+            bank = psum.tile([P, 2, 2 * P], F32, name=name)
+            for ql in range(2):
+                for j in range(2):
+                    q = 2 * r + ql
+                    nc.tensor.transpose(bank[:, ql, j * P : (j + 1) * P], a_t[e, si, h][:, j, q * P : (q + 1) * P], ident[:])
+            nc.scalar.activation(out=slope[e, si, r][:, :, h * 2 * P : (h + 1) * 2 * P], in_=bank[:], func=RELU, scale=2.0)
+
+        def first(e, si, q, s, name=None):
             if s == 0:
-                banks[e, j] = psum.tile([P, C], F32, name=f"dh{(e * SI * PACK + j) % 6}")
+                banks[e, si, q] = psum.tile([P, PASS], F32, name=name)
             nc.tensor.matmul_mx(
-                out=banks[e, j][:],
-                lhsT=w2_p[e][:, s, 2 * j * P : 2 * (j + 1) * P].bitcast(E2M1),
-                lhsT_scale=w2s_p[e * SN + s][:, j * P : (j + 1) * P],
-                rhs=g_codes[e, s][:].bitcast(E5M2),
-                rhs_scale=g_scales[e, s][:],
+                out=banks[e, si, q][:],
+                lhsT=g_codes[e, s][:, q * P : (q + 1) * P].bitcast(E5M2),
+                lhsT_scale=g_scales[e, s][:, q * P : (q + 1) * P],
+                rhs=w2_t[e][:, s, 2 * si * PASS : 2 * (si + 1) * PASS].bitcast(E2M1),
+                rhs_scale=w2s_t[:, e * SN + s, si * PASS : (si + 1) * PASS],
                 start=(s == 0),
                 stop=(s == SN - 1),
             )
 
-        def derive(e, j):
-            si, t = divmod(j, PACK)
-            if (e, j) not in banks:
-                first(e, j, 0)
-            first(e, j, 1)
-            nc.vector.scalar_tensor_tensor(
-                out=da[e, si][:, t, :], in0=a_t[e][si][:, t, :], scalar=0.0, in1=banks[e, j][:], op0=ALU.max, op1=ALU.mult
+        def derive(e, si, q):
+            nc.vector.tensor_tensor(
+                da_t[e, si, q][:].rearrange("c (u p d) -> c p u d", u=2, d=2),
+                banks[e, si, q][:].rearrange("c (p u d) -> c p u d", u=2, d=2),
+                slope[e, si, q // 2][:, q % 2, :].rearrange("c (p u d) -> c p u d", u=2, d=2),
+                ALU.mult,
             )
-            if t == PACK - 1:
-                interleave(dai[e, si], da[e, si])
 
-        def second(e, si):
-            quantize(da_codes[e, si], da_scales[e, si], dai[e, si])
-            for k in range(KT):
-                if si == 0:
-                    banks[e, "x", k] = psum.tile([P, C], F32, name=f"acc{k}")
-                nc.tensor.matmul_mx(
-                    out=banks[e, "x", k][:],
-                    lhsT=w1_t[:, e * SI + si, 2 * k * P : 2 * (k + 1) * P].bitcast(E2M1),
-                    lhsT_scale=w1s_t[:, e * SI + si, k * P : (k + 1) * P],
-                    rhs=da_codes[e, si][:].bitcast(E5M2),
-                    rhs_scale=da_scales[e, si][:],
-                    start=(si == 0),
-                    stop=(si == SI - 1),
-                )
-                if si == SI - 1:
-                    nc.scalar.activation(out=dx[e, k][:], in_=banks[e, "x", k][:], func=COPY, scale=2.0)
+        def turn_da(e, si, h, name):
+            bank = psum.tile([P, 2, 2, P], F32, name=name)
+            for ql in range(2):
+                words = da_t[e, si, 2 * h + ql][:].bitcast(F32)
+                for u in range(2):
+                    nc.tensor.transpose(bank[:, ql, u, :], words[:, u * P : (u + 1) * P], ident[:])
+            nc.scalar.copy(
+                out=dai[e, si][:, h * C * 2 : (h + 1) * C * 2].bitcast(F32).rearrange("p (q c u) -> p q c u", q=2, u=2),
+                in_=bank[:].rearrange("p q u c -> p q c u"),
+            )
+
+        def quantize_da(e, si):
+            quantize(da_codes[e, si], da_scales[e, si], dai[e, si][:])
+
+        def second(e, k, s):
+            if s == 0:
+                banks[e, k] = psum.tile([P, C], F32, name=f"B{k}")
+            nc.tensor.matmul_mx(
+                out=banks[e, k][:],
+                lhsT=w1_t[:, e * SI + s, 2 * k * P : 2 * (k + 1) * P].bitcast(E2M1),
+                lhsT_scale=w1s_t[:, e * SI + s, k * P : (k + 1) * P],
+                rhs=da_codes[e, s][:].bitcast(E5M2),
+                rhs_scale=da_scales[e, s][:],
+                start=(s == 0),
+                stop=(s == SI - 1),
+            )
+            if s == SI - 1:
+                nc.scalar.copy(out=dx[e, k][:], in_=banks[e, k][:])
 
         def scatter(e, k):
+            if e == 0:
+                win[k] = held.tile([P, T], F32, name=win_name[k], align_bytes=64)
             nc.vector.tensor_copy(win[k][:].indirect(offsets[:, e * C // 16 : (e + 1) * C // 16]), dx[e, k][:])
 
-        permute_w2_words(0)
-        for s in range(SN):
-            for t in range(PACK):
-                gather(0, s, t)
-        permute_w2_scales()
-        quantize_g(0, 0)
-        for j in range(6):
-            first(0, j, 0)
-        for t in range(3):
+        for t in range(PACK):
+            gather(0, 0, t)
             gather(1, 0, t)
-        quantize_g(0, 1)
-        gather(1, 0, 3)
-        for j in range(4):
-            derive(0, j)
-        for t in range(3):
-            gather(1, 1, t)
+        for si in range(SI):
+            for q in range(Q):
+                turn_a(0, si, q // 2, q % 2, f"B{q}")
+        weave_g(0, 0)
+        weave_g(1, 0)
+        for t in range(PACK):
+            gather(0, 1, t)
+        weave_g(0, 1)
+        quantize_g(0, 0)
+        for q in range(Q):
+            first(0, 0, q, 0, f"A{q}")
+        gather(1, 1, 0)
+        gather(1, 1, 1)
         quantize_g(1, 0)
+        quantize_g(0, 1)
+        for q in range(Q):
+            first(0, 0, q, 1)
+        for q in range(Q):
+            turn_a(1, 0, q // 2, q % 2, f"B{q}")
+        turn_a(1, 1, 0, 0, "B2")
+        turn_a(1, 1, 0, 1, "B3")
+        gather(1, 1, 2)
         gather(1, 1, 3)
-        second(0, 0)
-        permute_w2_words(1)
-        for j in range(4, 6):
-            derive(0, j)
+        weave_g(1, 1)
+        for q in range(Q):
+            first(0, 1, q, 0, f"B{q}")
+            first(0, 1, q, 1)
+        derive(0, 0, 0)
+        derive(0, 0, 1)
+        turn_da(0, 0, 0, "A0")
+        turn_a(1, 1, 1, 0, "A1")
+        derive(0, 0, 2)
+        turn_a(1, 1, 1, 1, "A2")
+        derive(0, 0, 3)
+        turn_da(0, 0, 1, "A3")
+        derive(0, 1, 0)
+        derive(0, 1, 1)
         quantize_g(1, 1)
-        for j in range(6, 8):
-            derive(0, j)
-        for j in range(6):
-            first(1, j, 0)
-        for j in range(5):
-            derive(1, j)
-        second(0, 1)
-        for j in range(5, 8):
-            derive(1, j)
-        second(1, 0)
+        for q in range(Q):
+            first(1, 0, q, 0, ("B0", "B1", "A0", "A1")[q])
+            first(1, 0, q, 1)
+        derive(0, 1, 2)
+        turn_da(0, 1, 0, "B2")
+        derive(0, 1, 3)
+        turn_da(0, 1, 1, "B3")
+        for q in range(Q):
+            first(1, 1, q, 0, ("A2", "A3", "B2", "B3")[q])
+            first(1, 1, q, 1)
+        quantize_da(0, 0)
+        derive(1, 0, 0)
+        derive(1, 0, 1)
+        quantize_da(0, 1)
+        for k in range(KT):
+            second(0, k, 0)
+            second(0, k, 1)
+        derive(1, 0, 2)
+        turn_da(1, 0, 0, "A0")
+        derive(1, 0, 3)
+        turn_da(1, 0, 1, "A1")
+        for h in range(2):
+            derive(1, 1, 2 * h)
+            derive(1, 1, 2 * h + 1)
+            turn_da(1, 1, h, f"A{2 + h}")
+        quantize_da(1, 0)
+        for k in range(KT):
+            second(1, k, 0)
         scatter(0, 0)
-        second(1, 1)
+        quantize_da(1, 1)
+        for k in range(KT):
+            second(1, k, 1)
         scatter(0, 1)
         for k in range(KT):
             scatter(1, k)

@@ -28,18 +28,20 @@ def tile_moe_bdx_mlp_relu2_kernel(
     nc = tc.nc
     SN, SI, KT, Q = N // PASS, H // PASS, K // P, C // P
 
+
     with ExitStack() as ctx:
         held = ctx.enter_context(tc.tile_pool(name="held", bufs=1))
+        heirs = ctx.enter_context(tc.tile_pool(name="heirs", bufs=1))
         psum = ctx.enter_context(tc.psum_pool(name="psum", bufs=1))
 
         pairs = [(e, s) for e in range(E) for s in range(2)]
         offsets = held.tile([P, E * C // 16], U16, name="offsets")
         dy_t = [[held.tile([P, T], F32, name=f"dy{s}{t}") for t in range(PACK)] for s in range(SN)]
-        g = {x: held.tile([P, PACK * C], F32, name=f"g{x[0]}{x[1]}", align_bytes=64) for x in pairs}
-        gate_t = [g[1, 1][:, C // 2 : C // 2 + C], held.tile([P, C], F32, name="gate1")[:]]
+        g = {x: held.tile([P, PACK, C], F32, name=f"g{x[0]}{x[1]}", align_bytes=64)[:] for x in pairs if x != (1, 1)}
+        gate_t = [heirs.tile([P, C], F32, name="gate0", offset=0, align_bytes=64)[:], held.tile([P, C], F32, name="gate1")[:]]
         a_t = {(e, s, h): held.tile([P, 2, C], F32, name=f"a{e}{s}{h}", align_bytes=64) for e, s in pairs for h in range(2)}
         w2_t = [held.tile([P, SN, 2 * H], U8, name=f"w2{e}", align_bytes=64) for e in range(E)]
-        w2s_t = held.tile([P, E * SN, H], U8, name="w2s", align_bytes=64)
+        w2s_t = [held.tile([P, SN, H], U8, name=f"w2s{e}", align_bytes=64) for e in range(E)]
         w1_t = held.tile([P, E * SI, 2 * K], U8, name="w1t", align_bytes=64)
         w1s_t = held.tile([P, E * SI, K], U8, name="w1s", align_bytes=64)
         ident = held.tile([P, P], F32, name="ident")
@@ -47,58 +49,67 @@ def tile_moe_bdx_mlp_relu2_kernel(
         dy_v = dyT.rearrange("(s p t) c -> s t p c", p=P, t=PACK)
         a_v = a.rearrange("(s h j p) (e c) -> e s h p j c", p=P, j=2, e=E, h=2)
         w2_v = w2_words.bitcast(I32).rearrange("e s p b -> e p s b")
-        w2s_v = w2_scales.bitcast(I32).rearrange("e s f i -> f (e s) i")
+        w2s_v = w2_scales.bitcast(I32).rearrange("e s (q r) i -> e r q s i", r=4)
         w1_v = w1_words.bitcast(I32).rearrange("e s p b -> p (e s) b")
-        w1s_v = w1_scales.bitcast(I32).rearrange("e s f i -> f (e s) i")
+        w1s_v = w1_scales.bitcast(I32).rearrange("e s (q r) i -> r q (e s) i", r=4)
 
         nc.sync.dma_start(offsets[:], offs)
-        nc.vector.memset(w2s_t[:].bitcast(I32), 0)
+        for e in range(E):
+            nc.vector.memset(w2s_t[e][:].bitcast(I32), 0)
         nc.vector.memset(w1s_t[:].bitcast(I32), 0)
         make_identity(nc, ident[:])
 
         def load_dy(s, t):
             nc.sync.dma_start(dy_t[s][t][:], dy_v[s, t])
 
+        def load_w2(e):
+            nc.sync.dma_start(w2_t[e][:].bitcast(I32), w2_v[e])
+            for r in range(4):
+                nc.sync.dma_start(w2s_t[e][r:P:32, :, :].bitcast(I32), w2s_v[e, r])
+
         def load_a(e, s, h):
             nc.sync.dma_start(a_t[e, s, h][:], a_v[e, s, h])
 
-        nc.sync.dma_start(gate_t[0], gate[0:P, 0:C])
-        load_dy(0, 0)
         nc.sync.dma_start(gate_t[1], gate[0:P, C : 2 * C])
+        load_dy(0, 0)
+        nc.sync.dma_start(gate_t[0], gate[0:P, 0:C])
         load_dy(0, 1)
         load_a(0, 0, 0)
         load_dy(0, 2)
         load_a(0, 0, 1)
-        load_a(0, 1, 0)
         load_dy(0, 3)
-        load_a(0, 1, 1)
+        load_a(0, 1, 0)
         for t in range(PACK):
             load_dy(1, t)
-        nc.sync.dma_start(w2_t[0][:].bitcast(I32), w2_v[0])
-        for q in range(4):
-            nc.sync.dma_start(w2s_t[32 * q : 32 * q + 4, :, :].bitcast(I32), w2s_v[4 * q : 4 * q + 4])
-        for s in range(SI):
-            for h in range(2):
-                load_a(1, s, h)
-        nc.sync.dma_start(w2_t[1][:].bitcast(I32), w2_v[1])
+        load_a(0, 1, 1)
+        load_a(1, 0, 0)
+        load_w2(0)
+        load_a(1, 0, 1)
+        load_a(1, 1, 0)
+        load_a(1, 1, 1)
+        load_w2(1)
         nc.sync.dma_start(w1_t[:].bitcast(I32), w1_v)
-        for q in range(4):
-            nc.sync.dma_start(w1s_t[32 * q : 32 * q + 4, :, :].bitcast(I32), w1s_v[4 * q : 4 * q + 4])
+        for r in range(4):
+            nc.sync.dma_start(w1s_t[r:P:32, :, :].bitcast(I32), w1s_v[r])
 
         gi = {}
-        gi_name = {(0, 0): "a011", (1, 0): "g00", (1, 1): "a110"}
+        gi_name = {(0, 0): "gi00", (1, 0): "gi10", (1, 1): "a101"}
         g_codes = {x: held.tile([P, C], U32, name=f"gc{x[0]}{x[1]}", align_bytes=64) for x in pairs}
-        g_scales = {x: held.tile([P, C], U8, name=f"gs{x[0]}{x[1]}", align_bytes=64) for x in pairs}
+        g_scales = {x: held.tile([P, C], U8, name=f"gs{x[0]}{x[1]}", align_bytes=64)[:] for x in pairs if x[1] == 1}
+        for e in range(E):
+            g_scales[e, 0] = heirs.tile([P, C], U8, name=f"gs{e}0", offset=e * C, align_bytes=64)[:]
+        last = heirs.tile([P, (PACK + 1) * C], F32, name="last", offset=E * C, align_bytes=64)
+        g[1, 1] = last[:, 0 : PACK * C].rearrange("p (t c) -> p t c", t=PACK)
         slope = {
             (e, s, r): held.tile([P, 2, PASS], F32, name=f"slope{e}{s}{r}", align_bytes=64) for e, s in pairs for r in range(2)
         }
-        gi[0, 1] = g[1, 1][:, 2 * C : 4 * C].bitcast(BF16)
+        gi[0, 1] = last[:, (PACK - 1) * C : (PACK + 1) * C].bitcast(BF16)
         da_t = {(e, s, q): held.tile([P, PASS], BF16, name=f"da{e}{s}{q}") for e, s in pairs for q in range(Q)}
         dai = {x: held.tile([P, C * PACK], BF16, name=f"dai{x[0]}{x[1]}", align_bytes=64) for x in pairs}
         da_codes = {x: held.tile([P, C], U32, name=f"dc{x[0]}{x[1]}", align_bytes=64) for x in pairs}
         da_scales = {x: held.tile([P, C], U8, name=f"ds{x[0]}{x[1]}", align_bytes=64) for x in pairs}
         dx = {(e, k): held.tile([P, C], F32, name=f"dx{e}{k}") for e in range(E) for k in range(KT)}
-        win_name = ["slope111", "dai11"]
+        win_name = ["slope110", "dai11"]
         win, banks = {}, {}
 
         def quantize(codes, scales, src):
@@ -106,14 +117,14 @@ def tile_moe_bdx_mlp_relu2_kernel(
 
         def gather(e, s, t, c0=0, c1=C):
             o = offsets[:, (e * C + c0) // 16 : (e * C + c1) // 16]
-            nc.vector.tensor_tensor(g[e, s][:, t * C + c0 : t * C + c1], dy_t[s][t][:].indirect(o), gate_t[e][:, c0:c1], ALU.mult)
+            nc.vector.tensor_tensor(g[e, s][:, t, c0:c1], dy_t[s][t][:].indirect(o), gate_t[e][:, c0:c1], ALU.mult)
 
         def weave_g(e, s):
             if (e, s) in gi_name:
                 gi[e, s] = held.tile([P, C * PACK], BF16, name=gi_name[e, s], align_bytes=64)[:]
             nc.scalar.copy(
                 out=gi[e, s].rearrange("p (c i t) -> p c t i", i=4, t=PACK),
-                in_=g[e, s][:].rearrange("p (t c i) -> p c t i", i=4, t=PACK),
+                in_=g[e, s].rearrange("p t (c i) -> p c t i", i=4),
             )
 
         def quantize_g(e, s):
@@ -125,7 +136,12 @@ def tile_moe_bdx_mlp_relu2_kernel(
                 for j in range(2):
                     q = 2 * r + ql
                     nc.tensor.transpose(bank[:, ql, j * P : (j + 1) * P], a_t[e, si, h][:, j, q * P : (q + 1) * P], ident[:])
-            nc.scalar.activation(out=slope[e, si, r][:, :, h * 2 * P : (h + 1) * 2 * P], in_=bank[:], func=RELU, scale=2.0)
+            nc.scalar.activation(
+                out=slope[e, si, r][:].rearrange("c q (u h p d) -> c h u q p d", u=2, h=2, d=2)[:, h],
+                in_=bank[:].rearrange("c q (p u d) -> c u q p d", u=2, d=2),
+                func=RELU,
+                scale=2.0,
+            )
 
         def first(e, si, q, s, name=None):
             if s == 0:
@@ -135,16 +151,16 @@ def tile_moe_bdx_mlp_relu2_kernel(
                 lhsT=g_codes[e, s][:, q * P : (q + 1) * P].bitcast(E5M2),
                 lhsT_scale=g_scales[e, s][:, q * P : (q + 1) * P],
                 rhs=w2_t[e][:, s, 2 * si * PASS : 2 * (si + 1) * PASS].bitcast(E2M1),
-                rhs_scale=w2s_t[:, e * SN + s, si * PASS : (si + 1) * PASS],
+                rhs_scale=w2s_t[e][:, s, si * PASS : (si + 1) * PASS],
                 start=(s == 0),
                 stop=(s == SN - 1),
             )
 
         def derive(e, si, q):
             nc.vector.tensor_tensor(
-                da_t[e, si, q][:].rearrange("c (u p d) -> c p u d", u=2, d=2),
-                banks[e, si, q][:].rearrange("c (p u d) -> c p u d", u=2, d=2),
-                slope[e, si, q // 2][:, q % 2, :].rearrange("c (p u d) -> c p u d", u=2, d=2),
+                da_t[e, si, q][:].rearrange("c (u p d) -> c u p d", u=2, d=2),
+                banks[e, si, q][:].rearrange("c (p u d) -> c u p d", u=2, d=2),
+                slope[e, si, q // 2][:, q % 2, :].rearrange("c (u p d) -> c u p d", u=2, d=2),
                 ALU.mult,
             )
 
@@ -183,55 +199,64 @@ def tile_moe_bdx_mlp_relu2_kernel(
             nc.vector.tensor_copy(win[k][:].indirect(offsets[:, e * C // 16 : (e + 1) * C // 16]), dx[e, k][:])
 
         for t in range(PACK):
-            gather(0, 0, t)
             gather(1, 0, t)
-        for si in range(SI):
-            for q in range(Q):
-                turn_a(0, si, q // 2, q % 2, f"B{q}")
-        weave_g(0, 0)
+            gather(0, 0, t)
+        for q in range(Q):
+            turn_a(0, 0, q // 2, q % 2, f"B{q}")
+        for r in range(2):
+            turn_a(0, 1, 0, r, f"B{r}")
         weave_g(1, 0)
+        weave_g(0, 0)
         for t in range(PACK):
             gather(0, 1, t)
         weave_g(0, 1)
+        for r in range(2):
+            turn_a(0, 1, 1, r, f"B{2 + r}")
+        for r in range(2):
+            turn_a(1, 0, 0, r, f"B{r}")
+        quantize_g(1, 0)
+        gather(1, 1, 0)
         quantize_g(0, 0)
         for q in range(Q):
             first(0, 0, q, 0, f"A{q}")
-        gather(1, 1, 0)
+        for r in range(2):
+            turn_a(1, 0, 1, r, f"B{2 + r}")
         gather(1, 1, 1)
-        quantize_g(1, 0)
         quantize_g(0, 1)
-        for q in range(Q):
-            first(0, 0, q, 1)
-        for q in range(Q):
-            turn_a(1, 0, q // 2, q % 2, f"B{q}")
-        turn_a(1, 1, 0, 0, "B2")
-        turn_a(1, 1, 0, 1, "B3")
         gather(1, 1, 2)
         gather(1, 1, 3)
         weave_g(1, 1)
+        for q in range(Q):
+            first(0, 0, q, 1)
         for q in range(Q):
             first(0, 1, q, 0, f"B{q}")
             first(0, 1, q, 1)
         derive(0, 0, 0)
         derive(0, 0, 1)
         turn_da(0, 0, 0, "A0")
-        turn_a(1, 1, 1, 0, "A1")
+        turn_a(1, 1, 0, 0, "A1")
         derive(0, 0, 2)
-        turn_a(1, 1, 1, 1, "A2")
+        turn_a(1, 1, 0, 1, "A2")
         derive(0, 0, 3)
         turn_da(0, 0, 1, "A3")
         derive(0, 1, 0)
         derive(0, 1, 1)
         quantize_g(1, 1)
-        for q in range(Q):
-            first(1, 0, q, 0, ("B0", "B1", "A0", "A1")[q])
+        for q in range(2):
+            first(1, 0, q, 0, f"B{q}")
+        turn_a(1, 1, 1, 0, "A0")
+        turn_a(1, 1, 1, 1, "A1")
+        for q in range(2):
             first(1, 0, q, 1)
         derive(0, 1, 2)
         turn_da(0, 1, 0, "B2")
         derive(0, 1, 3)
+        for q in range(2, Q):
+            first(1, 0, q, 0, f"A{q}")
+            first(1, 0, q, 1)
         turn_da(0, 1, 1, "B3")
         for q in range(Q):
-            first(1, 1, q, 0, ("A2", "A3", "B2", "B3")[q])
+            first(1, 1, q, 0, ("A0", "A1", "B2", "B3")[q])
             first(1, 1, q, 1)
         quantize_da(0, 0)
         derive(1, 0, 0)
@@ -241,13 +266,13 @@ def tile_moe_bdx_mlp_relu2_kernel(
             second(0, k, 0)
             second(0, k, 1)
         derive(1, 0, 2)
-        turn_da(1, 0, 0, "A0")
+        turn_da(1, 0, 0, "A2")
         derive(1, 0, 3)
-        turn_da(1, 0, 1, "A1")
+        turn_da(1, 0, 1, "A3")
         for h in range(2):
             derive(1, 1, 2 * h)
             derive(1, 1, 2 * h + 1)
-            turn_da(1, 1, h, f"A{2 + h}")
+            turn_da(1, 1, h, f"A{h}")
         quantize_da(1, 0)
         for k in range(KT):
             second(1, k, 0)

@@ -29,9 +29,12 @@ def tile_moe_bdx_mlp_relu2_kernel(
     SN, SI, KT, Q = N // PASS, H // PASS, K // P, C // P
 
 
+    SPLIT = 224
+
     with ExitStack() as ctx:
         held = ctx.enter_context(tc.tile_pool(name="held", bufs=1))
         heirs = ctx.enter_context(tc.tile_pool(name="heirs", bufs=1))
+        tail = ctx.enter_context(tc.tile_pool(name="tail", bufs=1))
         psum = ctx.enter_context(tc.psum_pool(name="psum", bufs=1))
 
         pairs = [(e, s) for e in range(E) for s in range(2)]
@@ -70,20 +73,21 @@ def tile_moe_bdx_mlp_relu2_kernel(
         def load_a(e, s, h):
             nc.sync.dma_start(a_t[e, s, h][:], a_v[e, s, h])
 
-        nc.sync.dma_start(gate_t[1], gate[0:P, C : 2 * C])
         load_dy(0, 0)
-        nc.sync.dma_start(gate_t[0], gate[0:P, 0:C])
+        nc.sync.dma_start(gate_t[0][:, 0:P], gate[0:P, 0:P])
+        nc.sync.dma_start(gate_t[0][:, P:C], gate[0:P, P:C])
+        nc.sync.dma_start(gate_t[1], gate[0:P, C : 2 * C])
         load_dy(0, 1)
         load_a(0, 0, 0)
         load_dy(0, 2)
         load_a(0, 0, 1)
-        load_dy(0, 3)
         load_a(0, 1, 0)
+        load_dy(0, 3)
+        load_a(0, 1, 1)
         for t in range(PACK):
             load_dy(1, t)
-        load_a(0, 1, 1)
-        load_a(1, 0, 0)
         load_w2(0)
+        load_a(1, 0, 0)
         load_a(1, 0, 1)
         load_a(1, 1, 0)
         load_a(1, 1, 1)
@@ -93,8 +97,8 @@ def tile_moe_bdx_mlp_relu2_kernel(
             nc.sync.dma_start(w1s_t[r:P:32, :, :].bitcast(I32), w1s_v[r])
 
         gi = {}
-        gi_name = {(0, 0): "gi00", (1, 0): "gi10", (1, 1): "a101"}
-        g_codes = {x: held.tile([P, C], U32, name=f"gc{x[0]}{x[1]}", align_bytes=64) for x in pairs}
+        gi_name = {(0, 0): "gi00", (1, 0): "a011", (1, 1): "gi11"}
+        g_codes = {x: held.tile([P, C], U32, name=f"gc{x[0]}{x[1]}", align_bytes=64) for x in pairs if x[1] == 0}
         g_scales = {x: held.tile([P, C], U8, name=f"gs{x[0]}{x[1]}", align_bytes=64)[:] for x in pairs if x[1] == 1}
         for e in range(E):
             g_scales[e, 0] = heirs.tile([P, C], U8, name=f"gs{e}0", offset=e * C, align_bytes=64)[:]
@@ -105,11 +109,14 @@ def tile_moe_bdx_mlp_relu2_kernel(
         }
         gi[0, 1] = last[:, (PACK - 1) * C : (PACK + 1) * C].bitcast(BF16)
         da_t = {(e, s, q): held.tile([P, PASS], BF16, name=f"da{e}{s}{q}") for e, s in pairs for q in range(Q)}
-        dai = {x: held.tile([P, C * PACK], BF16, name=f"dai{x[0]}{x[1]}", align_bytes=64) for x in pairs}
+        dai = {x: held.tile([P, C * PACK], BF16, name=f"dai{x[0]}{x[1]}", align_bytes=64) for x in pairs if x != (1, 1)}
+        dai[1, 1] = tail.tile([P, C * PACK], BF16, name="dai11", offset=0, align_bytes=64)
         da_codes = {x: held.tile([P, C], U32, name=f"dc{x[0]}{x[1]}", align_bytes=64) for x in pairs}
-        da_scales = {x: held.tile([P, C], U8, name=f"ds{x[0]}{x[1]}", align_bytes=64) for x in pairs}
+        da_scales = {x: held.tile([P, C], U8, name=f"ds{x[0]}{x[1]}", align_bytes=64) for x in pairs if x != (1, 0)}
+        da_scales[1, 0] = tail.tile([P, C], U8, name="ds10", offset=0, align_bytes=64)
+        dx_rest = tail.tile([P, C - SPLIT], F32, name="dx_rest", offset=C, align_bytes=64)
         dx = {(e, k): held.tile([P, C], F32, name=f"dx{e}{k}") for e in range(E) for k in range(KT)}
-        win_name = ["slope110", "dai11"]
+        win_name = ["slope110", "win1"]
         win, banks = {}, {}
 
         def quantize(codes, scales, src):
@@ -122,12 +129,19 @@ def tile_moe_bdx_mlp_relu2_kernel(
         def weave_g(e, s):
             if (e, s) in gi_name:
                 gi[e, s] = held.tile([P, C * PACK], BF16, name=gi_name[e, s], align_bytes=64)[:]
+            if (e, s) in ((1, 1), ):
+                nc.gpsimd.tensor_scalar(
+                    gi[e, s].rearrange("p (c t) -> p c t", t=PACK), g[e, s].rearrange("p t c -> p c t"), 1.0, 0.0, ALU.mult, ALU.add
+                )
+                return
             nc.scalar.copy(
                 out=gi[e, s].rearrange("p (c i t) -> p c t i", i=4, t=PACK),
                 in_=g[e, s].rearrange("p t (c i) -> p c t i", i=4),
             )
 
         def quantize_g(e, s):
+            if s == 1:
+                g_codes[e, s] = held.tile([P, C], U32, name=("a101", "slope001")[e], align_bytes=64)
             quantize(g_codes[e, s], g_scales[e, s], gi[e, s])
 
         def turn_a(e, si, h, r, name):
@@ -157,6 +171,14 @@ def tile_moe_bdx_mlp_relu2_kernel(
             )
 
         def derive(e, si, q):
+            if (e, si, q) in ((1, 1, 0), (1, 1, 2), (1, 1, 3), ):
+                dh = held.tile([P, PASS], F32, name=f"dh{e}{si}{q}")
+                nc.scalar.copy(
+                    out=dh[:].rearrange("c (u p d) -> c u p d", u=2, d=2),
+                    in_=banks[e, si, q][:].rearrange("c (p u d) -> c u p d", u=2, d=2),
+                )
+                nc.gpsimd.tensor_tensor(da_t[e, si, q][:], dh[:], slope[e, si, q // 2][:, q % 2, :], ALU.mult)
+                return
             nc.vector.tensor_tensor(
                 da_t[e, si, q][:].rearrange("c (u p d) -> c u p d", u=2, d=2),
                 banks[e, si, q][:].rearrange("c (p u d) -> c u p d", u=2, d=2),
@@ -178,49 +200,50 @@ def tile_moe_bdx_mlp_relu2_kernel(
         def quantize_da(e, si):
             quantize(da_codes[e, si], da_scales[e, si], dai[e, si][:])
 
-        def second(e, k, s):
+        def second(e, k, s, name=None):
             if s == 0:
-                banks[e, k] = psum.tile([P, C], F32, name=f"B{k}")
+                banks[e, k] = psum.tile([P, C], F32, name=name)
             nc.tensor.matmul_mx(
                 out=banks[e, k][:],
-                lhsT=w1_t[:, e * SI + s, 2 * k * P : 2 * (k + 1) * P].bitcast(E2M1),
-                lhsT_scale=w1s_t[:, e * SI + s, k * P : (k + 1) * P],
-                rhs=da_codes[e, s][:].bitcast(E5M2),
-                rhs_scale=da_scales[e, s][:],
+                lhsT=w1_t[:, e * SI + (s + e) % SI, 2 * k * P : 2 * (k + 1) * P].bitcast(E2M1),
+                lhsT_scale=w1s_t[:, e * SI + (s + e) % SI, k * P : (k + 1) * P],
+                rhs=da_codes[e, (s + e) % SI][:].bitcast(E5M2),
+                rhs_scale=da_scales[e, (s + e) % SI][:],
                 start=(s == 0),
                 stop=(s == SI - 1),
             )
-            if s == SI - 1:
-                nc.scalar.copy(out=dx[e, k][:], in_=banks[e, k][:])
 
-        def scatter(e, k):
-            if e == 0:
+        def drain(dst, e, k, c0, c1):
+            nc.scalar.copy(out=dst, in_=banks[e, k][:, c0:c1])
+
+        def scatter(src, e, k, c0, c1):
+            if k not in win:
                 win[k] = held.tile([P, T], F32, name=win_name[k], align_bytes=64)
-            nc.vector.tensor_copy(win[k][:].indirect(offsets[:, e * C // 16 : (e + 1) * C // 16]), dx[e, k][:])
+            nc.vector.tensor_copy(win[k][:].indirect(offsets[:, (e * C + c0) // 16 : (e * C + c1) // 16]), src)
 
-        for t in range(PACK):
-            gather(1, 0, t)
+        gather(0, 0, 0, 0, P)
+        gather(0, 0, 0, P, C)
+        gather(1, 0, 0)
+        for t in range(1, PACK):
             gather(0, 0, t)
-        for q in range(Q):
-            turn_a(0, 0, q // 2, q % 2, f"B{q}")
-        for r in range(2):
-            turn_a(0, 1, 0, r, f"B{r}")
-        weave_g(1, 0)
+            gather(1, 0, t)
+        for si in range(SI):
+            for q in range(Q):
+                turn_a(0, si, q // 2, q % 2, f"B{q}")
         weave_g(0, 0)
+        weave_g(1, 0)
         for t in range(PACK):
             gather(0, 1, t)
         weave_g(0, 1)
-        for r in range(2):
-            turn_a(0, 1, 1, r, f"B{2 + r}")
-        for r in range(2):
-            turn_a(1, 0, 0, r, f"B{r}")
-        quantize_g(1, 0)
-        gather(1, 1, 0)
         quantize_g(0, 0)
+        gather(1, 1, 0)
+        quantize_g(1, 0)
+        for q in range(Q):
+            turn_a(1, 0, q // 2, q % 2, f"B{q}")
         for q in range(Q):
             first(0, 0, q, 0, f"A{q}")
-        for r in range(2):
-            turn_a(1, 0, 1, r, f"B{2 + r}")
+        for q in range(2):
+            first(0, 1, q, 0, f"B{q}")
         gather(1, 1, 1)
         quantize_g(0, 1)
         gather(1, 1, 2)
@@ -228,59 +251,72 @@ def tile_moe_bdx_mlp_relu2_kernel(
         weave_g(1, 1)
         for q in range(Q):
             first(0, 0, q, 1)
-        for q in range(Q):
+        for r in range(2):
+            turn_a(1, 1, 0, r, f"B{2 + r}")
+        for q in range(2):
+            first(0, 1, q, 1)
+        for q in range(2, Q):
             first(0, 1, q, 0, f"B{q}")
             first(0, 1, q, 1)
         derive(0, 0, 0)
+        turn_a(1, 1, 1, 0, "A0")
         derive(0, 0, 1)
-        turn_da(0, 0, 0, "A0")
-        turn_a(1, 1, 0, 0, "A1")
+        turn_a(1, 1, 1, 1, "A1")
         derive(0, 0, 2)
-        turn_a(1, 1, 0, 1, "A2")
+        turn_da(0, 0, 0, "A2")
         derive(0, 0, 3)
         turn_da(0, 0, 1, "A3")
         derive(0, 1, 0)
         derive(0, 1, 1)
+        for q in range(2):
+            first(1, 0, q, 0, f"A{q}")
         quantize_g(1, 1)
         for q in range(2):
-            first(1, 0, q, 0, f"B{q}")
-        turn_a(1, 1, 1, 0, "A0")
-        turn_a(1, 1, 1, 1, "A1")
-        for q in range(2):
             first(1, 0, q, 1)
+        turn_da(0, 1, 0, "B0")
         derive(0, 1, 2)
-        turn_da(0, 1, 0, "B2")
         derive(0, 1, 3)
+        turn_da(0, 1, 1, "B1")
+        quantize_da(0, 0)
+        first(1, 1, 0, 0, "B2")
+        first(1, 1, 0, 1)
         for q in range(2, Q):
             first(1, 0, q, 0, f"A{q}")
             first(1, 0, q, 1)
-        turn_da(0, 1, 1, "B3")
-        for q in range(Q):
-            first(1, 1, q, 0, ("A0", "A1", "B2", "B3")[q])
-            first(1, 1, q, 1)
-        quantize_da(0, 0)
         derive(1, 0, 0)
         derive(1, 0, 1)
         quantize_da(0, 1)
-        for k in range(KT):
-            second(0, k, 0)
-            second(0, k, 1)
+        derive(1, 1, 0)
+        second(0, 0, 0, "A0")
+        second(0, 0, 1)
+        drain(dx[0, 0][:], 0, 0, 0, C)
+        for q in range(1, Q):
+            first(1, 1, q, 0, ("B3", "B0", "B1")[q - 1])
+            first(1, 1, q, 1)
         derive(1, 0, 2)
-        turn_da(1, 0, 0, "A2")
         derive(1, 0, 3)
+        derive(1, 1, 1)
+        derive(1, 1, 2)
+        derive(1, 1, 3)
+        second(0, 1, 0, "A1")
+        second(0, 1, 1)
+        drain(dx[0, 1][:, 0 : SPLIT], 0, 1, 0, SPLIT)
+        turn_da(1, 1, 0, "B2")
+        turn_da(1, 1, 1, "B3")
+        turn_da(1, 0, 0, "A2")
         turn_da(1, 0, 1, "A3")
-        for h in range(2):
-            derive(1, 1, 2 * h)
-            derive(1, 1, 2 * h + 1)
-            turn_da(1, 1, h, f"A{h}")
-        quantize_da(1, 0)
-        for k in range(KT):
-            second(1, k, 0)
-        scatter(0, 0)
+        scatter(dx[0, 0][:], 0, 0, 0, C)
+        scatter(dx[0, 1][:, 0 : SPLIT], 0, 1, 0, SPLIT)
         quantize_da(1, 1)
+        drain(dx_rest[:], 0, 1, SPLIT, C)
+        second(1, 0, 0, "B0")
+        quantize_da(1, 0)
+        second(1, 0, 1)
+        drain(dx[1, 0][:], 1, 0, 0, C)
+        second(1, 1, 0, "B0")
+        second(1, 1, 1)
+        drain(dx[1, 1][:], 1, 1, 0, C)
+        scatter(dx_rest[:], 0, 1, SPLIT, C)
         for k in range(KT):
-            second(1, k, 1)
-        scatter(0, 1)
-        for k in range(KT):
-            scatter(1, k)
+            scatter(dx[1, k][:], 1, k, 0, C)
             nc.sync.dma_start(out[k * P : (k + 1) * P, :], win[k][:])

@@ -116,7 +116,7 @@ def tile_moe_bdx_mlp_relu2_kernel(
         da_scales[1, 0] = tail.tile([P, C], U8, name="ds10", offset=0, align_bytes=64)
         dx_rest = tail.tile([P, C - SPLIT], F32, name="dx_rest", offset=C, align_bytes=64)
         dx = {(e, k): held.tile([P, C], F32, name=f"dx{e}{k}") for e in range(E) for k in range(KT)}
-        win_name = ["slope110", "win1"]
+        win_name = ["slope101", "win1"]
         win, banks = {}, {}
 
         def quantize(codes, scales, src):
@@ -141,7 +141,7 @@ def tile_moe_bdx_mlp_relu2_kernel(
 
         def quantize_g(e, s):
             if s == 1:
-                g_codes[e, s] = held.tile([P, C], U32, name=("a101", "slope001")[e], align_bytes=64)
+                g_codes[e, s] = held.tile([P, C], U32, name=("a101", "slope011")[e], align_bytes=64)
             quantize(g_codes[e, s], g_scales[e, s], gi[e, s])
 
         def turn_a(e, si, h, r, name):
@@ -171,7 +171,7 @@ def tile_moe_bdx_mlp_relu2_kernel(
             )
 
         def derive(e, si, q):
-            if (e, si, q) in ((1, 1, 0), (1, 1, 2), (1, 1, 3), ):
+            if (e, si, q) in ((0, 1, 1), (1, 0, 0), (1, 1, 1), (1, 1, 2), (1, 1, 3), ):
                 dh = held.tile([P, PASS], F32, name=f"dh{e}{si}{q}")
                 nc.scalar.copy(
                     out=dh[:].rearrange("c (u p d) -> c u p d", u=2, d=2),
@@ -242,60 +242,57 @@ def tile_moe_bdx_mlp_relu2_kernel(
             turn_a(1, 0, q // 2, q % 2, f"B{q}")
         for q in range(Q):
             first(0, 0, q, 0, f"A{q}")
-        for q in range(2):
-            first(0, 1, q, 0, f"B{q}")
+        for r in range(2):
+            turn_a(1, 1, 0, r, f"B{r}")
         gather(1, 1, 1)
         quantize_g(0, 1)
         gather(1, 1, 2)
         gather(1, 1, 3)
         weave_g(1, 1)
-        for q in range(Q):
+        for q in range(2):
             first(0, 0, q, 1)
         for r in range(2):
-            turn_a(1, 1, 0, r, f"B{2 + r}")
-        for q in range(2):
-            first(0, 1, q, 1)
+            turn_a(1, 1, 1, r, f"B{2 + r}")
         for q in range(2, Q):
+            first(0, 0, q, 1)
+        for q in range(Q):
             first(0, 1, q, 0, f"B{q}")
             first(0, 1, q, 1)
-        derive(0, 0, 0)
-        turn_a(1, 1, 1, 0, "A0")
-        derive(0, 0, 1)
-        turn_a(1, 1, 1, 1, "A1")
-        derive(0, 0, 2)
+        for q in range(Q):
+            derive(0, 0, q)
+        derive(0, 1, 1)
         turn_da(0, 0, 0, "A2")
-        derive(0, 0, 3)
         turn_da(0, 0, 1, "A3")
         derive(0, 1, 0)
-        derive(0, 1, 1)
+        derive(0, 1, 2)
+        derive(0, 1, 3)
         for q in range(2):
             first(1, 0, q, 0, f"A{q}")
+        turn_da(0, 1, 0, "B0")
+        turn_da(0, 1, 1, "B1")
         quantize_g(1, 1)
         for q in range(2):
             first(1, 0, q, 1)
-        turn_da(0, 1, 0, "B0")
-        derive(0, 1, 2)
-        derive(0, 1, 3)
-        turn_da(0, 1, 1, "B1")
-        quantize_da(0, 0)
-        first(1, 1, 0, 0, "B2")
-        first(1, 1, 0, 1)
+        derive(1, 0, 0)
         for q in range(2, Q):
             first(1, 0, q, 0, f"A{q}")
             first(1, 0, q, 1)
-        derive(1, 0, 0)
+        quantize_da(0, 0)
         derive(1, 0, 1)
         quantize_da(0, 1)
-        derive(1, 1, 0)
+        for q in range(2):
+            first(1, 1, q, 0, f"B{2 + q}")
+            first(1, 1, q, 1)
+        derive(1, 1, 1)
         second(0, 0, 0, "A0")
         second(0, 0, 1)
         drain(dx[0, 0][:], 0, 0, 0, C)
-        for q in range(1, Q):
-            first(1, 1, q, 0, ("B3", "B0", "B1")[q - 1])
+        for q in range(2, Q):
+            first(1, 1, q, 0, f"B{q - 2}")
             first(1, 1, q, 1)
         derive(1, 0, 2)
         derive(1, 0, 3)
-        derive(1, 1, 1)
+        derive(1, 1, 0)
         derive(1, 1, 2)
         derive(1, 1, 3)
         second(0, 1, 0, "A1")
@@ -309,11 +306,11 @@ def tile_moe_bdx_mlp_relu2_kernel(
         scatter(dx[0, 1][:, 0 : SPLIT], 0, 1, 0, SPLIT)
         quantize_da(1, 1)
         drain(dx_rest[:], 0, 1, SPLIT, C)
-        second(1, 0, 0, "B0")
+        second(1, 0, 0, "A0")
         quantize_da(1, 0)
         second(1, 0, 1)
         drain(dx[1, 0][:], 1, 0, 0, C)
-        second(1, 1, 0, "B0")
+        second(1, 1, 0, "A0")
         second(1, 1, 1)
         drain(dx[1, 1][:], 1, 1, 0, C)
         scatter(dx_rest[:], 0, 1, SPLIT, C)

@@ -81,13 +81,15 @@ def tile_moe_bdx_mlp_relu2_kernel(
         load_a(0, 0, 0)
         load_dy(0, 2)
         load_a(0, 0, 1)
-        load_a(0, 1, 0)
         load_dy(0, 3)
+        load_a(0, 1, 0)
+        load_dy(1, 0)
         load_a(0, 1, 1)
-        for t in range(PACK):
-            load_dy(1, t)
-        load_w2(0)
+        load_dy(1, 1)
+        load_dy(1, 2)
+        load_dy(1, 3)
         load_a(1, 0, 0)
+        load_w2(0)
         load_a(1, 0, 1)
         load_a(1, 1, 0)
         load_a(1, 1, 1)
@@ -97,17 +99,18 @@ def tile_moe_bdx_mlp_relu2_kernel(
             nc.sync.dma_start(w1s_t[r:P:32, :, :].bitcast(I32), w1s_v[r])
 
         gi = {}
-        gi_name = {(0, 0): "gi00", (1, 0): "a011", (1, 1): "gi11"}
+        gi_name = {(1, 0): "a011", (1, 1): "gi11"}
         g_codes = {x: held.tile([P, C], U32, name=f"gc{x[0]}{x[1]}", align_bytes=64) for x in pairs if x[1] == 0}
         g_scales = {x: held.tile([P, C], U8, name=f"gs{x[0]}{x[1]}", align_bytes=64)[:] for x in pairs if x[1] == 1}
         for e in range(E):
             g_scales[e, 0] = heirs.tile([P, C], U8, name=f"gs{e}0", offset=e * C, align_bytes=64)[:]
-        last = heirs.tile([P, (PACK + 1) * C], F32, name="last", offset=E * C, align_bytes=64)
+        last = held.tile([P, (PACK + 1) * C], F32, name="last", align_bytes=64)
         g[1, 1] = last[:, 0 : PACK * C].rearrange("p (t c) -> p t c", t=PACK)
         slope = {
             (e, s, r): held.tile([P, 2, PASS], F32, name=f"slope{e}{s}{r}", align_bytes=64) for e, s in pairs for r in range(2)
         }
-        gi[0, 1] = last[:, (PACK - 1) * C : (PACK + 1) * C].bitcast(BF16)
+        gi[0, 0] = last[:, C : 3 * C].bitcast(BF16)
+        gi[0, 1] = last[:, 3 * C : 5 * C].bitcast(BF16)
         da_t = {(e, s, q): held.tile([P, PASS], BF16, name=f"da{e}{s}{q}") for e, s in pairs for q in range(Q)}
         dai = {x: held.tile([P, C * PACK], BF16, name=f"dai{x[0]}{x[1]}", align_bytes=64) for x in pairs if x != (1, 1)}
         dai[1, 1] = tail.tile([P, C * PACK], BF16, name="dai11", offset=0, align_bytes=64)
@@ -116,7 +119,7 @@ def tile_moe_bdx_mlp_relu2_kernel(
         da_scales[1, 0] = tail.tile([P, C], U8, name="ds10", offset=0, align_bytes=64)
         dx_rest = tail.tile([P, C - SPLIT], F32, name="dx_rest", offset=C, align_bytes=64)
         dx = {(e, k): held.tile([P, C], F32, name=f"dx{e}{k}") for e in range(E) for k in range(KT)}
-        win_name = ["slope101", "win1"]
+        win_name = ["slope110", "win1"]
         win, banks = {}, {}
 
         def quantize(codes, scales, src):
@@ -171,7 +174,7 @@ def tile_moe_bdx_mlp_relu2_kernel(
             )
 
         def derive(e, si, q):
-            if (e, si, q) in ((0, 1, 1), (1, 0, 0), (1, 1, 1), (1, 1, 2), (1, 1, 3), ):
+            if (e, si, q) in ((0, 1, 0), (1, 0, 0), (1, 1, 2), (1, 1, 3), ):
                 dh = held.tile([P, PASS], F32, name=f"dh{e}{si}{q}")
                 nc.scalar.copy(
                     out=dh[:].rearrange("c (u p d) -> c u p d", u=2, d=2),
@@ -232,21 +235,22 @@ def tile_moe_bdx_mlp_relu2_kernel(
                 turn_a(0, si, q // 2, q % 2, f"B{q}")
         weave_g(0, 0)
         weave_g(1, 0)
-        for t in range(PACK):
-            gather(0, 1, t)
-        weave_g(0, 1)
-        quantize_g(0, 0)
+        gather(0, 1, 0)
         gather(1, 1, 0)
-        quantize_g(1, 0)
+        for t in range(1, PACK):
+            gather(0, 1, t)
+        quantize_g(0, 0)
+        weave_g(0, 1)
         for q in range(Q):
             turn_a(1, 0, q // 2, q % 2, f"B{q}")
         for q in range(Q):
             first(0, 0, q, 0, f"A{q}")
         for r in range(2):
             turn_a(1, 1, 0, r, f"B{r}")
+        quantize_g(1, 0)
         gather(1, 1, 1)
-        quantize_g(0, 1)
         gather(1, 1, 2)
+        quantize_g(0, 1)
         gather(1, 1, 3)
         weave_g(1, 1)
         for q in range(2):
@@ -260,10 +264,10 @@ def tile_moe_bdx_mlp_relu2_kernel(
             first(0, 1, q, 1)
         for q in range(Q):
             derive(0, 0, q)
-        derive(0, 1, 1)
+        derive(0, 1, 0)
         turn_da(0, 0, 0, "A2")
         turn_da(0, 0, 1, "A3")
-        derive(0, 1, 0)
+        derive(0, 1, 1)
         derive(0, 1, 2)
         derive(0, 1, 3)
         for q in range(2):
@@ -283,7 +287,6 @@ def tile_moe_bdx_mlp_relu2_kernel(
         for q in range(2):
             first(1, 1, q, 0, f"B{2 + q}")
             first(1, 1, q, 1)
-        derive(1, 1, 1)
         second(0, 0, 0, "A0")
         second(0, 0, 1)
         drain(dx[0, 0][:], 0, 0, 0, C)
@@ -293,6 +296,7 @@ def tile_moe_bdx_mlp_relu2_kernel(
         derive(1, 0, 2)
         derive(1, 0, 3)
         derive(1, 1, 0)
+        derive(1, 1, 1)
         derive(1, 1, 2)
         derive(1, 1, 3)
         second(0, 1, 0, "A1")

@@ -27,34 +27,39 @@ def tile_moe_bdx_mlp_relu2_kernel(
 ):
     nc = tc.nc
     SN, SI, KT, Q = N // PASS, H // PASS, K // P, C // P
-
-
+    STRIPE = 16
+    ROWS = 4
+    ALIGN = 64
     SPLIT = 224
+    ON_GPSIMD = ((0, 1, 0), (1, 0, 0), (1, 1, Q - 2), (1, 1, Q - 1))
 
     with ExitStack() as ctx:
         held = ctx.enter_context(tc.tile_pool(name="held", bufs=1))
         heirs = ctx.enter_context(tc.tile_pool(name="heirs", bufs=1))
-        tail = ctx.enter_context(tc.tile_pool(name="tail", bufs=1))
         psum = ctx.enter_context(tc.psum_pool(name="psum", bufs=1))
 
-        pairs = [(e, s) for e in range(E) for s in range(2)]
-        offsets = held.tile([P, E * C // 16], U16, name="offsets")
-        dy_t = [[held.tile([P, T], F32, name=f"dy{s}{t}") for t in range(PACK)] for s in range(SN)]
-        g = {x: held.tile([P, PACK, C], F32, name=f"g{x[0]}{x[1]}", align_bytes=64)[:] for x in pairs if x != (1, 1)}
-        gate_t = [heirs.tile([P, C], F32, name="gate0", offset=0, align_bytes=64)[:], held.tile([P, C], F32, name="gate1")[:]]
-        a_t = {(e, s, h): held.tile([P, 2, C], F32, name=f"a{e}{s}{h}", align_bytes=64) for e, s in pairs for h in range(2)}
-        w2_t = [held.tile([P, SN, 2 * H], U8, name=f"w2{e}", align_bytes=64) for e in range(E)]
-        w2s_t = [held.tile([P, SN, H], U8, name=f"w2s{e}", align_bytes=64) for e in range(E)]
-        w1_t = held.tile([P, E * SI, 2 * K], U8, name="w1t", align_bytes=64)
-        w1s_t = held.tile([P, E * SI, K], U8, name="w1s", align_bytes=64)
+        groups = [(e, s) for e in range(E) for s in range(2)]
+        offsets = held.tile([P, E * C // STRIPE], U16, name="offsets")
+        dy_t = [[held.tile([P, T], F32, name=f"dy{sn}{t}") for t in range(PACK)] for sn in range(SN)]
+        g = {x: held.tile([P, PACK, C], F32, name=f"g{x[0]}{x[1]}", align_bytes=ALIGN)[:] for x in groups if x != (1, 1)}
+        gate_t = [heirs.tile([P, C], F32, name="gate0", offset=0, align_bytes=ALIGN)[:], held.tile([P, C], F32, name="gate1")[:]]
+        a_t = {
+            (e, si, half): held.tile([P, 2, C], F32, name=f"a{e}{si}{half}", align_bytes=ALIGN)
+            for e, si in groups
+            for half in range(2)
+        }
+        w2_t = [held.tile([P, SN, 2 * H], U8, name=f"w2{e}", align_bytes=ALIGN) for e in range(E)]
+        w2s_t = [held.tile([P, SN, H], U8, name=f"w2s{e}", align_bytes=ALIGN) for e in range(E)]
+        w1_t = held.tile([P, E * SI, 2 * K], U8, name="w1t", align_bytes=ALIGN)
+        w1s_t = held.tile([P, E * SI, K], U8, name="w1s", align_bytes=ALIGN)
         ident = held.tile([P, P], F32, name="ident")
 
         dy_v = dyT.rearrange("(s p t) c -> s t p c", p=P, t=PACK)
         a_v = a.rearrange("(s h j p) (e c) -> e s h p j c", p=P, j=2, e=E, h=2)
         w2_v = w2_words.bitcast(I32).rearrange("e s p b -> e p s b")
-        w2s_v = w2_scales.bitcast(I32).rearrange("e s (q r) i -> e r q s i", r=4)
+        w2s_v = w2_scales.bitcast(I32).rearrange("e s (x r) i -> e r x s i", r=ROWS)
         w1_v = w1_words.bitcast(I32).rearrange("e s p b -> p (e s) b")
-        w1s_v = w1_scales.bitcast(I32).rearrange("e s (q r) i -> r q (e s) i", r=4)
+        w1s_v = w1_scales.bitcast(I32).rearrange("e s (x r) i -> r x (e s) i", r=ROWS)
 
         nc.sync.dma_start(offsets[:], offs)
         for e in range(E):
@@ -62,32 +67,26 @@ def tile_moe_bdx_mlp_relu2_kernel(
         nc.vector.memset(w1s_t[:].bitcast(I32), 0)
         make_identity(nc, ident[:])
 
-        def load_dy(s, t):
-            nc.sync.dma_start(dy_t[s][t][:], dy_v[s, t])
+        def load_dy(sn, t):
+            nc.sync.dma_start(dy_t[sn][t][:], dy_v[sn, t])
+
+        def load_a(e, si, half):
+            nc.sync.dma_start(a_t[e, si, half][:], a_v[e, si, half])
 
         def load_w2(e):
             nc.sync.dma_start(w2_t[e][:].bitcast(I32), w2_v[e])
-            for r in range(4):
-                nc.sync.dma_start(w2s_t[e][r:P:32, :, :].bitcast(I32), w2s_v[e, r])
-
-        def load_a(e, s, h):
-            nc.sync.dma_start(a_t[e, s, h][:], a_v[e, s, h])
+            for row in range(ROWS):
+                nc.sync.dma_start(w2s_t[e][row:P:32, :, :].bitcast(I32), w2s_v[e, row])
 
         load_dy(0, 0)
         nc.sync.dma_start(gate_t[0][:, 0:P], gate[0:P, 0:P])
         nc.sync.dma_start(gate_t[0][:, P:C], gate[0:P, P:C])
         nc.sync.dma_start(gate_t[1], gate[0:P, C : 2 * C])
-        load_dy(0, 1)
-        load_a(0, 0, 0)
-        load_dy(0, 2)
-        load_a(0, 0, 1)
-        load_dy(0, 3)
-        load_a(0, 1, 0)
-        load_dy(1, 0)
-        load_a(0, 1, 1)
-        load_dy(1, 1)
-        load_dy(1, 2)
-        load_dy(1, 3)
+        for block in range(2 * SI):
+            load_dy(*divmod(block + 1, PACK))
+            load_a(0, *divmod(block, 2))
+        for t in range(1, PACK):
+            load_dy(1, t)
         load_a(1, 0, 0)
         load_w2(0)
         load_a(1, 0, 1)
@@ -95,229 +94,230 @@ def tile_moe_bdx_mlp_relu2_kernel(
         load_a(1, 1, 1)
         load_w2(1)
         nc.sync.dma_start(w1_t[:].bitcast(I32), w1_v)
-        for r in range(4):
-            nc.sync.dma_start(w1s_t[r:P:32, :, :].bitcast(I32), w1s_v[r])
+        for row in range(ROWS):
+            nc.sync.dma_start(w1s_t[row:P:32, :, :].bitcast(I32), w1s_v[row])
 
-        gi = {}
-        gi_name = {(1, 0): "a011", (1, 1): "gi11"}
-        g_codes = {x: held.tile([P, C], U32, name=f"gc{x[0]}{x[1]}", align_bytes=64) for x in pairs if x[1] == 0}
-        g_scales = {x: held.tile([P, C], U8, name=f"gs{x[0]}{x[1]}", align_bytes=64)[:] for x in pairs if x[1] == 1}
+        g_codes = {(e, 0): held.tile([P, C], U32, name=f"gc{e}0", align_bytes=ALIGN) for e in range(E)}
+        g_scales = {(e, 1): held.tile([P, C], U8, name=f"gs{e}1", align_bytes=ALIGN)[:] for e in range(E)}
         for e in range(E):
-            g_scales[e, 0] = heirs.tile([P, C], U8, name=f"gs{e}0", offset=e * C, align_bytes=64)[:]
-        last = held.tile([P, (PACK + 1) * C], F32, name="last", align_bytes=64)
-        g[1, 1] = last[:, 0 : PACK * C].rearrange("p (t c) -> p t c", t=PACK)
+            g_scales[e, 0] = heirs.tile([P, C], U8, name=f"gs{e}0", offset=e * C, align_bytes=ALIGN)[:]
+        shared = held.tile([P, (PACK + 1) * C], F32, name="shared", align_bytes=ALIGN)
+        g[1, 1] = shared[:, 0 : PACK * C].rearrange("p (t c) -> p t c", t=PACK)
+        g_woven = {(0, 0): shared[:, C : 3 * C].bitcast(BF16), (0, 1): shared[:, 3 * C : 5 * C].bitcast(BF16)}
         slope = {
-            (e, s, r): held.tile([P, 2, PASS], F32, name=f"slope{e}{s}{r}", align_bytes=64) for e, s in pairs for r in range(2)
+            (e, si, pair): held.tile([P, 2, PASS], F32, name=f"slope{e}{si}{pair}", align_bytes=ALIGN)
+            for e, si in groups
+            for pair in range(Q // 2)
         }
-        gi[0, 0] = last[:, C : 3 * C].bitcast(BF16)
-        gi[0, 1] = last[:, 3 * C : 5 * C].bitcast(BF16)
-        da_t = {(e, s, q): held.tile([P, PASS], BF16, name=f"da{e}{s}{q}") for e, s in pairs for q in range(Q)}
-        dai = {x: held.tile([P, C * PACK], BF16, name=f"dai{x[0]}{x[1]}", align_bytes=64) for x in pairs if x != (1, 1)}
-        dai[1, 1] = tail.tile([P, C * PACK], BF16, name="dai11", offset=0, align_bytes=64)
-        da_codes = {x: held.tile([P, C], U32, name=f"dc{x[0]}{x[1]}", align_bytes=64) for x in pairs}
-        da_scales = {x: held.tile([P, C], U8, name=f"ds{x[0]}{x[1]}", align_bytes=64) for x in pairs if x != (1, 0)}
-        da_scales[1, 0] = tail.tile([P, C], U8, name="ds10", offset=0, align_bytes=64)
-        dx_rest = tail.tile([P, C - SPLIT], F32, name="dx_rest", offset=C, align_bytes=64)
-        dx = {(e, k): held.tile([P, C], F32, name=f"dx{e}{k}") for e in range(E) for k in range(KT)}
-        win_name = ["slope110", "win1"]
-        win, banks = {}, {}
+        da_t = {(e, si, q): held.tile([P, PASS], BF16, name=f"da{e}{si}{q}") for e, si in groups for q in range(Q)}
+        da_woven = {x: held.tile([P, C * PACK], BF16, name=f"daw{x[0]}{x[1]}", align_bytes=ALIGN) for x in groups}
+        da_codes = {x: held.tile([P, C], U32, name=f"dc{x[0]}{x[1]}", align_bytes=ALIGN) for x in groups}
+        da_scales = {x: held.tile([P, C], U8, name=f"ds{x[0]}{x[1]}", align_bytes=ALIGN) for x in groups}
+        dh_bank, dx_bank = {}, {}
 
-        def quantize(codes, scales, src):
-            nc.vector.quantize_mx(out=codes[:].bitcast(E5M2), scales=scales[:], in_=src)
+        def bank_tile(shape, bank):
+            return psum.tile(shape, F32, name=f"bank{bank}")
 
-        def gather(e, s, t, c0=0, c1=C):
-            o = offsets[:, (e * C + c0) // 16 : (e * C + c1) // 16]
-            nc.vector.tensor_tensor(g[e, s][:, t, c0:c1], dy_t[s][t][:].indirect(o), gate_t[e][:, c0:c1], ALU.mult)
+        def slots(e, c0, c1):
+            return offsets[:, (e * C + c0) // STRIPE : (e * C + c1) // STRIPE]
 
-        def weave_g(e, s):
-            if (e, s) in gi_name:
-                gi[e, s] = held.tile([P, C * PACK], BF16, name=gi_name[e, s], align_bytes=64)[:]
-            if (e, s) in ((1, 1), ):
-                nc.gpsimd.tensor_scalar(
-                    gi[e, s].rearrange("p (c t) -> p c t", t=PACK), g[e, s].rearrange("p t c -> p c t"), 1.0, 0.0, ALU.mult, ALU.add
-                )
-                return
+        def gather(e, sn, t, c0=0, c1=C):
+            window = dy_t[sn][t][:].indirect(slots(e, c0, c1))
+            nc.vector.tensor_tensor(g[e, sn][:, t, c0:c1], window, gate_t[e][:, c0:c1], ALU.mult)
+
+        def weave_on_scalar(e, sn):
             nc.scalar.copy(
-                out=gi[e, s].rearrange("p (c i t) -> p c t i", i=4, t=PACK),
-                in_=g[e, s].rearrange("p t (c i) -> p c t i", i=4),
+                out=g_woven[e, sn].rearrange("p (c v t) -> p c t v", v=4, t=PACK),
+                in_=g[e, sn].rearrange("p t (c v) -> p c t v", v=4),
             )
 
-        def quantize_g(e, s):
-            if s == 1:
-                g_codes[e, s] = held.tile([P, C], U32, name=("a101", "slope011")[e], align_bytes=64)
-            quantize(g_codes[e, s], g_scales[e, s], gi[e, s])
+        def weave_on_gpsimd(e, sn):
+            nc.gpsimd.tensor_scalar(
+                g_woven[e, sn].rearrange("p (c t) -> p c t", t=PACK), g[e, sn].rearrange("p t c -> p c t"), 1.0, 0.0, ALU.mult, ALU.add
+            )
 
-        def turn_a(e, si, h, r, name):
-            bank = psum.tile([P, 2, 2 * P], F32, name=name)
+        def quantize_g(e, sn):
+            nc.vector.quantize_mx(out=g_codes[e, sn][:].bitcast(E5M2), scales=g_scales[e, sn], in_=g_woven[e, sn])
+
+        def quantize_da(e, si):
+            nc.vector.quantize_mx(out=da_codes[e, si][:].bitcast(E5M2), scales=da_scales[e, si][:], in_=da_woven[e, si][:])
+
+        def turn_a(e, si, half, pair, bank):
+            turned = bank_tile([P, 2, 2 * P], bank)
             for ql in range(2):
+                q = 2 * pair + ql
                 for j in range(2):
-                    q = 2 * r + ql
-                    nc.tensor.transpose(bank[:, ql, j * P : (j + 1) * P], a_t[e, si, h][:, j, q * P : (q + 1) * P], ident[:])
+                    nc.tensor.transpose(turned[:, ql, j * P : (j + 1) * P], a_t[e, si, half][:, j, q * P : (q + 1) * P], ident[:])
             nc.scalar.activation(
-                out=slope[e, si, r][:].rearrange("c q (u h p d) -> c h u q p d", u=2, h=2, d=2)[:, h],
-                in_=bank[:].rearrange("c q (p u d) -> c u q p d", u=2, d=2),
+                out=slope[e, si, pair][:].rearrange("c q (u h p d) -> c h u q p d", u=2, h=2, d=2)[:, half],
+                in_=turned[:].rearrange("c q (p u d) -> c u q p d", u=2, d=2),
                 func=RELU,
                 scale=2.0,
             )
 
-        def first(e, si, q, s, name=None):
-            if s == 0:
-                banks[e, si, q] = psum.tile([P, PASS], F32, name=name)
+        def first_product(e, si, q, sn, bank=None):
+            if sn == 0:
+                dh_bank[e, si, q] = bank_tile([P, PASS], bank)
             nc.tensor.matmul_mx(
-                out=banks[e, si, q][:],
-                lhsT=g_codes[e, s][:, q * P : (q + 1) * P].bitcast(E5M2),
-                lhsT_scale=g_scales[e, s][:, q * P : (q + 1) * P],
-                rhs=w2_t[e][:, s, 2 * si * PASS : 2 * (si + 1) * PASS].bitcast(E2M1),
-                rhs_scale=w2s_t[e][:, s, si * PASS : (si + 1) * PASS],
-                start=(s == 0),
-                stop=(s == SN - 1),
+                out=dh_bank[e, si, q][:],
+                lhsT=g_codes[e, sn][:, q * P : (q + 1) * P].bitcast(E5M2),
+                lhsT_scale=g_scales[e, sn][:, q * P : (q + 1) * P],
+                rhs=w2_t[e][:, sn, 2 * si * PASS : 2 * (si + 1) * PASS].bitcast(E2M1),
+                rhs_scale=w2s_t[e][:, sn, si * PASS : (si + 1) * PASS],
+                start=(sn == 0),
+                stop=(sn == SN - 1),
             )
+
+        def both_passes(e, si, q, bank):
+            first_product(e, si, q, 0, bank)
+            first_product(e, si, q, 1)
 
         def derive(e, si, q):
-            if (e, si, q) in ((0, 1, 0), (1, 0, 0), (1, 1, 2), (1, 1, 3), ):
-                dh = held.tile([P, PASS], F32, name=f"dh{e}{si}{q}")
-                nc.scalar.copy(
-                    out=dh[:].rearrange("c (u p d) -> c u p d", u=2, d=2),
-                    in_=banks[e, si, q][:].rearrange("c (p u d) -> c u p d", u=2, d=2),
+            dh = dh_bank[e, si, q][:].rearrange("c (p u d) -> c u p d", u=2, d=2)
+            factor = slope[e, si, q // 2][:, q % 2, :]
+            if (e, si, q) in ON_GPSIMD:
+                dh_copy = held.tile([P, PASS], F32, name=f"dh{e}{si}{q}")
+                nc.scalar.copy(out=dh_copy[:].rearrange("c (u p d) -> c u p d", u=2, d=2), in_=dh)
+                nc.gpsimd.tensor_tensor(da_t[e, si, q][:], dh_copy[:], factor, ALU.mult)
+            else:
+                nc.vector.tensor_tensor(
+                    da_t[e, si, q][:].rearrange("c (u p d) -> c u p d", u=2, d=2),
+                    dh,
+                    factor.rearrange("c (u p d) -> c u p d", u=2, d=2),
+                    ALU.mult,
                 )
-                nc.gpsimd.tensor_tensor(da_t[e, si, q][:], dh[:], slope[e, si, q // 2][:, q % 2, :], ALU.mult)
-                return
-            nc.vector.tensor_tensor(
-                da_t[e, si, q][:].rearrange("c (u p d) -> c u p d", u=2, d=2),
-                banks[e, si, q][:].rearrange("c (p u d) -> c u p d", u=2, d=2),
-                slope[e, si, q // 2][:, q % 2, :].rearrange("c (u p d) -> c u p d", u=2, d=2),
-                ALU.mult,
-            )
 
-        def turn_da(e, si, h, name):
-            bank = psum.tile([P, 2, 2, P], F32, name=name)
+        def turn_da(e, si, pair, bank):
+            turned = bank_tile([P, 2, 2, P], bank)
             for ql in range(2):
-                words = da_t[e, si, 2 * h + ql][:].bitcast(F32)
+                words = da_t[e, si, 2 * pair + ql][:].bitcast(F32)
                 for u in range(2):
-                    nc.tensor.transpose(bank[:, ql, u, :], words[:, u * P : (u + 1) * P], ident[:])
+                    nc.tensor.transpose(turned[:, ql, u, :], words[:, u * P : (u + 1) * P], ident[:])
+            woven_words = da_woven[e, si][:, pair * 2 * PASS : (pair + 1) * 2 * PASS].bitcast(F32)
             nc.scalar.copy(
-                out=dai[e, si][:, h * C * 2 : (h + 1) * C * 2].bitcast(F32).rearrange("p (q c u) -> p q c u", q=2, u=2),
-                in_=bank[:].rearrange("p q u c -> p q c u"),
+                out=woven_words.rearrange("p (q c u) -> p q c u", q=2, u=2),
+                in_=turned[:].rearrange("p q u c -> p q c u"),
             )
 
-        def quantize_da(e, si):
-            quantize(da_codes[e, si], da_scales[e, si], dai[e, si][:])
-
-        def second(e, k, s, name=None):
-            if s == 0:
-                banks[e, k] = psum.tile([P, C], F32, name=name)
+        def second_product(e, k, si, bank=None):
+            if si == 0:
+                dx_bank[e, k] = bank_tile([P, C], bank)
             nc.tensor.matmul_mx(
-                out=banks[e, k][:],
-                lhsT=w1_t[:, e * SI + (s + e) % SI, 2 * k * P : 2 * (k + 1) * P].bitcast(E2M1),
-                lhsT_scale=w1s_t[:, e * SI + (s + e) % SI, k * P : (k + 1) * P],
-                rhs=da_codes[e, (s + e) % SI][:].bitcast(E5M2),
-                rhs_scale=da_scales[e, (s + e) % SI][:],
-                start=(s == 0),
-                stop=(s == SI - 1),
+                out=dx_bank[e, k][:],
+                lhsT=w1_t[:, e * SI + si, 2 * k * P : 2 * (k + 1) * P].bitcast(E2M1),
+                lhsT_scale=w1s_t[:, e * SI + si, k * P : (k + 1) * P],
+                rhs=da_codes[e, si][:].bitcast(E5M2),
+                rhs_scale=da_scales[e, si][:],
+                start=(si == 0),
+                stop=(si == SI - 1),
             )
 
-        def drain(dst, e, k, c0, c1):
-            nc.scalar.copy(out=dst, in_=banks[e, k][:, c0:c1])
+        def drain(e, k, c0, c1, name):
+            dx = held.tile([P, c1 - c0], F32, name=name)
+            nc.scalar.copy(out=dx[:], in_=dx_bank[e, k][:, c0:c1])
+            return dx
 
-        def scatter(src, e, k, c0, c1):
-            if k not in win:
-                win[k] = held.tile([P, T], F32, name=win_name[k], align_bytes=64)
-            nc.vector.tensor_copy(win[k][:].indirect(offsets[:, (e * C + c0) // 16 : (e * C + c1) // 16]), src)
+        def scatter(window, dx, e, c0, c1):
+            nc.vector.tensor_copy(window[:].indirect(slots(e, c0, c1)), dx[:])
 
         gather(0, 0, 0, 0, P)
         gather(0, 0, 0, P, C)
         gather(1, 0, 0)
         for t in range(1, PACK):
-            gather(0, 0, t)
-            gather(1, 0, t)
+            for e in range(E):
+                gather(e, 0, t)
         for si in range(SI):
-            for q in range(Q):
-                turn_a(0, si, q // 2, q % 2, f"B{q}")
-        weave_g(0, 0)
-        weave_g(1, 0)
-        gather(0, 1, 0)
-        gather(1, 1, 0)
+            for half in range(2):
+                for pair in range(2):
+                    turn_a(0, si, half, pair, 4 + 2 * half + pair)
+        weave_on_scalar(0, 0)
+        g_woven[1, 0] = held.tile([P, C * PACK], BF16, name="a011", align_bytes=ALIGN)[:]
+        weave_on_scalar(1, 0)
+
+        for e in range(E):
+            gather(e, 1, 0)
         for t in range(1, PACK):
             gather(0, 1, t)
         quantize_g(0, 0)
-        weave_g(0, 1)
+        weave_on_scalar(0, 1)
+        for half in range(2):
+            for pair in range(2):
+                turn_a(1, 0, half, pair, 4 + 2 * half + pair)
         for q in range(Q):
-            turn_a(1, 0, q // 2, q % 2, f"B{q}")
-        for q in range(Q):
-            first(0, 0, q, 0, f"A{q}")
-        for r in range(2):
-            turn_a(1, 1, 0, r, f"B{r}")
+            first_product(0, 0, q, 0, q)
+        for pair in range(2):
+            turn_a(1, 1, 0, pair, 4 + pair)
         quantize_g(1, 0)
         gather(1, 1, 1)
         gather(1, 1, 2)
+        g_codes[0, 1] = held.tile([P, C], U32, name="a101", align_bytes=ALIGN)
         quantize_g(0, 1)
         gather(1, 1, 3)
-        weave_g(1, 1)
+        g_woven[1, 1] = held.tile([P, C * PACK], BF16, name="gw11", align_bytes=ALIGN)[:]
+        weave_on_gpsimd(1, 1)
+
         for q in range(2):
-            first(0, 0, q, 1)
-        for r in range(2):
-            turn_a(1, 1, 1, r, f"B{2 + r}")
+            first_product(0, 0, q, 1)
+        for pair in range(2):
+            turn_a(1, 1, 1, pair, 6 + pair)
         for q in range(2, Q):
-            first(0, 0, q, 1)
+            first_product(0, 0, q, 1)
         for q in range(Q):
-            first(0, 1, q, 0, f"B{q}")
-            first(0, 1, q, 1)
+            both_passes(0, 1, q, 4 + q)
         for q in range(Q):
             derive(0, 0, q)
         derive(0, 1, 0)
-        turn_da(0, 0, 0, "A2")
-        turn_da(0, 0, 1, "A3")
-        derive(0, 1, 1)
-        derive(0, 1, 2)
-        derive(0, 1, 3)
+        for pair in range(2):
+            turn_da(0, 0, pair, 2 + pair)
+        for q in range(1, Q):
+            derive(0, 1, q)
         for q in range(2):
-            first(1, 0, q, 0, f"A{q}")
-        turn_da(0, 1, 0, "B0")
-        turn_da(0, 1, 1, "B1")
+            first_product(1, 0, q, 0, q)
+        for pair in range(2):
+            turn_da(0, 1, pair, 4 + pair)
+
+        g_codes[1, 1] = held.tile([P, C], U32, name="slope011", align_bytes=ALIGN)
         quantize_g(1, 1)
         for q in range(2):
-            first(1, 0, q, 1)
+            first_product(1, 0, q, 1)
         derive(1, 0, 0)
         for q in range(2, Q):
-            first(1, 0, q, 0, f"A{q}")
-            first(1, 0, q, 1)
+            both_passes(1, 0, q, q)
         quantize_da(0, 0)
         derive(1, 0, 1)
         quantize_da(0, 1)
         for q in range(2):
-            first(1, 1, q, 0, f"B{2 + q}")
-            first(1, 1, q, 1)
-        second(0, 0, 0, "A0")
-        second(0, 0, 1)
-        drain(dx[0, 0][:], 0, 0, 0, C)
+            both_passes(1, 1, q, 6 + q)
+        second_product(0, 0, 0, 0)
+        second_product(0, 0, 1)
+        dx00 = drain(0, 0, 0, C, "dx00")
         for q in range(2, Q):
-            first(1, 1, q, 0, f"B{q - 2}")
-            first(1, 1, q, 1)
-        derive(1, 0, 2)
-        derive(1, 0, 3)
-        derive(1, 1, 0)
-        derive(1, 1, 1)
-        derive(1, 1, 2)
-        derive(1, 1, 3)
-        second(0, 1, 0, "A1")
-        second(0, 1, 1)
-        drain(dx[0, 1][:, 0 : SPLIT], 0, 1, 0, SPLIT)
-        turn_da(1, 1, 0, "B2")
-        turn_da(1, 1, 1, "B3")
-        turn_da(1, 0, 0, "A2")
-        turn_da(1, 0, 1, "A3")
-        scatter(dx[0, 0][:], 0, 0, 0, C)
-        scatter(dx[0, 1][:, 0 : SPLIT], 0, 1, 0, SPLIT)
-        quantize_da(1, 1)
-        drain(dx_rest[:], 0, 1, SPLIT, C)
-        second(1, 0, 0, "A0")
+            both_passes(1, 1, q, 2 + q)
+        for q in range(2, Q):
+            derive(1, 0, q)
+        for q in range(Q):
+            derive(1, 1, q)
+        second_product(0, 1, 0, 1)
+        second_product(0, 1, 1)
+        dx01_first = drain(0, 1, 0, SPLIT, "dx01")
+        for pair in range(2):
+            turn_da(1, 0, pair, 2 + pair)
+        for pair in range(2):
+            turn_da(1, 1, pair, 6 + pair)
+        dx01_rest = drain(0, 1, SPLIT, C, f"da11{Q - 1}")
+
+        windows = [held.tile([P, T], F32, name=name, align_bytes=ALIGN) for name in ("slope101", "window1")]
+        scatter(windows[0], dx00, 0, 0, C)
+        scatter(windows[1], dx01_first, 0, 0, SPLIT)
         quantize_da(1, 0)
-        second(1, 0, 1)
-        drain(dx[1, 0][:], 1, 0, 0, C)
-        second(1, 1, 0, "A0")
-        second(1, 1, 1)
-        drain(dx[1, 1][:], 1, 1, 0, C)
-        scatter(dx_rest[:], 0, 1, SPLIT, C)
+        second_product(1, 0, 0, 0)
+        quantize_da(1, 1)
+        second_product(1, 0, 1)
+        dx1 = [drain(1, 0, 0, C, "dx10")]
+        second_product(1, 1, 0, 0)
+        second_product(1, 1, 1)
+        dx1.append(drain(1, 1, 0, C, "dx11"))
+        scatter(windows[1], dx01_rest, 0, SPLIT, C)
         for k in range(KT):
-            scatter(dx[1, k][:], 1, k, 0, C)
-            nc.sync.dma_start(out[k * P : (k + 1) * P, :], win[k][:])
+            scatter(windows[k], dx1[k], 1, 0, C)
+            nc.sync.dma_start(out[k * P : (k + 1) * P, :], windows[k][:])

@@ -1,7 +1,6 @@
 from contextlib import ExitStack
 
 import concourse.mybir as mybir
-from concourse.masks import make_identity
 
 K, T, E, C, H, N = 256, 1024, 2, 512, 1024, 1024
 P = 128
@@ -19,7 +18,7 @@ U8 = mybir.dt.uint8
 E5M2 = mybir.dt.float8_e5m2_x4
 E2M1 = mybir.dt.float4_e2m1fn_x4
 ALU = mybir.AluOpType
-RELU = mybir.ActivationFunctionType.Relu
+COPY = mybir.ActivationFunctionType.Copy
 
 
 def tile_moe_bdx_mlp_relu2_kernel(
@@ -30,294 +29,232 @@ def tile_moe_bdx_mlp_relu2_kernel(
     STRIPE = 16
     ROWS = 4
     ALIGN = 64
-    SPLIT = 224
-    ON_GPSIMD = ((0, 1, 0), (1, 0, 0), (1, 1, Q - 2), (1, 1, Q - 1))
+    PIECES = (((0, 256), (256, 256)), ((0, 256), (256, 128), (384, 128)))
 
     with ExitStack() as ctx:
         held = ctx.enter_context(tc.tile_pool(name="held", bufs=1))
-        heirs = ctx.enter_context(tc.tile_pool(name="heirs", bufs=1))
         psum = ctx.enter_context(tc.psum_pool(name="psum", bufs=1))
+
+        def tile(shape, dtype, name):
+            return held.tile(shape, dtype, name=name, align_bytes=ALIGN)
 
         groups = [(e, s) for e in range(E) for s in range(2)]
         offsets = held.tile([P, E * C // STRIPE], U16, name="offsets")
-        dy_t = [[held.tile([P, T], F32, name=f"dy{sn}{t}") for t in range(PACK)] for sn in range(SN)]
-        g = {x: held.tile([P, PACK, C], F32, name=f"g{x[0]}{x[1]}", align_bytes=ALIGN)[:] for x in groups if x != (1, 1)}
-        gate_t = [heirs.tile([P, C], F32, name="gate0", offset=0, align_bytes=ALIGN)[:], held.tile([P, C], F32, name="gate1")[:]]
-        a_t = {
-            (e, si, half): held.tile([P, 2, C], F32, name=f"a{e}{si}{half}", align_bytes=ALIGN)
-            for e, si in groups
-            for half in range(2)
-        }
-        w2_t = [held.tile([P, SN, 2 * H], U8, name=f"w2{e}", align_bytes=ALIGN) for e in range(E)]
-        w2s_t = [held.tile([P, SN, H], U8, name=f"w2s{e}", align_bytes=ALIGN) for e in range(E)]
-        w1_t = held.tile([P, E * SI, 2 * K], U8, name="w1t", align_bytes=ALIGN)
-        w1s_t = held.tile([P, E * SI, K], U8, name="w1s", align_bytes=ALIGN)
-        ident = held.tile([P, P], F32, name="ident")
+        dy_t = [[tile([P, T], F32, f"dy{sn}{t}") for t in range(PACK)] for sn in range(SN)]
+        gate_t = [tile([P, C], F32, f"gate{e}") for e in range(E)]
+        a_t = {x: tile([P, PACK, C], F32, f"a{x[0]}{x[1]}") for x in groups}
+        w2_raw = [tile([P, SN, 2 * H], U8, f"w2raw{e}") for e in range(E)]
+        w2s_raw = tile([P, E * SN, H], U8, "w2sraw")
+        w2_t = {x: tile([P, 2 * H], U8, f"w2{x[0]}{x[1]}") for x in groups}
+        w2s_t = [tile([P, SN, H], U8, f"w2s{e}") for e in range(E)]
+        w1_t = tile([P, E * SI, 2 * K], U8, "w1t")
+        w1s_t = tile([P, E * SI, K], U8, "w1s")
 
         dy_v = dyT.rearrange("(s p t) c -> s t p c", p=P, t=PACK)
-        a_v = a.rearrange("(s h j p) (e c) -> e s h p j c", p=P, j=2, e=E, h=2)
+        a_v = a.rearrange("(s p t) (e c) -> e s p t c", p=P, t=PACK, e=E)
         w2_v = w2_words.bitcast(I32).rearrange("e s p b -> e p s b")
-        w2s_v = w2_scales.bitcast(I32).rearrange("e s (x r) i -> e r x s i", r=ROWS)
+        w2s_v = w2_scales.bitcast(I32).rearrange("e s (x r) i -> r x (e s) i", r=ROWS)
         w1_v = w1_words.bitcast(I32).rearrange("e s p b -> p (e s) b")
         w1s_v = w1_scales.bitcast(I32).rearrange("e s (x r) i -> r x (e s) i", r=ROWS)
 
         nc.sync.dma_start(offsets[:], offs)
-        for e in range(E):
-            nc.vector.memset(w2s_t[e][:].bitcast(I32), 0)
+        nc.vector.memset(w2s_raw[:].bitcast(I32), 0)
         nc.vector.memset(w1s_t[:].bitcast(I32), 0)
-        make_identity(nc, ident[:])
 
         def load_dy(sn, t):
             nc.sync.dma_start(dy_t[sn][t][:], dy_v[sn, t])
 
-        def load_a(e, si, half):
-            nc.sync.dma_start(a_t[e, si, half][:], a_v[e, si, half])
-
-        def load_w2(e):
-            nc.sync.dma_start(w2_t[e][:].bitcast(I32), w2_v[e])
-            for row in range(ROWS):
-                nc.sync.dma_start(w2s_t[e][row:P:32, :, :].bitcast(I32), w2s_v[e, row])
-
         load_dy(0, 0)
-        nc.sync.dma_start(gate_t[0][:, 0:P], gate[0:P, 0:P])
-        nc.sync.dma_start(gate_t[0][:, P:C], gate[0:P, P:C])
-        nc.sync.dma_start(gate_t[1], gate[0:P, C : 2 * C])
-        for block in range(2 * SI):
-            load_dy(*divmod(block + 1, PACK))
-            load_a(0, *divmod(block, 2))
+        nc.sync.dma_start(gate_t[1][:], gate[0:P, C : 2 * C])
         for t in range(1, PACK):
+            load_dy(0, t)
+        nc.sync.dma_start(gate_t[0][:], gate[0:P, 0:C])
+        for row in range(ROWS):
+            nc.sync.dma_start(w2s_raw[row:P:32, :, :].bitcast(I32), w2s_v[row])
+        for t in range(PACK):
             load_dy(1, t)
-        load_a(1, 0, 0)
-        load_w2(0)
-        load_a(1, 0, 1)
-        load_a(1, 1, 0)
-        load_a(1, 1, 1)
-        load_w2(1)
+        nc.sync.dma_start(w2_raw[0][:].bitcast(I32), w2_v[0])
+        for si in range(SI):
+            nc.sync.dma_start(a_t[0, si][:], a_v[0, si])
+        nc.sync.dma_start(w2_raw[1][:].bitcast(I32), w2_v[1])
         nc.sync.dma_start(w1_t[:].bitcast(I32), w1_v)
         for row in range(ROWS):
             nc.sync.dma_start(w1s_t[row:P:32, :, :].bitcast(I32), w1s_v[row])
+        for si in range(SI):
+            nc.sync.dma_start(a_t[1, si][:], a_v[1, si])
 
-        g_codes = {(e, 0): held.tile([P, C], U32, name=f"gc{e}0", align_bytes=ALIGN) for e in range(E)}
-        g_scales = {(e, 1): held.tile([P, C], U8, name=f"gs{e}1", align_bytes=ALIGN)[:] for e in range(E)}
+        g = {x: tile([P, PACK, C], F32, f"g{x[0]}{x[1]}") for x in groups if x != (1, 1)}
+        g_woven = {x: tile([P, C * PACK], BF16, f"gw{x[0]}{x[1]}") for x in groups}
+        g_codes = {x: tile([P, C], U32, f"gc{x[0]}{x[1]}") for x in groups}
+        g_scales = {x: tile([P, C], U8, f"gs{x[0]}{x[1]}") for x in groups}
+        da_woven, da_codes, da_scales = {}, {}, {}
         for e in range(E):
-            g_scales[e, 0] = heirs.tile([P, C], U8, name=f"gs{e}0", offset=e * C, align_bytes=ALIGN)[:]
-        shared = held.tile([P, (PACK + 1) * C], F32, name="shared", align_bytes=ALIGN)
-        g[1, 1] = shared[:, 0 : PACK * C].rearrange("p (t c) -> p t c", t=PACK)
-        g_woven = {(0, 0): shared[:, C : 3 * C].bitcast(BF16), (0, 1): shared[:, 3 * C : 5 * C].bitcast(BF16)}
-        slope = {
-            (e, si, pair): held.tile([P, 2, PASS], F32, name=f"slope{e}{si}{pair}", align_bytes=ALIGN)
-            for e, si in groups
-            for pair in range(Q // 2)
-        }
-        da_t = {(e, si, q): held.tile([P, PASS], BF16, name=f"da{e}{si}{q}") for e, si in groups for q in range(Q)}
-        da_woven = {x: held.tile([P, C * PACK], BF16, name=f"daw{x[0]}{x[1]}", align_bytes=ALIGN) for x in groups}
-        da_codes = {x: held.tile([P, C], U32, name=f"dc{x[0]}{x[1]}", align_bytes=ALIGN) for x in groups}
-        da_scales = {x: held.tile([P, C], U8, name=f"ds{x[0]}{x[1]}", align_bytes=ALIGN) for x in groups}
-        dh_bank, dx_bank = {}, {}
+            for c0, n in PIECES[e]:
+                da_woven[e, c0] = tile([P, SI, n * PACK], BF16, f"daw{e}{c0}")
+                da_codes[e, c0] = tile([P, SI, n], U32, f"dc{e}{c0}")
+                da_scales[e, c0] = tile([P, SI, n], U8, f"ds{e}{c0}")
+        windows = [tile([P, T], F32, f"window{k}") for k in range(KT)]
+        dh_bank = {}
 
         def bank_tile(shape, bank):
             return psum.tile(shape, F32, name=f"bank{bank}")
 
-        def slots(e, c0, c1):
-            return offsets[:, (e * C + c0) // STRIPE : (e * C + c1) // STRIPE]
+        def slots(c0, n, e):
+            return offsets[:, (e * C + c0) // STRIPE : (e * C + c0 + n) // STRIPE]
 
-        def gather(e, sn, t, c0=0, c1=C):
-            window = dy_t[sn][t][:].indirect(slots(e, c0, c1))
-            nc.vector.tensor_tensor(g[e, sn][:, t, c0:c1], window, gate_t[e][:, c0:c1], ALU.mult)
+        def gather_on_scalar(e, sn, t):
+            nc.scalar.activation(g[e, sn][:, t, :], dy_t[sn][t][:].indirect(slots(0, C, e)), COPY)
 
-        def weave_on_scalar(e, sn):
-            nc.scalar.copy(
-                out=g_woven[e, sn].rearrange("p (c v t) -> p c t v", v=4, t=PACK),
-                in_=g[e, sn].rearrange("p t (c v) -> p c t v", v=4),
+        def gather_gated(e, sn, t):
+            nc.vector.tensor_tensor(g[e, sn][:, t, :], dy_t[sn][t][:].indirect(slots(0, C, e)), gate_t[e][:], ALU.mult)
+
+        def weave_gating(e, sn):
+            nc.vector.tensor_tensor(
+                g_woven[e, sn][:].rearrange("p (c v t) -> p c t v", v=2, t=PACK),
+                g[e, sn][:].rearrange("p t (c v) -> p c t v", v=2),
+                gate_t[e][:].rearrange("p (c v) -> p c v", v=2).unsqueeze(2).to_broadcast([P, C // 2, PACK, 2]),
+                ALU.mult,
             )
 
-        def weave_on_gpsimd(e, sn):
-            nc.gpsimd.tensor_scalar(
-                g_woven[e, sn].rearrange("p (c t) -> p c t", t=PACK), g[e, sn].rearrange("p t c -> p c t"), 1.0, 0.0, ALU.mult, ALU.add
+        def weave(e, sn):
+            nc.vector.tensor_copy(
+                g_woven[e, sn][:].rearrange("p (c v t) -> p c t v", v=4, t=PACK),
+                g[e, sn][:].rearrange("p t (c v) -> p c t v", v=4),
             )
 
         def quantize_g(e, sn):
-            nc.vector.quantize_mx(out=g_codes[e, sn][:].bitcast(E5M2), scales=g_scales[e, sn], in_=g_woven[e, sn])
+            nc.vector.quantize_mx(out=g_codes[e, sn][:].bitcast(E5M2), scales=g_scales[e, sn][:], in_=g_woven[e, sn][:])
 
-        def quantize_da(e, si):
-            nc.vector.quantize_mx(out=da_codes[e, si][:].bitcast(E5M2), scales=da_scales[e, si][:], in_=da_woven[e, si][:])
+        def permute_words(e, sn):
+            nc.scalar.copy(
+                out=w2_t[e, sn][:].bitcast(U16).rearrange("p (s t m) -> p s t m", s=SI, t=PACK),
+                in_=w2_raw[e][:, sn, :].bitcast(U16).rearrange("p (s m t) -> p s t m", s=SI, t=PACK),
+            )
 
-        def turn_a(e, si, half, pair, bank):
-            turned = bank_tile([P, 2, 2 * P], bank)
-            for ql in range(2):
-                q = 2 * pair + ql
-                for j in range(2):
-                    nc.tensor.transpose(turned[:, ql, j * P : (j + 1) * P], a_t[e, si, half][:, j, q * P : (q + 1) * P], ident[:])
-            nc.scalar.activation(
-                out=slope[e, si, pair][:].rearrange("c q (u h p d) -> c h u q p d", u=2, h=2, d=2)[:, half],
-                in_=turned[:].rearrange("c q (p u d) -> c u q p d", u=2, d=2),
-                func=RELU,
-                scale=2.0,
+        def permute_scales(e):
+            nc.vector.tensor_copy(
+                w2s_t[e][:].rearrange("p n (s t m) -> p (n s) t m", s=SI, t=PACK),
+                w2s_raw[:, e * SN : (e + 1) * SN, :].rearrange("p n (s m t) -> p (n s) t m", s=SI, t=PACK),
             )
 
         def first_product(e, si, q, sn, bank=None):
             if sn == 0:
-                dh_bank[e, si, q] = bank_tile([P, PASS], bank)
-            nc.tensor.matmul_mx(
-                out=dh_bank[e, si, q][:],
-                lhsT=g_codes[e, sn][:, q * P : (q + 1) * P].bitcast(E5M2),
-                lhsT_scale=g_scales[e, sn][:, q * P : (q + 1) * P],
-                rhs=w2_t[e][:, sn, 2 * si * PASS : 2 * (si + 1) * PASS].bitcast(E2M1),
-                rhs_scale=w2s_t[e][:, sn, si * PASS : (si + 1) * PASS],
-                start=(sn == 0),
-                stop=(sn == SN - 1),
-            )
-
-        def both_passes(e, si, q, bank):
-            first_product(e, si, q, 0, bank)
-            first_product(e, si, q, 1)
-
-        def derive(e, si, q):
-            dh = dh_bank[e, si, q][:].rearrange("c (p u d) -> c u p d", u=2, d=2)
-            factor = slope[e, si, q // 2][:, q % 2, :]
-            if (e, si, q) in ON_GPSIMD:
-                dh_copy = held.tile([P, PASS], F32, name=f"dh{e}{si}{q}")
-                nc.scalar.copy(out=dh_copy[:].rearrange("c (u p d) -> c u p d", u=2, d=2), in_=dh)
-                nc.gpsimd.tensor_tensor(da_t[e, si, q][:], dh_copy[:], factor, ALU.mult)
-            else:
-                nc.vector.tensor_tensor(
-                    da_t[e, si, q][:].rearrange("c (u p d) -> c u p d", u=2, d=2),
-                    dh,
-                    factor.rearrange("c (u p d) -> c u p d", u=2, d=2),
-                    ALU.mult,
+                dh_bank[e, si, q] = bank_tile([P, PACK, P], bank)
+            for t in range(PACK):
+                col = si * PASS + t * P
+                nc.tensor.matmul_mx(
+                    out=dh_bank[e, si, q][:, t, :],
+                    lhsT=w2_t[e, sn][:, 2 * col : 2 * (col + P)].bitcast(E2M1),
+                    lhsT_scale=w2s_t[e][:, sn, col : col + P],
+                    rhs=g_codes[e, sn][:, q * P : (q + 1) * P].bitcast(E5M2),
+                    rhs_scale=g_scales[e, sn][:, q * P : (q + 1) * P],
+                    start=(sn == 0 and t == 0),
+                    stop=(sn == SN - 1 and t == PACK - 1),
                 )
 
-        def turn_da(e, si, pair, bank):
-            turned = bank_tile([P, 2, 2, P], bank)
-            for ql in range(2):
-                words = da_t[e, si, 2 * pair + ql][:].bitcast(F32)
-                for u in range(2):
-                    nc.tensor.transpose(turned[:, ql, u, :], words[:, u * P : (u + 1) * P], ident[:])
-            woven_words = da_woven[e, si][:, pair * 2 * PASS : (pair + 1) * 2 * PASS].bitcast(F32)
-            nc.scalar.copy(
-                out=woven_words.rearrange("p (q c u) -> p q c u", q=2, u=2),
-                in_=turned[:].rearrange("p q u c -> p q c u"),
+        def derive(e, si, q):
+            c0 = max(first for first, n in PIECES[e] if first <= q * P)
+            at = (q * P - c0) * PACK
+            nc.vector.scalar_tensor_tensor(
+                da_woven[e, c0][:, si, at : at + PASS].rearrange("p (c t) -> p c t", t=PACK),
+                a_t[e, si][:, :, q * P : (q + 1) * P].rearrange("p t c -> p c t"),
+                0.0,
+                dh_bank[e, si, q][:].rearrange("p t c -> p c t"),
+                ALU.max,
+                ALU.mult,
             )
 
-        def second_product(e, k, si, bank=None):
-            if si == 0:
-                dx_bank[e, k] = bank_tile([P, C], bank)
-            nc.tensor.matmul_mx(
-                out=dx_bank[e, k][:],
-                lhsT=w1_t[:, e * SI + si, 2 * k * P : 2 * (k + 1) * P].bitcast(E2M1),
-                lhsT_scale=w1s_t[:, e * SI + si, k * P : (k + 1) * P],
-                rhs=da_codes[e, si][:].bitcast(E5M2),
-                rhs_scale=da_scales[e, si][:],
-                start=(si == 0),
-                stop=(si == SI - 1),
+        def quantize_da(e, c0):
+            nc.vector.quantize_mx(
+                out=da_codes[e, c0][:].rearrange("p s c -> p (s c)").bitcast(E5M2),
+                scales=da_scales[e, c0][:].rearrange("p s c -> p (s c)"),
+                in_=da_woven[e, c0][:].rearrange("p s c -> p (s c)"),
             )
 
-        def drain(e, k, c0, c1, name):
-            dx = held.tile([P, c1 - c0], F32, name=name)
-            nc.scalar.copy(out=dx[:], in_=dx_bank[e, k][:, c0:c1])
+        def second_product(e, c0, n, bank):
+            dx_bank = bank_tile([P, KT, n], bank)
+            for k in range(KT):
+                for si in range(SI):
+                    nc.tensor.matmul_mx(
+                        out=dx_bank[:, k, :],
+                        lhsT=w1_t[:, e * SI + si, 2 * k * P : 2 * (k + 1) * P].bitcast(E2M1),
+                        lhsT_scale=w1s_t[:, e * SI + si, k * P : (k + 1) * P],
+                        rhs=da_codes[e, c0][:, si, :].bitcast(E5M2),
+                        rhs_scale=da_scales[e, c0][:, si, :],
+                        start=(si == 0),
+                        stop=(si == SI - 1),
+                    )
+            dx = tile([P, KT, n], F32, f"dx{e}{c0}")
+            nc.scalar.activation(dx[:], dx_bank[:], COPY, scale=2.0)
             return dx
 
-        def scatter(window, dx, e, c0, c1):
-            nc.vector.tensor_copy(window[:].indirect(slots(e, c0, c1)), dx[:])
+        def scatter_on_scalar(dx, e, c0, n, k):
+            nc.scalar.activation(windows[k][:].indirect(slots(c0, n, e)), dx[:, k, :], COPY)
 
-        gather(0, 0, 0, 0, P)
-        gather(0, 0, 0, P, C)
-        gather(1, 0, 0)
-        for t in range(1, PACK):
-            for e in range(E):
-                gather(e, 0, t)
-        for si in range(SI):
-            for half in range(2):
-                for pair in range(2):
-                    turn_a(0, si, half, pair, 4 + 2 * half + pair)
-        weave_on_scalar(0, 0)
-        g_woven[1, 0] = held.tile([P, C * PACK], BF16, name="a011", align_bytes=ALIGN)[:]
-        weave_on_scalar(1, 0)
+        def scatter_on_vector(dx, e, c0, n, k):
+            nc.vector.tensor_copy(windows[k][:].indirect(slots(c0, n, e)), dx[:, k, :])
 
-        for e in range(E):
-            gather(e, 1, 0)
-        for t in range(1, PACK):
-            gather(0, 1, t)
+        for t in range(PACK):
+            gather_on_scalar(0, 0, t)
+            gather_gated(1, 0, t)
+        weave_gating(0, 0)
+        permute_scales(0)
         quantize_g(0, 0)
-        weave_on_scalar(0, 1)
-        for half in range(2):
-            for pair in range(2):
-                turn_a(1, 0, half, pair, 4 + 2 * half + pair)
-        for q in range(Q):
-            first_product(0, 0, q, 0, q)
-        for pair in range(2):
-            turn_a(1, 1, 0, pair, 4 + pair)
+        weave(1, 0)
+        for t in range(PACK):
+            gather_on_scalar(0, 1, t)
+        weave_gating(0, 1)
         quantize_g(1, 0)
-        gather(1, 1, 1)
-        gather(1, 1, 2)
-        g_codes[0, 1] = held.tile([P, C], U32, name="a101", align_bytes=ALIGN)
         quantize_g(0, 1)
-        gather(1, 1, 3)
-        g_woven[1, 1] = held.tile([P, C * PACK], BF16, name="gw11", align_bytes=ALIGN)[:]
-        weave_on_gpsimd(1, 1)
+        for sn in range(SN):
+            permute_words(0, sn)
+        for si in range(SI):
+            for q in range(Q):
+                first_product(0, si, q, 0, si * Q + q)
+        permute_scales(1)
+        g[1, 1] = tile([P, PACK, C], F32, "w2raw0")
+        for t in range(PACK):
+            gather_on_scalar(1, 1, t)
 
-        for q in range(2):
-            first_product(0, 0, q, 1)
-        for pair in range(2):
-            turn_a(1, 1, 1, pair, 6 + pair)
-        for q in range(2, Q):
-            first_product(0, 0, q, 1)
-        for q in range(Q):
-            both_passes(0, 1, q, 4 + q)
-        for q in range(Q):
-            derive(0, 0, q)
-        derive(0, 1, 0)
-        for pair in range(2):
-            turn_da(0, 0, pair, 2 + pair)
-        for q in range(1, Q):
-            derive(0, 1, q)
-        for q in range(2):
-            first_product(1, 0, q, 0, q)
-        for pair in range(2):
-            turn_da(0, 1, pair, 4 + pair)
-
-        g_codes[1, 1] = held.tile([P, C], U32, name="slope011", align_bytes=ALIGN)
-        quantize_g(1, 1)
-        for q in range(2):
-            first_product(1, 0, q, 1)
-        derive(1, 0, 0)
-        for q in range(2, Q):
-            both_passes(1, 0, q, q)
-        quantize_da(0, 0)
-        derive(1, 0, 1)
-        quantize_da(0, 1)
-        for q in range(2):
-            both_passes(1, 1, q, 6 + q)
-        second_product(0, 0, 0, 0)
-        second_product(0, 0, 1)
-        dx00 = drain(0, 0, 0, C, "dx00")
-        for q in range(2, Q):
-            both_passes(1, 1, q, 2 + q)
-        for q in range(2, Q):
-            derive(1, 0, q)
-        for q in range(Q):
-            derive(1, 1, q)
-        second_product(0, 1, 0, 1)
-        second_product(0, 1, 1)
-        dx01_first = drain(0, 1, 0, SPLIT, "dx01")
-        for pair in range(2):
-            turn_da(1, 0, pair, 2 + pair)
-        for pair in range(2):
-            turn_da(1, 1, pair, 6 + pair)
-        dx01_rest = drain(0, 1, SPLIT, C, f"da11{Q - 1}")
-
-        windows = [held.tile([P, T], F32, name=name, align_bytes=ALIGN) for name in ("slope101", "window1")]
-        scatter(windows[0], dx00, 0, 0, C)
-        scatter(windows[1], dx01_first, 0, 0, SPLIT)
-        quantize_da(1, 0)
-        second_product(1, 0, 0, 0)
-        quantize_da(1, 1)
-        second_product(1, 0, 1)
-        dx1 = [drain(1, 0, 0, C, "dx10")]
-        second_product(1, 1, 0, 0)
-        second_product(1, 1, 1)
-        dx1.append(drain(1, 1, 0, C, "dx11"))
-        scatter(windows[1], dx01_rest, 0, SPLIT, C)
+        for si in range(SI):
+            for q in range(Q):
+                first_product(0, si, q, 1)
+                derive(0, si, q)
+                if (si, q) == (1, 2):
+                    quantize_da(0, 0)
+        for sn in range(SN):
+            permute_words(1, sn)
+        dx = second_product(0, 0, 256, 0)
+        weave_gating(1, 1)
+        quantize_da(0, 256)
         for k in range(KT):
-            scatter(windows[k], dx1[k], 1, 0, C)
+            scatter_on_scalar(dx, 0, 0, 256, k)
+        quantize_g(1, 1)
+        order = [(si, q) for q in range(Q) for si in range(SI)]
+        for x, (si, q) in enumerate(order[:6]):
+            first_product(1, si, q, 0, 2 + x)
+        dx = second_product(0, 256, 256, 1)
+        for k in range(KT):
+            scatter_on_scalar(dx, 0, 256, 256, k)
+
+        for x, (si, q) in enumerate(order):
+            if x >= 6:
+                first_product(1, si, q, 0, x - 6)
+            first_product(1, si, q, 1)
+            derive(1, si, q)
+            if x == 4:
+                quantize_da(1, 0)
+                dx = second_product(1, 0, 256, 2)
+                for k in range(KT):
+                    scatter_on_scalar(dx, 1, 0, 256, k)
+            if x == 6:
+                quantize_da(1, 256)
+                dx_mid = second_product(1, 256, 128, 3)
+        quantize_da(1, 384)
+        dx = second_product(1, 384, 128, 4)
+        scatter_on_scalar(dx_mid, 1, 256, 128, 0)
+        scatter_on_vector(dx_mid, 1, 256, 128, 1)
+        scatter_on_scalar(dx, 1, 384, 128, 0)
+        scatter_on_vector(dx, 1, 384, 128, 1)
+        for k in range(KT):
             nc.sync.dma_start(out[k * P : (k + 1) * P, :], windows[k][:])

@@ -29,7 +29,7 @@ def tile_moe_bdx_mlp_relu2_kernel(
     STRIPE = 16
     ROWS = 4
     ALIGN = 64
-    PIECES = (((0, 256), (256, 256)), ((0, 256), (256, 128), (384, 128)))
+    PIECES = (((0, 256), (256, 256)), ((0, 128), (128, 128), (256, 128), (384, 128)))
 
     with ExitStack() as ctx:
         held = ctx.enter_context(tc.tile_pool(name="held", bufs=1))
@@ -44,48 +44,66 @@ def tile_moe_bdx_mlp_relu2_kernel(
         gate_t = [tile([P, C], F32, f"gate{e}") for e in range(E)]
         a_t = {x: tile([P, PACK, C], F32, f"a{x[0]}{x[1]}") for x in groups}
         w2_raw = [tile([P, SN, 2 * H], U8, f"w2raw{e}") for e in range(E)]
-        w2s_raw = tile([P, E * SN, H], U8, "w2sraw")
+        w2s_raw = tile([P, H], U8, "w2sraw")
         w2_t = {x: tile([P, 2 * H], U8, f"w2{x[0]}{x[1]}") for x in groups}
-        w2s_t = [tile([P, SN, H], U8, f"w2s{e}") for e in range(E)]
+        w2s_t = {x: tile([P, H], U8, f"w2s{x[0]}{x[1]}") for x in groups}
         w1_t = tile([P, E * SI, 2 * K], U8, "w1t")
         w1s_t = tile([P, E * SI, K], U8, "w1s")
 
         dy_v = dyT.rearrange("(s p t) c -> s t p c", p=P, t=PACK)
         a_v = a.rearrange("(s p t) (e c) -> e s p t c", p=P, t=PACK, e=E)
         w2_v = w2_words.bitcast(I32).rearrange("e s p b -> e p s b")
-        w2s_v = w2_scales.bitcast(I32).rearrange("e s (x r) i -> r x (e s) i", r=ROWS)
+        w2s_v = w2_scales.bitcast(I32).rearrange("e s (x r) i -> x (e s) r i", r=ROWS)
         w1_v = w1_words.bitcast(I32).rearrange("e s p b -> p (e s) b")
         w1s_v = w1_scales.bitcast(I32).rearrange("e s (x r) i -> r x (e s) i", r=ROWS)
 
         nc.sync.dma_start(offsets[:], offs)
         nc.vector.memset(w2s_raw[:].bitcast(I32), 0)
         nc.vector.memset(w1s_t[:].bitcast(I32), 0)
+        for x in groups[1:]:
+            nc.vector.memset(w2s_t[x][:].bitcast(I32), 0)
 
         def load_dy(sn, t):
             nc.sync.dma_start(dy_t[sn][t][:], dy_v[sn, t])
 
+        def load_a(e, si):
+            nc.sync.dma_start(a_t[e, si][:], a_v[e, si])
+
+        def move_scales(e, sn):
+            at = ROWS * (e * SN + sn)
+            for row in range(ROWS):
+                nc.gpsimd.dma_start(w2s_t[e, sn][row:P:32, :].bitcast(I32), w2s_t[0, 0][at + row : P : 32, :].bitcast(I32))
+
         load_dy(0, 0)
+        for x in range(P // 32):
+            nc.sync.dma_start(w2s_raw[32 * x : 32 * x + E * SN * ROWS, :].bitcast(I32), w2s_v[x])
+        nc.vector.tensor_copy(
+            w2s_t[0, 0][:].rearrange("p (s t m) -> p s t m", s=SI, t=PACK),
+            w2s_raw[:].rearrange("p (s m t) -> p s t m", s=SI, t=PACK),
+        )
         nc.sync.dma_start(gate_t[1][:], gate[0:P, C : 2 * C])
         for t in range(1, PACK):
             load_dy(0, t)
         nc.sync.dma_start(gate_t[0][:], gate[0:P, 0:C])
-        for row in range(ROWS):
-            nc.sync.dma_start(w2s_raw[row:P:32, :, :].bitcast(I32), w2s_v[row])
-        for t in range(PACK):
+        load_dy(1, 0)
+        move_scales(0, 1)
+        for t in range(1, PACK):
             load_dy(1, t)
         nc.sync.dma_start(w2_raw[0][:].bitcast(I32), w2_v[0])
-        for si in range(SI):
-            nc.sync.dma_start(a_t[0, si][:], a_v[0, si])
-        nc.sync.dma_start(w2_raw[1][:].bitcast(I32), w2_v[1])
-        nc.sync.dma_start(w1_t[:].bitcast(I32), w1_v)
+        load_a(0, 0)
+        move_scales(1, 0)
+        load_a(0, 1)
         for row in range(ROWS):
             nc.sync.dma_start(w1s_t[row:P:32, :, :].bitcast(I32), w1s_v[row])
-        for si in range(SI):
-            nc.sync.dma_start(a_t[1, si][:], a_v[1, si])
+        nc.sync.dma_start(w1_t[:].bitcast(I32), w1_v)
+        nc.sync.dma_start(w2_raw[1][:].bitcast(I32), w2_v[1])
+        load_a(1, 0)
+        move_scales(1, 1)
+        load_a(1, 1)
 
         g = {x: tile([P, PACK, C], F32, f"g{x[0]}{x[1]}") for x in groups if x != (1, 1)}
-        g_woven = {x: tile([P, C * PACK], BF16, f"gw{x[0]}{x[1]}") for x in groups}
-        g_codes = {x: tile([P, C], U32, f"gc{x[0]}{x[1]}") for x in groups}
+        g_woven = {x: tile([P, C * PACK], BF16, f"gw{x[0]}{x[1]}") for x in groups if x[0] == 0}
+        g_codes = {x: tile([P, C], U32, f"gc{x[0]}{x[1]}") for x in groups if x != (1, 0)}
         g_scales = {x: tile([P, C], U8, f"gs{x[0]}{x[1]}") for x in groups}
         da_woven, da_codes, da_scales = {}, {}, {}
         for e in range(E):
@@ -105,14 +123,17 @@ def tile_moe_bdx_mlp_relu2_kernel(
         def gather_on_scalar(e, sn, t):
             nc.scalar.activation(g[e, sn][:, t, :], dy_t[sn][t][:].indirect(slots(0, C, e)), COPY)
 
+        def gather_on_vector(e, sn, t):
+            nc.vector.tensor_copy(g[e, sn][:, t, :], dy_t[sn][t][:].indirect(slots(0, C, e)))
+
         def gather_gated(e, sn, t):
             nc.vector.tensor_tensor(g[e, sn][:, t, :], dy_t[sn][t][:].indirect(slots(0, C, e)), gate_t[e][:], ALU.mult)
 
-        def weave_gating(e, sn):
+        def weave_gating(e, sn, c0=0, c1=C):
             nc.vector.tensor_tensor(
-                g_woven[e, sn][:].rearrange("p (c v t) -> p c t v", v=2, t=PACK),
-                g[e, sn][:].rearrange("p t (c v) -> p c t v", v=2),
-                gate_t[e][:].rearrange("p (c v) -> p c v", v=2).unsqueeze(2).to_broadcast([P, C // 2, PACK, 2]),
+                g_woven[e, sn][:, PACK * c0 : PACK * c1].rearrange("p (c v t) -> p c t v", v=2, t=PACK),
+                g[e, sn][:, :, c0:c1].rearrange("p t (c v) -> p c t v", v=2),
+                gate_t[e][:, c0:c1].rearrange("p (c v) -> p c v", v=2).unsqueeze(2).to_broadcast([P, (c1 - c0) // 2, PACK, 2]),
                 ALU.mult,
             )
 
@@ -122,19 +143,15 @@ def tile_moe_bdx_mlp_relu2_kernel(
                 g[e, sn][:].rearrange("p t (c v) -> p c t v", v=4),
             )
 
-        def quantize_g(e, sn):
-            nc.vector.quantize_mx(out=g_codes[e, sn][:].bitcast(E5M2), scales=g_scales[e, sn][:], in_=g_woven[e, sn][:])
+        def quantize_g(e, sn, c0=0, c1=C):
+            nc.vector.quantize_mx(
+                out=g_codes[e, sn][:, c0:c1].bitcast(E5M2), scales=g_scales[e, sn][:, c0:c1], in_=g_woven[e, sn][:, PACK * c0 : PACK * c1]
+            )
 
         def permute_words(e, sn):
             nc.scalar.copy(
                 out=w2_t[e, sn][:].bitcast(U16).rearrange("p (s t m) -> p s t m", s=SI, t=PACK),
                 in_=w2_raw[e][:, sn, :].bitcast(U16).rearrange("p (s m t) -> p s t m", s=SI, t=PACK),
-            )
-
-        def permute_scales(e):
-            nc.vector.tensor_copy(
-                w2s_t[e][:].rearrange("p n (s t m) -> p (n s) t m", s=SI, t=PACK),
-                w2s_raw[:, e * SN : (e + 1) * SN, :].rearrange("p n (s m t) -> p (n s) t m", s=SI, t=PACK),
             )
 
         def first_product(e, si, q, sn, bank=None):
@@ -145,7 +162,7 @@ def tile_moe_bdx_mlp_relu2_kernel(
                 nc.tensor.matmul_mx(
                     out=dh_bank[e, si, q][:, t, :],
                     lhsT=w2_t[e, sn][:, 2 * col : 2 * (col + P)].bitcast(E2M1),
-                    lhsT_scale=w2s_t[e][:, sn, col : col + P],
+                    lhsT_scale=w2s_t[e, sn][:, col : col + P],
                     rhs=g_codes[e, sn][:, q * P : (q + 1) * P].bitcast(E5M2),
                     rhs_scale=g_scales[e, sn][:, q * P : (q + 1) * P],
                     start=(sn == 0 and t == 0),
@@ -171,90 +188,101 @@ def tile_moe_bdx_mlp_relu2_kernel(
                 in_=da_woven[e, c0][:].rearrange("p s c -> p (s c)"),
             )
 
-        def second_product(e, c0, n, bank):
-            dx_bank = bank_tile([P, KT, n], bank)
-            for k in range(KT):
-                for si in range(SI):
-                    nc.tensor.matmul_mx(
-                        out=dx_bank[:, k, :],
-                        lhsT=w1_t[:, e * SI + si, 2 * k * P : 2 * (k + 1) * P].bitcast(E2M1),
-                        lhsT_scale=w1s_t[:, e * SI + si, k * P : (k + 1) * P],
-                        rhs=da_codes[e, c0][:, si, :].bitcast(E5M2),
-                        rhs_scale=da_scales[e, c0][:, si, :],
-                        start=(si == 0),
-                        stop=(si == SI - 1),
-                    )
-            dx = tile([P, KT, n], F32, f"dx{e}{c0}")
-            nc.scalar.activation(dx[:], dx_bank[:], COPY, scale=2.0)
-            return dx
+        def second_product(e, c0, n, k, dx_bank):
+            for si in range(SI):
+                nc.tensor.matmul_mx(
+                    out=dx_bank,
+                    lhsT=w1_t[:, e * SI + si, 2 * k * P : 2 * (k + 1) * P].bitcast(E2M1),
+                    lhsT_scale=w1s_t[:, e * SI + si, k * P : (k + 1) * P],
+                    rhs=da_codes[e, c0][:, si, :].bitcast(E5M2),
+                    rhs_scale=da_scales[e, c0][:, si, :],
+                    start=(si == 0),
+                    stop=(si == SI - 1),
+                )
 
         def scatter_on_scalar(dx, e, c0, n, k):
-            nc.scalar.activation(windows[k][:].indirect(slots(c0, n, e)), dx[:, k, :], COPY)
+            nc.scalar.activation(windows[k][:].indirect(slots(c0, n, e)), dx, COPY)
 
-        def scatter_on_vector(dx, e, c0, n, k):
-            nc.vector.tensor_copy(windows[k][:].indirect(slots(c0, n, e)), dx[:, k, :])
+        def back_on_scalar(e, c0, n, bank):
+            dx_bank = bank_tile([P, KT, n], bank)
+            for k in range(KT):
+                second_product(e, c0, n, k, dx_bank[:, k, :])
+            dx = tile([P, KT, n], F32, f"dx{e}{c0}")
+            nc.scalar.activation(dx[:], dx_bank[:], COPY, scale=2.0)
+            for k in reversed(range(KT)):
+                scatter_on_scalar(dx[:, k, :], e, c0, n, k)
+
+        def back_on_both(e, c0, n, banks):
+            dx_banks = [bank_tile([P, n], bank) for bank in banks]
+            dx = [tile([P, n], F32, f"dx{e}{c0}{k}") for k in range(KT)]
+            for k in range(KT):
+                second_product(e, c0, n, k, dx_banks[k][:])
+            nc.scalar.activation(dx[0][:], dx_banks[0][:], COPY, scale=2.0)
+            scatter_on_scalar(dx[0][:], e, c0, n, 0)
+            return dx_banks[1], dx[1]
+
+        def finish_on_vector(e, c0, n, dx_bank, dx):
+            nc.vector.tensor_scalar(dx[:], dx_bank[:], 2.0, None, ALU.mult)
+            nc.vector.tensor_copy(windows[1][:].indirect(slots(c0, n, e)), dx[:])
 
         for t in range(PACK):
             gather_on_scalar(0, 0, t)
             gather_gated(1, 0, t)
         weave_gating(0, 0)
-        permute_scales(0)
         quantize_g(0, 0)
-        weave(1, 0)
-        for t in range(PACK):
+        for t in range(PACK - 1):
             gather_on_scalar(0, 1, t)
+        gather_on_vector(0, 1, PACK - 1)
         weave_gating(0, 1)
-        quantize_g(1, 0)
         quantize_g(0, 1)
+        g_woven[1, 0] = tile([P, C * PACK], BF16, "g01")
+        weave(1, 0)
         for sn in range(SN):
             permute_words(0, sn)
-        for si in range(SI):
-            for q in range(Q):
-                first_product(0, si, q, 0, si * Q + q)
-        permute_scales(1)
+        order0 = [(si, 2 * pair + ql) for pair in range(2) for si in range(SI) for ql in range(2)]
+        for x, (si, q) in enumerate(order0[:4]):
+            first_product(0, si, q, 0, x)
         g[1, 1] = tile([P, PACK, C], F32, "w2raw0")
         for t in range(PACK):
             gather_on_scalar(1, 1, t)
-
-        for si in range(SI):
-            for q in range(Q):
-                first_product(0, si, q, 1)
-                derive(0, si, q)
-                if (si, q) == (1, 2):
-                    quantize_da(0, 0)
         for sn in range(SN):
             permute_words(1, sn)
-        dx = second_product(0, 0, 256, 0)
-        weave_gating(1, 1)
-        quantize_da(0, 256)
-        for k in range(KT):
-            scatter_on_scalar(dx, 0, 0, 256, k)
-        quantize_g(1, 1)
-        order = [(si, q) for q in range(Q) for si in range(SI)]
-        for x, (si, q) in enumerate(order[:6]):
-            first_product(1, si, q, 0, 2 + x)
-        dx = second_product(0, 256, 256, 1)
-        for k in range(KT):
-            scatter_on_scalar(dx, 0, 256, 256, k)
 
-        for x, (si, q) in enumerate(order):
+        order1 = [(si, q) for q in range(Q) for si in range(SI)]
+        for x, (si, q) in enumerate(order0):
+            first_product(0, si, q, 1)
+            if x < 4:
+                first_product(0, *order0[x + 4], 0, x + 4)
+            derive(0, si, q)
+            if x == 4:
+                quantize_da(0, 0)
+                back_on_scalar(0, 0, 256, 0)
+        g_codes[1, 0] = tile([P, C], U32, "daw00")
+        quantize_g(1, 0)
+        quantize_da(0, 256)
+        back_on_scalar(0, 256, 256, 1)
+        g_woven[1, 1] = tile([P, C * PACK], BF16, "a00")
+        for half in range(2):
+            weave_gating(1, 1, half * C // 2, (half + 1) * C // 2)
+        for half in range(2):
+            quantize_g(1, 1, half * C // 2, (half + 1) * C // 2)
+        for x, (si, q) in enumerate(order1[:6]):
+            first_product(1, si, q, 0, 2 + x)
+
+        for x, (si, q) in enumerate(order1):
             if x >= 6:
                 first_product(1, si, q, 0, x - 6)
             first_product(1, si, q, 1)
             derive(1, si, q)
-            if x == 4:
-                quantize_da(1, 0)
-                dx = second_product(1, 0, 256, 2)
-                for k in range(KT):
-                    scatter_on_scalar(dx, 1, 0, 256, k)
+            if x in (2, 4):
+                quantize_da(1, (x // 2 - 1) * P)
+                back_on_scalar(1, (x // 2 - 1) * P, P, x // 2 + 1)
             if x == 6:
                 quantize_da(1, 256)
-                dx_mid = second_product(1, 256, 128, 3)
+                middle = back_on_both(1, 256, 128, (4, 5))
         quantize_da(1, 384)
-        dx = second_product(1, 384, 128, 4)
-        scatter_on_scalar(dx_mid, 1, 256, 128, 0)
-        scatter_on_vector(dx_mid, 1, 256, 128, 1)
-        scatter_on_scalar(dx, 1, 384, 128, 0)
-        scatter_on_vector(dx, 1, 384, 128, 1)
+        last = back_on_both(1, 384, 128, (6, 7))
+        finish_on_vector(1, 256, 128, *middle)
+        finish_on_vector(1, 384, 128, *last)
         for k in range(KT):
             nc.sync.dma_start(out[k * P : (k + 1) * P, :], windows[k][:])

@@ -29,7 +29,8 @@ def tile_moe_bdx_mlp_relu2_kernel(
     STRIPE = 16
     ROWS = 4
     ALIGN = 64
-    PIECES = (((0, 256), (256, 256)), ((0, 128), (128, 128), (256, 128), (384, 128)))
+    PIECES = (((0, 256), (256, 256)), ((0, 256), (256, 128), (384, 128)))
+    HALF = C // 2
 
     with ExitStack() as ctx:
         held = ctx.enter_context(tc.tile_pool(name="held", bufs=1))
@@ -44,24 +45,22 @@ def tile_moe_bdx_mlp_relu2_kernel(
         gate_t = [tile([P, C], F32, f"gate{e}") for e in range(E)]
         a_t = {x: tile([P, PACK, C], F32, f"a{x[0]}{x[1]}") for x in groups}
         w2_raw = [tile([P, SN, 2 * H], U8, f"w2raw{e}") for e in range(E)]
-        w2s_raw = tile([P, H], U8, "w2sraw")
+        w2s_raw = tile([P, E * SN, H], U8, "w2sraw")
         w2_t = {x: tile([P, 2 * H], U8, f"w2{x[0]}{x[1]}") for x in groups}
-        w2s_t = {x: tile([P, H], U8, f"w2s{x[0]}{x[1]}") for x in groups}
+        w2s_t = [tile([P, SN, H], U8, f"w2s{e}") for e in range(E)]
         w1_t = tile([P, E * SI, 2 * K], U8, "w1t")
         w1s_t = tile([P, E * SI, K], U8, "w1s")
 
         dy_v = dyT.rearrange("(s p t) c -> s t p c", p=P, t=PACK)
         a_v = a.rearrange("(s p t) (e c) -> e s p t c", p=P, t=PACK, e=E)
         w2_v = w2_words.bitcast(I32).rearrange("e s p b -> e p s b")
-        w2s_v = w2_scales.bitcast(I32).rearrange("e s (x r) i -> x (e s) r i", r=ROWS)
+        w2s_v = w2_scales.bitcast(I32).rearrange("e s (x r) i -> r x (e s) i", r=ROWS)
         w1_v = w1_words.bitcast(I32).rearrange("e s p b -> p (e s) b")
         w1s_v = w1_scales.bitcast(I32).rearrange("e s (x r) i -> r x (e s) i", r=ROWS)
 
         nc.sync.dma_start(offsets[:], offs)
         nc.vector.memset(w2s_raw[:].bitcast(I32), 0)
         nc.vector.memset(w1s_t[:].bitcast(I32), 0)
-        for x in groups[1:]:
-            nc.vector.memset(w2s_t[x][:].bitcast(I32), 0)
 
         def load_dy(sn, t):
             nc.sync.dma_start(dy_t[sn][t][:], dy_v[sn, t])
@@ -69,41 +68,33 @@ def tile_moe_bdx_mlp_relu2_kernel(
         def load_a(e, si):
             nc.sync.dma_start(a_t[e, si][:], a_v[e, si])
 
-        def move_scales(e, sn):
-            at = ROWS * (e * SN + sn)
-            for row in range(ROWS):
-                nc.gpsimd.dma_start(w2s_t[e, sn][row:P:32, :].bitcast(I32), w2s_t[0, 0][at + row : P : 32, :].bitcast(I32))
-
         load_dy(0, 0)
-        for x in range(P // 32):
-            nc.sync.dma_start(w2s_raw[32 * x : 32 * x + E * SN * ROWS, :].bitcast(I32), w2s_v[x])
-        nc.vector.tensor_copy(
-            w2s_t[0, 0][:].rearrange("p (s t m) -> p s t m", s=SI, t=PACK),
-            w2s_raw[:].rearrange("p (s m t) -> p s t m", s=SI, t=PACK),
-        )
         nc.sync.dma_start(gate_t[1][:], gate[0:P, C : 2 * C])
-        for t in range(1, PACK):
+        load_dy(0, 1)
+        for row in range(ROWS):
+            nc.sync.dma_start(w2s_raw[row:P:32, :, :].bitcast(I32), w2s_v[row])
+        for t in range(2, PACK):
             load_dy(0, t)
-        nc.sync.dma_start(gate_t[0][:], gate[0:P, 0:C])
         load_dy(1, 0)
-        move_scales(0, 1)
+        nc.sync.dma_start(gate_t[0][:], gate[0:P, 0:C])
         for t in range(1, PACK):
             load_dy(1, t)
         nc.sync.dma_start(w2_raw[0][:].bitcast(I32), w2_v[0])
         load_a(0, 0)
-        move_scales(1, 0)
         load_a(0, 1)
+        nc.sync.dma_start(w2_raw[1][:].bitcast(I32), w2_v[1])
         for row in range(ROWS):
             nc.sync.dma_start(w1s_t[row:P:32, :, :].bitcast(I32), w1s_v[row])
         nc.sync.dma_start(w1_t[:].bitcast(I32), w1_v)
-        nc.sync.dma_start(w2_raw[1][:].bitcast(I32), w2_v[1])
         load_a(1, 0)
-        move_scales(1, 1)
         load_a(1, 1)
 
-        g = {x: tile([P, PACK, C], F32, f"g{x[0]}{x[1]}") for x in groups if x != (1, 1)}
-        g_woven = {x: tile([P, C * PACK], BF16, f"gw{x[0]}{x[1]}") for x in groups if x[0] == 0}
-        g_codes = {x: tile([P, C], U32, f"gc{x[0]}{x[1]}") for x in groups if x != (1, 0)}
+        g = {(e, 0): tile([P, PACK, C], F32, f"g{e}0")[:] for e in range(E)}
+        shared = tile([P, PACK + 1, C], F32, "g1")
+        g[1, 1] = shared[:, 0:PACK, :]
+        g[0, 1] = shared[:, 1 : PACK + 1, :]
+        g_woven = {x: tile([P, C * PACK], BF16, f"gw{x[0]}{x[1]}") for x in groups if x != (1, 1)}
+        g_codes = {x: tile([P, C], U32, f"gc{x[0]}{x[1]}") for x in groups if x[0] == 0}
         g_scales = {x: tile([P, C], U8, f"gs{x[0]}{x[1]}") for x in groups}
         da_woven, da_codes, da_scales = {}, {}, {}
         for e in range(E):
@@ -120,11 +111,8 @@ def tile_moe_bdx_mlp_relu2_kernel(
         def slots(c0, n, e):
             return offsets[:, (e * C + c0) // STRIPE : (e * C + c0 + n) // STRIPE]
 
-        def gather_on_scalar(e, sn, t):
-            nc.scalar.activation(g[e, sn][:, t, :], dy_t[sn][t][:].indirect(slots(0, C, e)), COPY)
-
-        def gather_on_vector(e, sn, t):
-            nc.vector.tensor_copy(g[e, sn][:, t, :], dy_t[sn][t][:].indirect(slots(0, C, e)))
+        def gather_on_scalar(e, sn, t, c0=0, n=C):
+            nc.scalar.activation(g[e, sn][:, t, c0 : c0 + n], dy_t[sn][t][:].indirect(slots(c0, n, e)), COPY)
 
         def gather_gated(e, sn, t):
             nc.vector.tensor_tensor(g[e, sn][:, t, :], dy_t[sn][t][:].indirect(slots(0, C, e)), gate_t[e][:], ALU.mult)
@@ -137,10 +125,18 @@ def tile_moe_bdx_mlp_relu2_kernel(
                 ALU.mult,
             )
 
+        def weave_last(q):
+            nc.gpsimd.tensor_tensor(
+                g_woven[1, 1][:, q * PASS : (q + 1) * PASS].rearrange("p (c t) -> p c t", t=PACK),
+                g[1, 1][:, :, q * P : (q + 1) * P].rearrange("p t c -> p c t"),
+                gate_t[1][:, q * P : (q + 1) * P].unsqueeze(2).to_broadcast([P, P, PACK]),
+                ALU.mult,
+            )
+
         def weave(e, sn):
             nc.vector.tensor_copy(
                 g_woven[e, sn][:].rearrange("p (c v t) -> p c t v", v=4, t=PACK),
-                g[e, sn][:].rearrange("p t (c v) -> p c t v", v=4),
+                g[e, sn].rearrange("p t (c v) -> p c t v", v=4),
             )
 
         def quantize_g(e, sn, c0=0, c1=C):
@@ -154,6 +150,12 @@ def tile_moe_bdx_mlp_relu2_kernel(
                 in_=w2_raw[e][:, sn, :].bitcast(U16).rearrange("p (s m t) -> p s t m", s=SI, t=PACK),
             )
 
+        def permute_scales(e):
+            nc.vector.tensor_copy(
+                w2s_t[e][:].rearrange("p n (s t m) -> p (n s) t m", s=SI, t=PACK),
+                w2s_raw[:, e * SN : (e + 1) * SN, :].rearrange("p n (s m t) -> p (n s) t m", s=SI, t=PACK),
+            )
+
         def first_product(e, si, q, sn, bank=None):
             if sn == 0:
                 dh_bank[e, si, q] = bank_tile([P, PACK, P], bank)
@@ -162,7 +164,7 @@ def tile_moe_bdx_mlp_relu2_kernel(
                 nc.tensor.matmul_mx(
                     out=dh_bank[e, si, q][:, t, :],
                     lhsT=w2_t[e, sn][:, 2 * col : 2 * (col + P)].bitcast(E2M1),
-                    lhsT_scale=w2s_t[e, sn][:, col : col + P],
+                    lhsT_scale=w2s_t[e][:, sn, col : col + P],
                     rhs=g_codes[e, sn][:, q * P : (q + 1) * P].bitcast(E5M2),
                     rhs_scale=g_scales[e, sn][:, q * P : (q + 1) * P],
                     start=(sn == 0 and t == 0),
@@ -203,14 +205,17 @@ def tile_moe_bdx_mlp_relu2_kernel(
         def scatter_on_scalar(dx, e, c0, n, k):
             nc.scalar.activation(windows[k][:].indirect(slots(c0, n, e)), dx, COPY)
 
-        def back_on_scalar(e, c0, n, bank):
+        def scatter_on_vector(dx, e, c0, n, k):
+            nc.vector.tensor_copy(windows[k][:].indirect(slots(c0, n, e)), dx)
+
+        def both_rows(e, c0, n, bank):
             dx_bank = bank_tile([P, KT, n], bank)
             for k in range(KT):
                 second_product(e, c0, n, k, dx_bank[:, k, :])
             dx = tile([P, KT, n], F32, f"dx{e}{c0}")
-            nc.scalar.activation(dx[:], dx_bank[:], COPY, scale=2.0)
-            for k in reversed(range(KT)):
-                scatter_on_scalar(dx[:, k, :], e, c0, n, k)
+            for k in (1, 0):
+                nc.scalar.activation(dx[:, k, :], dx_bank[:, k, :], COPY, scale=2.0)
+            return dx
 
         def back_on_both(e, c0, n, banks):
             dx_banks = [bank_tile([P, n], bank) for bank in banks]
@@ -223,65 +228,74 @@ def tile_moe_bdx_mlp_relu2_kernel(
 
         def finish_on_vector(e, c0, n, dx_bank, dx):
             nc.vector.tensor_scalar(dx[:], dx_bank[:], 2.0, None, ALU.mult)
-            nc.vector.tensor_copy(windows[1][:].indirect(slots(c0, n, e)), dx[:])
+            scatter_on_vector(dx[:], e, c0, n, 1)
 
         for t in range(PACK):
             gather_on_scalar(0, 0, t)
             gather_gated(1, 0, t)
+            if t == 1:
+                for e in range(E):
+                    permute_scales(e)
+        weave(1, 0)
         weave_gating(0, 0)
         quantize_g(0, 0)
-        for t in range(PACK - 1):
+        for t in range(PACK):
             gather_on_scalar(0, 1, t)
-        gather_on_vector(0, 1, PACK - 1)
-        weave_gating(0, 1)
-        quantize_g(0, 1)
-        g_woven[1, 0] = tile([P, C * PACK], BF16, "g01")
-        weave(1, 0)
+        for half in range(2):
+            weave_gating(0, 1, half * HALF, (half + 1) * HALF)
+        for half in range(2):
+            quantize_g(0, 1, half * HALF, (half + 1) * HALF)
+        g_codes[1, 0] = tile([P, C], U32, "gate0")
+        quantize_g(1, 0)
         for sn in range(SN):
             permute_words(0, sn)
-        order0 = [(si, 2 * pair + ql) for pair in range(2) for si in range(SI) for ql in range(2)]
-        for x, (si, q) in enumerate(order0[:4]):
+        order = [(si, 2 * pair + ql) for pair in range(2) for si in range(SI) for ql in range(2)]
+        for x, (si, q) in enumerate(order[:4]):
             first_product(0, si, q, 0, x)
-        g[1, 1] = tile([P, PACK, C], F32, "w2raw0")
-        for t in range(PACK):
-            gather_on_scalar(1, 1, t)
+        gather_on_scalar(1, 1, 0)
+        g_woven[1, 1] = tile([P, C * PACK], BF16, "gw01")
+        for half in range(2):
+            for t in range(1, PACK):
+                gather_on_scalar(1, 1, t, half * HALF, HALF)
+            for q in (2 * half, 2 * half + 1):
+                weave_last(q)
         for sn in range(SN):
             permute_words(1, sn)
 
-        order1 = [(si, q) for q in range(Q) for si in range(SI)]
-        for x, (si, q) in enumerate(order0):
+        for x, (si, q) in enumerate(order):
             first_product(0, si, q, 1)
             if x < 4:
-                first_product(0, *order0[x + 4], 0, x + 4)
+                first_product(0, *order[x + 4], 0, x + 4)
             derive(0, si, q)
             if x == 4:
                 quantize_da(0, 0)
-                back_on_scalar(0, 0, 256, 0)
-        g_codes[1, 0] = tile([P, C], U32, "daw00")
-        quantize_g(1, 0)
+                dx = both_rows(0, 0, 256, 0)
+                for k in (1, 0):
+                    scatter_on_scalar(dx[:, k, :], 0, 0, 256, k)
+        g_codes[1, 1] = tile([P, C], U32, "a01")
+        quantize_g(1, 1)
         quantize_da(0, 256)
-        back_on_scalar(0, 256, 256, 1)
-        g_woven[1, 1] = tile([P, C * PACK], BF16, "a00")
-        for half in range(2):
-            weave_gating(1, 1, half * C // 2, (half + 1) * C // 2)
-        for half in range(2):
-            quantize_g(1, 1, half * C // 2, (half + 1) * C // 2)
-        for x, (si, q) in enumerate(order1[:6]):
+        dx = both_rows(0, 256, 256, 1)
+        for k in (1, 0):
+            scatter_on_scalar(dx[:, k, :], 0, 256, 256, k)
+        for x, (si, q) in enumerate(order[:6]):
             first_product(1, si, q, 0, 2 + x)
 
-        for x, (si, q) in enumerate(order1):
+        for x, (si, q) in enumerate(order):
             if x >= 6:
                 first_product(1, si, q, 0, x - 6)
             first_product(1, si, q, 1)
             derive(1, si, q)
-            if x in (2, 4):
-                quantize_da(1, (x // 2 - 1) * P)
-                back_on_scalar(1, (x // 2 - 1) * P, P, x // 2 + 1)
-            if x == 6:
-                quantize_da(1, 256)
-                middle = back_on_both(1, 256, 128, (4, 5))
+            if x == 4:
+                quantize_da(1, 0)
+                dx = both_rows(1, 0, 256, 2)
+                scatter_on_scalar(dx[:, 1, 0:P], 1, 0, P, 1)
+                scatter_on_scalar(dx[:, 0, :], 1, 0, 256, 0)
+        quantize_da(1, 256)
+        middle = back_on_both(1, 256, 128, (4, 5))
         quantize_da(1, 384)
         last = back_on_both(1, 384, 128, (6, 7))
+        scatter_on_vector(dx[:, 1, P : 2 * P], 1, P, P, 1)
         finish_on_vector(1, 256, 128, *middle)
         finish_on_vector(1, 384, 128, *last)
         for k in range(KT):

@@ -29,7 +29,7 @@ def tile_moe_bdx_mlp_relu2_kernel(
     STRIPE = 16
     ROWS = 4
     ALIGN = 64
-    PIECES = (((0, 256), (256, 256)), ((0, 256), (256, 128), (384, 128)))
+    PIECES = (((0, 256), (256, 256)), ((0, 128), (128, 128), (256, 128), (384, 128)))
     HALF = C // 2
 
     with ExitStack() as ctx:
@@ -45,22 +45,24 @@ def tile_moe_bdx_mlp_relu2_kernel(
         gate_t = [tile([P, C], F32, f"gate{e}") for e in range(E)]
         a_t = {x: tile([P, PACK, C], F32, f"a{x[0]}{x[1]}") for x in groups}
         w2_raw = [tile([P, SN, 2 * H], U8, f"w2raw{e}") for e in range(E)]
-        w2s_raw = tile([P, E * SN, H], U8, "w2sraw")
+        w2s_raw = tile([P, H], U8, "w2sraw")
         w2_t = {x: tile([P, 2 * H], U8, f"w2{x[0]}{x[1]}") for x in groups}
-        w2s_t = [tile([P, SN, H], U8, f"w2s{e}") for e in range(E)]
+        w2s_t = {x: tile([P, H], U8, f"w2s{x[0]}{x[1]}") for x in groups}
         w1_t = tile([P, E * SI, 2 * K], U8, "w1t")
         w1s_t = tile([P, E * SI, K], U8, "w1s")
 
         dy_v = dyT.rearrange("(s p t) c -> s t p c", p=P, t=PACK)
         a_v = a.rearrange("(s p t) (e c) -> e s p t c", p=P, t=PACK, e=E)
         w2_v = w2_words.bitcast(I32).rearrange("e s p b -> e p s b")
-        w2s_v = w2_scales.bitcast(I32).rearrange("e s (x r) i -> r x (e s) i", r=ROWS)
+        w2s_v = w2_scales.bitcast(I32).rearrange("e s (x r) i -> x (e s) r i", r=ROWS)
         w1_v = w1_words.bitcast(I32).rearrange("e s p b -> p (e s) b")
         w1s_v = w1_scales.bitcast(I32).rearrange("e s (x r) i -> r x (e s) i", r=ROWS)
 
         nc.sync.dma_start(offsets[:], offs)
         nc.vector.memset(w2s_raw[:].bitcast(I32), 0)
         nc.vector.memset(w1s_t[:].bitcast(I32), 0)
+        for x in groups[1:]:
+            nc.vector.memset(w2s_t[x][:].bitcast(I32), 0)
 
         def load_dy(sn, t):
             nc.sync.dma_start(dy_t[sn][t][:], dy_v[sn, t])
@@ -70,10 +72,9 @@ def tile_moe_bdx_mlp_relu2_kernel(
 
         load_dy(0, 0)
         nc.sync.dma_start(gate_t[1][:], gate[0:P, C : 2 * C])
-        load_dy(0, 1)
-        for row in range(ROWS):
-            nc.sync.dma_start(w2s_raw[row:P:32, :, :].bitcast(I32), w2s_v[row])
-        for t in range(2, PACK):
+        for x in range(P // 32):
+            nc.sync.dma_start(w2s_raw[32 * x : 32 * x + E * SN * ROWS, :].bitcast(I32), w2s_v[x])
+        for t in range(1, PACK):
             load_dy(0, t)
         load_dy(1, 0)
         nc.sync.dma_start(gate_t[0][:], gate[0:P, 0:C])
@@ -93,8 +94,8 @@ def tile_moe_bdx_mlp_relu2_kernel(
         shared = tile([P, PACK + 1, C], F32, "g1")
         g[1, 1] = shared[:, 0:PACK, :]
         g[0, 1] = shared[:, 1 : PACK + 1, :]
-        g_woven = {x: tile([P, C * PACK], BF16, f"gw{x[0]}{x[1]}") for x in groups if x != (1, 1)}
-        g_codes = {x: tile([P, C], U32, f"gc{x[0]}{x[1]}") for x in groups if x[0] == 0}
+        g_woven = {x: tile([P, C * PACK], BF16, f"gw{x[0]}{x[1]}") for x in groups if x[0] == 0}
+        g_codes = {x: tile([P, C], U32, f"gc{x[0]}{x[1]}") for x in groups if x != (1, 0)}
         g_scales = {x: tile([P, C], U8, f"gs{x[0]}{x[1]}") for x in groups}
         da_woven, da_codes, da_scales = {}, {}, {}
         for e in range(E):
@@ -114,6 +115,9 @@ def tile_moe_bdx_mlp_relu2_kernel(
         def gather_on_scalar(e, sn, t, c0=0, n=C):
             nc.scalar.activation(g[e, sn][:, t, c0 : c0 + n], dy_t[sn][t][:].indirect(slots(c0, n, e)), COPY)
 
+        def gather_on_vector(e, sn, t):
+            nc.vector.tensor_copy(g[e, sn][:, t, :], dy_t[sn][t][:].indirect(slots(0, C, e)))
+
         def gather_gated(e, sn, t):
             nc.vector.tensor_tensor(g[e, sn][:, t, :], dy_t[sn][t][:].indirect(slots(0, C, e)), gate_t[e][:], ALU.mult)
 
@@ -125,18 +129,10 @@ def tile_moe_bdx_mlp_relu2_kernel(
                 ALU.mult,
             )
 
-        def weave_last(q):
-            nc.gpsimd.tensor_tensor(
-                g_woven[1, 1][:, q * PASS : (q + 1) * PASS].rearrange("p (c t) -> p c t", t=PACK),
-                g[1, 1][:, :, q * P : (q + 1) * P].rearrange("p t c -> p c t"),
-                gate_t[1][:, q * P : (q + 1) * P].unsqueeze(2).to_broadcast([P, P, PACK]),
-                ALU.mult,
-            )
-
         def weave(e, sn):
-            nc.vector.tensor_copy(
-                g_woven[e, sn][:].rearrange("p (c v t) -> p c t v", v=4, t=PACK),
-                g[e, sn].rearrange("p t (c v) -> p c t v", v=4),
+            nc.scalar.copy(
+                out=g_woven[e, sn][:].rearrange("p (c v t) -> p c t v", v=4, t=PACK),
+                in_=g[e, sn].rearrange("p t (c v) -> p c t v", v=4),
             )
 
         def quantize_g(e, sn, c0=0, c1=C):
@@ -150,11 +146,15 @@ def tile_moe_bdx_mlp_relu2_kernel(
                 in_=w2_raw[e][:, sn, :].bitcast(U16).rearrange("p (s m t) -> p s t m", s=SI, t=PACK),
             )
 
-        def permute_scales(e):
+        def permute_scales():
             nc.vector.tensor_copy(
-                w2s_t[e][:].rearrange("p n (s t m) -> p (n s) t m", s=SI, t=PACK),
-                w2s_raw[:, e * SN : (e + 1) * SN, :].rearrange("p n (s m t) -> p (n s) t m", s=SI, t=PACK),
+                w2s_t[0, 0][:].rearrange("p (s t m) -> p s t m", s=SI, t=PACK),
+                w2s_raw[:].rearrange("p (s m t) -> p s t m", s=SI, t=PACK),
             )
+            for e, sn in groups[1:]:
+                at = ROWS * (e * SN + sn)
+                for row in range(ROWS):
+                    nc.gpsimd.dma_start(w2s_t[e, sn][row:P:32, :].bitcast(I32), w2s_t[0, 0][at + row : P : 32, :].bitcast(I32))
 
         def first_product(e, si, q, sn, bank=None):
             if sn == 0:
@@ -164,7 +164,7 @@ def tile_moe_bdx_mlp_relu2_kernel(
                 nc.tensor.matmul_mx(
                     out=dh_bank[e, si, q][:, t, :],
                     lhsT=w2_t[e, sn][:, 2 * col : 2 * (col + P)].bitcast(E2M1),
-                    lhsT_scale=w2s_t[e][:, sn, col : col + P],
+                    lhsT_scale=w2s_t[e, sn][:, col : col + P],
                     rhs=g_codes[e, sn][:, q * P : (q + 1) * P].bitcast(E5M2),
                     rhs_scale=g_scales[e, sn][:, q * P : (q + 1) * P],
                     start=(sn == 0 and t == 0),
@@ -233,69 +233,75 @@ def tile_moe_bdx_mlp_relu2_kernel(
         for t in range(PACK):
             gather_on_scalar(0, 0, t)
             gather_gated(1, 0, t)
-            if t == 1:
-                for e in range(E):
-                    permute_scales(e)
-        weave(1, 0)
+            if t == 0:
+                permute_scales()
         weave_gating(0, 0)
         quantize_g(0, 0)
-        for t in range(PACK):
+        for t in range(PACK - 1):
             gather_on_scalar(0, 1, t)
+        gather_on_vector(0, 1, PACK - 1)
         for half in range(2):
             weave_gating(0, 1, half * HALF, (half + 1) * HALF)
         for half in range(2):
             quantize_g(0, 1, half * HALF, (half + 1) * HALF)
-        g_codes[1, 0] = tile([P, C], U32, "gate0")
-        quantize_g(1, 0)
         for sn in range(SN):
             permute_words(0, sn)
         order = [(si, 2 * pair + ql) for pair in range(2) for si in range(SI) for ql in range(2)]
-        for x, (si, q) in enumerate(order[:4]):
+        for x, (si, q) in enumerate(order[:3]):
             first_product(0, si, q, 0, x)
         gather_on_scalar(1, 1, 0)
-        g_woven[1, 1] = tile([P, C * PACK], BF16, "gw01")
-        for half in range(2):
-            for t in range(1, PACK):
-                gather_on_scalar(1, 1, t, half * HALF, HALF)
-            for q in (2 * half, 2 * half + 1):
-                weave_last(q)
+        for t in range(1, PACK):
+            gather_on_scalar(1, 1, t)
+        g_woven[1, 0] = tile([P, C * PACK], BF16, "gw01")
+        weave(1, 0)
         for sn in range(SN):
             permute_words(1, sn)
 
         for x, (si, q) in enumerate(order):
             first_product(0, si, q, 1)
-            if x < 4:
-                first_product(0, *order[x + 4], 0, x + 4)
+            if x < 5:
+                first_product(0, *order[x + 3], 0, x + 3)
             derive(0, si, q)
             if x == 4:
                 quantize_da(0, 0)
                 dx = both_rows(0, 0, 256, 0)
                 for k in (1, 0):
                     scatter_on_scalar(dx[:, k, :], 0, 0, 256, k)
-        g_codes[1, 1] = tile([P, C], U32, "a01")
-        quantize_g(1, 1)
+        g_codes[1, 0] = tile([P, C], U32, "daw00")
+        quantize_g(1, 0)
+        g_woven[1, 1] = tile([P, C * PACK], BF16, "a00")
+        weave_gating(1, 1, 0, HALF)
         quantize_da(0, 256)
         dx = both_rows(0, 256, 256, 1)
         for k in (1, 0):
             scatter_on_scalar(dx[:, k, :], 0, 256, 256, k)
-        for x, (si, q) in enumerate(order[:6]):
+        weave_gating(1, 1, HALF, C)
+        for half in range(2):
+            quantize_g(1, 1, half * HALF, (half + 1) * HALF)
+        order = [(si, q) for q in range(Q) for si in range(SI)]
+        for x, (si, q) in enumerate(order[:4]):
             first_product(1, si, q, 0, 2 + x)
 
         for x, (si, q) in enumerate(order):
-            if x >= 6:
-                first_product(1, si, q, 0, x - 6)
             first_product(1, si, q, 1)
+            if x < 4:
+                first_product(1, *order[x + 4], 0, (x + 6) % 8)
             derive(1, si, q)
-            if x == 4:
+            if x == 2:
                 quantize_da(1, 0)
-                dx = both_rows(1, 0, 256, 2)
-                scatter_on_scalar(dx[:, 1, 0:P], 1, 0, P, 1)
-                scatter_on_scalar(dx[:, 0, :], 1, 0, 256, 0)
-        quantize_da(1, 256)
-        middle = back_on_both(1, 256, 128, (4, 5))
+                dx = both_rows(1, 0, P, 2)
+                for k in (1, 0):
+                    scatter_on_scalar(dx[:, k, :], 1, 0, P, k)
+            if x == 4:
+                quantize_da(1, P)
+                dx = both_rows(1, P, P, 3)
+                for k in (1, 0):
+                    scatter_on_scalar(dx[:, k, :], 1, P, P, k)
+            if x == 6:
+                quantize_da(1, 256)
+                middle = back_on_both(1, 256, 128, (4, 5))
         quantize_da(1, 384)
         last = back_on_both(1, 384, 128, (6, 7))
-        scatter_on_vector(dx[:, 1, P : 2 * P], 1, P, P, 1)
         finish_on_vector(1, 256, 128, *middle)
         finish_on_vector(1, 384, 128, *last)
         for k in range(KT):

@@ -19,6 +19,7 @@ E5M2 = mybir.dt.float8_e5m2_x4
 E2M1 = mybir.dt.float4_e2m1fn_x4
 ALU = mybir.AluOpType
 COPY = mybir.ActivationFunctionType.Copy
+F32_MAX = 3.4028234663852886e38
 
 
 def tile_moe_bdx_mlp_relu2_kernel(
@@ -34,10 +35,14 @@ def tile_moe_bdx_mlp_relu2_kernel(
 
     with ExitStack() as ctx:
         held = ctx.enter_context(tc.tile_pool(name="held", bufs=1))
+        heirs = ctx.enter_context(tc.tile_pool(name="heirs", bufs=1))
         psum = ctx.enter_context(tc.psum_pool(name="psum", bufs=1))
 
         def tile(shape, dtype, name):
             return held.tile(shape, dtype, name=name, align_bytes=ALIGN)
+
+        def heir(shape, dtype, name, offset):
+            return heirs.tile(shape, dtype, name=name, offset=offset, align_bytes=ALIGN)
 
         groups = [(e, s) for e in range(E) for s in range(2)]
         offsets = held.tile([P, E * C // STRIPE], U16, name="offsets")
@@ -83,28 +88,27 @@ def tile_moe_bdx_mlp_relu2_kernel(
         nc.sync.dma_start(w2_raw[0][:].bitcast(I32), w2_v[0])
         load_a(0, 0)
         load_a(0, 1)
-        nc.sync.dma_start(w2_raw[1][:].bitcast(I32), w2_v[1])
         for row in range(ROWS):
             nc.sync.dma_start(w1s_t[row:P:32, :, :].bitcast(I32), w1s_v[row])
         nc.sync.dma_start(w1_t[:].bitcast(I32), w1_v)
+        nc.sync.dma_start(w2_raw[1][:].bitcast(I32), w2_v[1])
         load_a(1, 0)
         load_a(1, 1)
 
-        g = {(e, 0): tile([P, PACK, C], F32, f"g{e}0")[:] for e in range(E)}
-        shared = tile([P, PACK + 1, C], F32, "g1")
-        g[1, 1] = shared[:, 0:PACK, :]
-        g[0, 1] = shared[:, 1 : PACK + 1, :]
-        g_woven = {x: tile([P, C * PACK], BF16, f"gw{x[0]}{x[1]}") for x in groups if x[0] == 0}
+        g = {x: tile([P, PACK, C], F32, f"g{x[0]}{x[1]}")[:] for x in groups if x != (1, 1)}
+        g_woven = {(0, 0): tile([P, C * PACK], BF16, "gw00"), (0, 1): tile([P, C * PACK], BF16, "gw01")}
         g_codes = {x: tile([P, C], U32, f"gc{x[0]}{x[1]}") for x in groups if x != (1, 0)}
         g_scales = {x: tile([P, C], U8, f"gs{x[0]}{x[1]}") for x in groups}
         da_woven, da_codes, da_scales = {}, {}, {}
         for e in range(E):
             for c0, n in PIECES[e]:
-                da_woven[e, c0] = tile([P, SI, n * PACK], BF16, f"daw{e}{c0}")
+                if (e, c0) != (0, 0):
+                    da_woven[e, c0] = tile([P, SI, n * PACK], BF16, f"daw{e}{c0}")
                 da_codes[e, c0] = tile([P, SI, n], U32, f"dc{e}{c0}")
                 da_scales[e, c0] = tile([P, SI, n], U8, f"ds{e}{c0}")
+        da_woven[0, 0] = heir([P, SI, HALF * PACK], BF16, "daw_first", 0)
         windows = [tile([P, T], F32, f"window{k}") for k in range(KT)]
-        dh_bank = {}
+        dh_bank, rectified = {}, {}
 
         def bank_tile(shape, bank):
             return psum.tile(shape, F32, name=f"bank{bank}")
@@ -130,9 +134,9 @@ def tile_moe_bdx_mlp_relu2_kernel(
             )
 
         def weave(e, sn):
-            nc.scalar.copy(
-                out=g_woven[e, sn][:].rearrange("p (c v t) -> p c t v", v=4, t=PACK),
-                in_=g[e, sn].rearrange("p t (c v) -> p c t v", v=4),
+            nc.vector.tensor_copy(
+                g_woven[e, sn][:].rearrange("p (c v t) -> p c t v", v=4, t=PACK),
+                g[e, sn].rearrange("p t (c v) -> p c t v", v=4),
             )
 
         def quantize_g(e, sn, c0=0, c1=C):
@@ -151,10 +155,16 @@ def tile_moe_bdx_mlp_relu2_kernel(
                 w2s_t[0, 0][:].rearrange("p (s t m) -> p s t m", s=SI, t=PACK),
                 w2s_raw[:].rearrange("p (s m t) -> p s t m", s=SI, t=PACK),
             )
-            for e, sn in groups[1:]:
-                at = ROWS * (e * SN + sn)
-                for row in range(ROWS):
-                    nc.gpsimd.dma_start(w2s_t[e, sn][row:P:32, :].bitcast(I32), w2s_t[0, 0][at + row : P : 32, :].bitcast(I32))
+
+        def move_scales(e, sn):
+            at = ROWS * (e * SN + sn)
+            for row in range(ROWS):
+                nc.gpsimd.dma_start(w2s_t[e, sn][row:P:32, :].bitcast(I32), w2s_t[0, 0][at + row : P : 32, :].bitcast(I32))
+
+        def rectify(e):
+            rectified[e] = tile([P, SI, PACK, HALF], F32, "g10")
+            for si in range(SI):
+                nc.gpsimd.tensor_scalar(rectified[e][:, si], a_t[e, si][:, :, HALF:C], F32_MAX, 0.0, ALU.min, ALU.max)
 
         def first_product(e, si, q, sn, bank=None):
             if sn == 0:
@@ -174,6 +184,14 @@ def tile_moe_bdx_mlp_relu2_kernel(
         def derive(e, si, q):
             c0 = max(first for first, n in PIECES[e] if first <= q * P)
             at = (q * P - c0) * PACK
+            if e == 0 and q >= Q // 2:
+                nc.vector.tensor_tensor(
+                    da_woven[e, c0][:, si, at : at + PASS].rearrange("p (c v t) -> p c t v", v=2, t=PACK),
+                    rectified[e][:, si, :, q * P - HALF : (q + 1) * P - HALF].rearrange("p t (c v) -> p c t v", v=2),
+                    dh_bank[e, si, q][:].rearrange("p t (c v) -> p c t v", v=2),
+                    ALU.mult,
+                )
+                return
             nc.vector.scalar_tensor_tensor(
                 da_woven[e, c0][:, si, at : at + PASS].rearrange("p (c t) -> p c t", t=PACK),
                 a_t[e, si][:, :, q * P : (q + 1) * P].rearrange("p t c -> p c t"),
@@ -208,33 +226,34 @@ def tile_moe_bdx_mlp_relu2_kernel(
         def scatter_on_vector(dx, e, c0, n, k):
             nc.vector.tensor_copy(windows[k][:].indirect(slots(c0, n, e)), dx)
 
-        def both_rows(e, c0, n, bank):
+        def both_rows(e, c0, n, bank, name):
             dx_bank = bank_tile([P, KT, n], bank)
             for k in range(KT):
                 second_product(e, c0, n, k, dx_bank[:, k, :])
-            dx = tile([P, KT, n], F32, f"dx{e}{c0}")
+            dx = tile([P, KT, n], F32, name)
             for k in (1, 0):
                 nc.scalar.activation(dx[:, k, :], dx_bank[:, k, :], COPY, scale=2.0)
             return dx
 
         def back_on_both(e, c0, n, banks):
             dx_banks = [bank_tile([P, n], bank) for bank in banks]
-            dx = [tile([P, n], F32, f"dx{e}{c0}{k}") for k in range(KT)]
             for k in range(KT):
                 second_product(e, c0, n, k, dx_banks[k][:])
-            nc.scalar.activation(dx[0][:], dx_banks[0][:], COPY, scale=2.0)
-            scatter_on_scalar(dx[0][:], e, c0, n, 0)
-            return dx_banks[1], dx[1]
+            dx = tile([P, n], F32, f"dx{e}{c0}0")
+            nc.scalar.activation(dx[:], dx_banks[0][:], COPY, scale=2.0)
+            scatter_on_scalar(dx[:], e, c0, n, 0)
+            return dx_banks[1]
 
-        def finish_on_vector(e, c0, n, dx_bank, dx):
-            nc.vector.tensor_scalar(dx[:], dx_bank[:], 2.0, None, ALU.mult)
-            scatter_on_vector(dx[:], e, c0, n, 1)
+        def drain_on_vector(dx, dx_bank):
+            nc.vector.tensor_scalar(dx, dx_bank[:], 2.0, None, ALU.mult)
 
         for t in range(PACK):
             gather_on_scalar(0, 0, t)
             gather_gated(1, 0, t)
             if t == 0:
                 permute_scales()
+                move_scales(0, 1)
+                move_scales(1, 0)
         weave_gating(0, 0)
         quantize_g(0, 0)
         for t in range(PACK - 1):
@@ -244,18 +263,21 @@ def tile_moe_bdx_mlp_relu2_kernel(
             weave_gating(0, 1, half * HALF, (half + 1) * HALF)
         for half in range(2):
             quantize_g(0, 1, half * HALF, (half + 1) * HALF)
+        g_woven[1, 0] = tile([P, C * PACK], BF16, "g01")
+        weave(1, 0)
         for sn in range(SN):
             permute_words(0, sn)
         order = [(si, 2 * pair + ql) for pair in range(2) for si in range(SI) for ql in range(2)]
         for x, (si, q) in enumerate(order[:3]):
             first_product(0, si, q, 0, x)
-        gather_on_scalar(1, 1, 0)
-        for t in range(1, PACK):
+        g[1, 1] = tile([P, PACK, C], F32, "w2raw0")[:]
+        for t in range(PACK):
             gather_on_scalar(1, 1, t)
-        g_woven[1, 0] = tile([P, C * PACK], BF16, "gw01")
-        weave(1, 0)
         for sn in range(SN):
             permute_words(1, sn)
+
+        rectify(0)
+        move_scales(1, 1)
 
         for x, (si, q) in enumerate(order):
             first_product(0, si, q, 1)
@@ -264,45 +286,48 @@ def tile_moe_bdx_mlp_relu2_kernel(
             derive(0, si, q)
             if x == 4:
                 quantize_da(0, 0)
-                dx = both_rows(0, 0, 256, 0)
+                dx = both_rows(0, 0, 256, 0, "w2raw1")
                 for k in (1, 0):
                     scatter_on_scalar(dx[:, k, :], 0, 0, 256, k)
-        g_codes[1, 0] = tile([P, C], U32, "daw00")
-        quantize_g(1, 0)
-        g_woven[1, 1] = tile([P, C * PACK], BF16, "a00")
+            if x == 5:
+                g_codes[1, 0] = heir([P, C], U32, "gc10", 0)
+                quantize_g(1, 0)
+        g_woven[1, 1] = heir([P, C * PACK], BF16, "gw11", 4 * C)
         weave_gating(1, 1, 0, HALF)
         quantize_da(0, 256)
-        dx = both_rows(0, 256, 256, 1)
+        dx = both_rows(0, 256, 256, 1, "dx01")
         for k in (1, 0):
             scatter_on_scalar(dx[:, k, :], 0, 256, 256, k)
+        quantize_g(1, 1, 0, HALF)
         weave_gating(1, 1, HALF, C)
-        for half in range(2):
-            quantize_g(1, 1, half * HALF, (half + 1) * HALF)
+        quantize_g(1, 1, HALF, C)
         order = [(si, q) for q in range(Q) for si in range(SI)]
-        for x, (si, q) in enumerate(order[:4]):
-            first_product(1, si, q, 0, 2 + x)
+        for x, (si, q) in enumerate(order[:7]):
+            first_product(1, si, q, 0, (x + 2) % 8)
 
         for x, (si, q) in enumerate(order):
             first_product(1, si, q, 1)
-            if x < 4:
-                first_product(1, *order[x + 4], 0, (x + 6) % 8)
             derive(1, si, q)
+            if x == 0:
+                first_product(1, *order[7], 0, 2)
             if x == 2:
                 quantize_da(1, 0)
-                dx = both_rows(1, 0, P, 2)
+                dx = both_rows(1, 0, P, 3, "dx10")
                 for k in (1, 0):
                     scatter_on_scalar(dx[:, k, :], 1, 0, P, k)
             if x == 4:
                 quantize_da(1, P)
-                dx = both_rows(1, P, P, 3)
-                for k in (1, 0):
-                    scatter_on_scalar(dx[:, k, :], 1, P, P, k)
+                second = back_on_both(1, P, P, (4, 5))
             if x == 6:
                 quantize_da(1, 256)
-                middle = back_on_both(1, 256, 128, (4, 5))
+                third = back_on_both(1, 256, 128, (6, 7))
         quantize_da(1, 384)
-        last = back_on_both(1, 384, 128, (6, 7))
-        finish_on_vector(1, 256, 128, *middle)
-        finish_on_vector(1, 384, 128, *last)
+        last = back_on_both(1, 384, 128, (0, 1))
+        dx = tile([P, 3 * P], F32, "a11")
+        drain_on_vector(dx[:, 0:P], second)
+        drain_on_vector(dx[:, P : 2 * P], third)
+        scatter_on_vector(dx[:, 0 : 2 * P], 1, P, 2 * P, 1)
+        drain_on_vector(dx[:, 2 * P : 3 * P], last)
+        scatter_on_vector(dx[:, 2 * P : 3 * P], 1, 3 * P, P, 1)
         for k in range(KT):
             nc.sync.dma_start(out[k * P : (k + 1) * P, :], windows[k][:])

@@ -50,24 +50,23 @@ def tile_moe_bdx_mlp_relu2_kernel(
         gate_t = [tile([P, C], F32, f"gate{e}") for e in range(E)]
         a_t = {x: tile([P, PACK, C], F32, f"a{x[0]}{x[1]}") for x in groups}
         w2_raw = [tile([P, SN, 2 * H], U8, f"w2raw{e}") for e in range(E)]
-        w2s_raw = tile([P, H], U8, "w2sraw")
+        w2s_raw = tile([P, SN, H], U8, "w2sraw")
         w2_t = {x: tile([P, 2 * H], U8, f"w2{x[0]}{x[1]}") for x in groups}
-        w2s_t = {x: tile([P, H], U8, f"w2s{x[0]}{x[1]}") for x in groups}
+        w2s_t = [tile([P, SN, H], U8, f"w2s{e}") for e in range(E)]
         w1_t = tile([P, E * SI, 2 * K], U8, "w1t")
         w1s_t = tile([P, E * SI, K], U8, "w1s")
 
         dy_v = dyT.rearrange("(s p t) c -> s t p c", p=P, t=PACK)
         a_v = a.rearrange("(s p t) (e c) -> e s p t c", p=P, t=PACK, e=E)
         w2_v = w2_words.bitcast(I32).rearrange("e s p b -> e p s b")
-        w2s_v = w2_scales.bitcast(I32).rearrange("e s (x r) i -> x (e s) r i", r=ROWS)
+        w2s_v = w2_scales.bitcast(I32).rearrange("e s (x r) i -> e r x s i", r=ROWS)
         w1_v = w1_words.bitcast(I32).rearrange("e s p b -> p (e s) b")
         w1s_v = w1_scales.bitcast(I32).rearrange("e s (x r) i -> r x (e s) i", r=ROWS)
 
         nc.sync.dma_start(offsets[:], offs)
         nc.vector.memset(w2s_raw[:].bitcast(I32), 0)
         nc.vector.memset(w1s_t[:].bitcast(I32), 0)
-        for x in groups[1:]:
-            nc.vector.memset(w2s_t[x][:].bitcast(I32), 0)
+        nc.vector.memset(w2s_t[1][:].bitcast(I32), 0)
 
         def load_dy(sn, t):
             nc.sync.dma_start(dy_t[sn][t][:], dy_v[sn, t])
@@ -75,12 +74,17 @@ def tile_moe_bdx_mlp_relu2_kernel(
         def load_a(e, si):
             nc.sync.dma_start(a_t[e, si][:], a_v[e, si])
 
+        def load_scales(e):
+            for row in range(ROWS):
+                nc.sync.dma_start(w2s_raw[ROWS * e + row : P : 32, :, :].bitcast(I32), w2s_v[e, row])
+
         load_dy(0, 0)
         nc.sync.dma_start(gate_t[1][:], gate[0:P, C : 2 * C])
-        for x in range(P // 32):
-            nc.sync.dma_start(w2s_raw[32 * x : 32 * x + E * SN * ROWS, :].bitcast(I32), w2s_v[x])
-        for t in range(1, PACK):
-            load_dy(0, t)
+        load_dy(0, 1)
+        load_dy(0, 2)
+        load_scales(0)
+        load_dy(0, 3)
+        load_scales(1)
         load_dy(1, 0)
         nc.sync.dma_start(gate_t[0][:], gate[0:P, 0:C])
         for t in range(1, PACK):
@@ -152,14 +156,11 @@ def tile_moe_bdx_mlp_relu2_kernel(
 
         def permute_scales():
             nc.vector.tensor_copy(
-                w2s_t[0, 0][:].rearrange("p (s t m) -> p s t m", s=SI, t=PACK),
-                w2s_raw[:].rearrange("p (s m t) -> p s t m", s=SI, t=PACK),
+                w2s_t[0][:].rearrange("p n (s t m) -> p (n s) t m", s=SI, t=PACK),
+                w2s_raw[:].rearrange("p n (s m t) -> p (n s) t m", s=SI, t=PACK),
             )
-
-        def move_scales(e, sn):
-            at = ROWS * (e * SN + sn)
             for row in range(ROWS):
-                nc.gpsimd.dma_start(w2s_t[e, sn][row:P:32, :].bitcast(I32), w2s_t[0, 0][at + row : P : 32, :].bitcast(I32))
+                nc.gpsimd.dma_start(w2s_t[1][row:P:32, :, :].bitcast(I32), w2s_t[0][ROWS + row : P : 32, :, :].bitcast(I32))
 
         def rectify(e):
             rectified[e] = tile([P, SI, PACK, HALF], F32, "g10")
@@ -174,7 +175,7 @@ def tile_moe_bdx_mlp_relu2_kernel(
                 nc.tensor.matmul_mx(
                     out=dh_bank[e, si, q][:, t, :],
                     lhsT=w2_t[e, sn][:, 2 * col : 2 * (col + P)].bitcast(E2M1),
-                    lhsT_scale=w2s_t[e, sn][:, col : col + P],
+                    lhsT_scale=w2s_t[e][:, sn, col : col + P],
                     rhs=g_codes[e, sn][:, q * P : (q + 1) * P].bitcast(E5M2),
                     rhs_scale=g_scales[e, sn][:, q * P : (q + 1) * P],
                     start=(sn == 0 and t == 0),
@@ -250,10 +251,7 @@ def tile_moe_bdx_mlp_relu2_kernel(
         for t in range(PACK):
             gather_on_scalar(0, 0, t)
             gather_gated(1, 0, t)
-            if t == 0:
-                permute_scales()
-                move_scales(0, 1)
-                move_scales(1, 0)
+        permute_scales()
         weave_gating(0, 0)
         quantize_g(0, 0)
         for t in range(PACK - 1):
@@ -277,7 +275,6 @@ def tile_moe_bdx_mlp_relu2_kernel(
             permute_words(1, sn)
 
         rectify(0)
-        move_scales(1, 1)
 
         for x, (si, q) in enumerate(order):
             first_product(0, si, q, 1)
@@ -321,11 +318,11 @@ def tile_moe_bdx_mlp_relu2_kernel(
             if x == 6:
                 quantize_da(1, 256)
                 third = back_on_both(1, 256, 128, (6, 7))
-        quantize_da(1, 384)
-        last = back_on_both(1, 384, 128, (0, 1))
-        dx = tile([P, 3 * P], F32, "a11")
+        dx = tile([P, 3 * P], F32, "a10")
         drain_on_vector(dx[:, 0:P], second)
         drain_on_vector(dx[:, P : 2 * P], third)
+        quantize_da(1, 384)
+        last = back_on_both(1, 384, 128, (0, 1))
         scatter_on_vector(dx[:, 0 : 2 * P], 1, P, 2 * P, 1)
         drain_on_vector(dx[:, 2 * P : 3 * P], last)
         scatter_on_vector(dx[:, 2 * P : 3 * P], 1, 3 * P, P, 1)

@@ -30,7 +30,7 @@ def tile_moe_bdx_mlp_relu2_kernel(
     STRIPE = 16
     ROWS = 4
     ALIGN = 64
-    PIECES = (((0, 256), (256, 256)), ((0, 128), (128, 128), (256, 128), (384, 128)))
+    PIECES = (((0, 256), (256, 256)), ((0, 256), (256, 128), (384, 128)))
     HALF = C // 2
 
     with ExitStack() as ctx:
@@ -106,7 +106,7 @@ def tile_moe_bdx_mlp_relu2_kernel(
         da_woven, da_codes, da_scales = {}, {}, {}
         for e in range(E):
             for c0, n in PIECES[e]:
-                if (e, c0) != (0, 0):
+                if c0 != 0:
                     da_woven[e, c0] = tile([P, SI, n * PACK], BF16, f"daw{e}{c0}")
                 da_codes[e, c0] = tile([P, SI, n], U32, f"dc{e}{c0}")
                 da_scales[e, c0] = tile([P, SI, n], U8, f"ds{e}{c0}")
@@ -162,10 +162,9 @@ def tile_moe_bdx_mlp_relu2_kernel(
             for row in range(ROWS):
                 nc.gpsimd.dma_start(w2s_t[1][row:P:32, :, :].bitcast(I32), w2s_t[0][ROWS + row : P : 32, :, :].bitcast(I32))
 
-        def rectify(e):
-            rectified[e] = tile([P, SI, PACK, HALF], F32, "g10")
-            for si in range(SI):
-                nc.gpsimd.tensor_scalar(rectified[e][:, si], a_t[e, si][:, :, HALF:C], F32_MAX, 0.0, ALU.min, ALU.max)
+        def rectify(e, si, half, planes):
+            rectified[e, si, half] = planes
+            nc.gpsimd.tensor_scalar(planes, a_t[e, si][:, :, half * HALF : (half + 1) * HALF], F32_MAX, 0.0, ALU.min, ALU.max)
 
         def first_product(e, si, q, sn, bank=None):
             if sn == 0:
@@ -185,10 +184,10 @@ def tile_moe_bdx_mlp_relu2_kernel(
         def derive(e, si, q):
             c0 = max(first for first, n in PIECES[e] if first <= q * P)
             at = (q * P - c0) * PACK
-            if e == 0 and q >= Q // 2:
+            if (e, si, q // 2) in rectified:
                 nc.vector.tensor_tensor(
                     da_woven[e, c0][:, si, at : at + PASS].rearrange("p (c v t) -> p c t v", v=2, t=PACK),
-                    rectified[e][:, si, :, q * P - HALF : (q + 1) * P - HALF].rearrange("p t (c v) -> p c t v", v=2),
+                    rectified[e, si, q // 2][:, :, q % 2 * P : (q % 2 + 1) * P].rearrange("p t (c v) -> p c t v", v=2),
                     dh_bank[e, si, q][:].rearrange("p t (c v) -> p c t v", v=2),
                     ALU.mult,
                 )
@@ -274,7 +273,9 @@ def tile_moe_bdx_mlp_relu2_kernel(
         for sn in range(SN):
             permute_words(1, sn)
 
-        rectify(0)
+        upper = tile([P, SI, PACK, HALF], F32, "g10")
+        for si in range(SI):
+            rectify(0, si, 1, upper[:, si])
 
         for x, (si, q) in enumerate(order):
             first_product(0, si, q, 1)
@@ -286,45 +287,46 @@ def tile_moe_bdx_mlp_relu2_kernel(
                 dx = both_rows(0, 0, 256, 0, "w2raw1")
                 for k in (1, 0):
                     scatter_on_scalar(dx[:, k, :], 0, 0, 256, k)
-            if x == 5:
                 g_codes[1, 0] = heir([P, C], U32, "gc10", 0)
+                g_woven[1, 1] = heir([P, C * PACK], BF16, "gw11", 4 * C)
+                weave_gating(1, 1, 0, HALF)
                 quantize_g(1, 0)
-        g_woven[1, 1] = heir([P, C * PACK], BF16, "gw11", 4 * C)
-        weave_gating(1, 1, 0, HALF)
+                weave_gating(1, 1, HALF, C)
+                for half in range(2):
+                    quantize_g(1, 1, half * HALF, (half + 1) * HALF)
+                rectify(1, 0, 0, heir([P, PACK, HALF], F32, "lower", 4 * C)[:])
+                for y, bank in enumerate((1, 2, 3, 4, 0)):
+                    first_product(1, *order[y], 0, bank)
         quantize_da(0, 256)
-        dx = both_rows(0, 256, 256, 1, "dx01")
+        dx = both_rows(0, 256, 256, 5, "dx01")
         for k in (1, 0):
             scatter_on_scalar(dx[:, k, :], 0, 256, 256, k)
-        quantize_g(1, 1, 0, HALF)
-        weave_gating(1, 1, HALF, C)
-        quantize_g(1, 1, HALF, C)
-        order = [(si, q) for q in range(Q) for si in range(SI)]
-        for x, (si, q) in enumerate(order[:7]):
-            first_product(1, si, q, 0, (x + 2) % 8)
+        da_woven[1, 0] = tile([P, SI, HALF * PACK], BF16, "g10")
+        upper = tile([P, SI, PACK, HALF], F32, "daw0256")
+        for si in range(SI):
+            rectify(1, si, 1, upper[:, si])
+        order = order[:4] + [(si, q) for q in (2, 3) for si in range(SI)]
+        for y, bank in ((5, 6), (6, 7)):
+            first_product(1, *order[y], 0, bank)
 
         for x, (si, q) in enumerate(order):
             first_product(1, si, q, 1)
             derive(1, si, q)
             if x == 0:
-                first_product(1, *order[7], 0, 2)
-            if x == 2:
-                quantize_da(1, 0)
-                dx = both_rows(1, 0, P, 3, "dx10")
-                for k in (1, 0):
-                    scatter_on_scalar(dx[:, k, :], 1, 0, P, k)
+                first_product(1, *order[7], 0, 1)
             if x == 4:
-                quantize_da(1, P)
-                second = back_on_both(1, P, P, (4, 5))
+                quantize_da(1, 0)
+                second = back_on_both(1, 0, HALF, (2, 3))
             if x == 6:
                 quantize_da(1, 256)
-                third = back_on_both(1, 256, 128, (6, 7))
-        dx = tile([P, 3 * P], F32, "a10")
-        drain_on_vector(dx[:, 0:P], second)
-        drain_on_vector(dx[:, P : 2 * P], third)
+                third = back_on_both(1, 256, 128, (4, 0))
+        dx = tile([P, C], F32, "g10")
+        drain_on_vector(dx[:, 0:HALF], second)
         quantize_da(1, 384)
-        last = back_on_both(1, 384, 128, (0, 1))
-        scatter_on_vector(dx[:, 0 : 2 * P], 1, P, 2 * P, 1)
-        drain_on_vector(dx[:, 2 * P : 3 * P], last)
-        scatter_on_vector(dx[:, 2 * P : 3 * P], 1, 3 * P, P, 1)
+        last = back_on_both(1, 384, 128, (6, 7))
+        scatter_on_vector(dx[:, 0:HALF], 1, 0, HALF, 1)
+        drain_on_vector(dx[:, HALF : 3 * P], third)
+        drain_on_vector(dx[:, 3 * P : C], last)
+        scatter_on_vector(dx[:, HALF:C], 1, HALF, HALF, 1)
         for k in range(KT):
             nc.sync.dma_start(out[k * P : (k + 1) * P, :], windows[k][:])

@@ -49,7 +49,7 @@ def tile_moe_bdx_mlp_relu2_kernel(
         dy_t = [[tile([P, T], F32, f"dy{sn}{t}") for t in range(PACK)] for sn in range(SN)]
         gate_t = [tile([P, C], F32, f"gate{e}") for e in range(E)]
         a_t = {x: tile([P, PACK, C], F32, f"a{x[0]}{x[1]}") for x in groups}
-        w2_raw = [tile([P, SN, 2 * H], U8, f"w2raw{e}") for e in range(E)]
+        w2_raw = {x: tile([P, 2 * H], U8, f"w2raw{x[0]}{x[1]}") for x in groups}
         w2s_raw = tile([P, SN, H], U8, "w2sraw")
         w2_t = {x: tile([P, 2 * H], U8, f"w2{x[0]}{x[1]}") for x in groups}
         w2s_t = [tile([P, SN, H], U8, f"w2s{e}") for e in range(E)]
@@ -58,8 +58,8 @@ def tile_moe_bdx_mlp_relu2_kernel(
 
         dy_v = dyT.rearrange("(s p t) c -> s t p c", p=P, t=PACK)
         a_v = a.rearrange("(s p t) (e c) -> e s p t c", p=P, t=PACK, e=E)
-        w2_v = w2_words.bitcast(I32).rearrange("e s p b -> e p s b")
-        w2s_v = w2_scales.bitcast(I32).rearrange("e s (x r) i -> e r x s i", r=ROWS)
+        w2_v = w2_words.bitcast(I32)
+        w2s_v = w2_scales.bitcast(I32).rearrange("e s (x r) i -> s x e r i", r=ROWS)
         w1_v = w1_words.bitcast(I32).rearrange("e s p b -> p (e s) b")
         w1s_v = w1_scales.bitcast(I32).rearrange("e s (x r) i -> r x (e s) i", r=ROWS)
 
@@ -74,9 +74,13 @@ def tile_moe_bdx_mlp_relu2_kernel(
         def load_a(e, si):
             nc.sync.dma_start(a_t[e, si][:], a_v[e, si])
 
-        def load_scales(e):
-            for row in range(ROWS):
-                nc.sync.dma_start(w2s_raw[ROWS * e + row : P : 32, :, :].bitcast(I32), w2s_v[e, row])
+        def load_w2(e):
+            for sn in range(SN):
+                nc.sync.dma_start(w2_raw[e, sn][:].bitcast(I32), w2_v[e, sn])
+
+        def load_scales(sn):
+            for x in (0, 2, 1, 3):
+                nc.sync.dma_start(w2s_raw[32 * x : 32 * x + E * ROWS, sn, :].bitcast(I32), w2s_v[sn, x])
 
         load_dy(0, 0)
         nc.sync.dma_start(gate_t[1][:], gate[0:P, C : 2 * C])
@@ -89,13 +93,13 @@ def tile_moe_bdx_mlp_relu2_kernel(
         nc.sync.dma_start(gate_t[0][:], gate[0:P, 0:C])
         for t in range(1, PACK):
             load_dy(1, t)
-        nc.sync.dma_start(w2_raw[0][:].bitcast(I32), w2_v[0])
+        load_w2(0)
         load_a(0, 0)
         load_a(0, 1)
         for row in range(ROWS):
             nc.sync.dma_start(w1s_t[row:P:32, :, :].bitcast(I32), w1s_v[row])
         nc.sync.dma_start(w1_t[:].bitcast(I32), w1_v)
-        nc.sync.dma_start(w2_raw[1][:].bitcast(I32), w2_v[1])
+        load_w2(1)
         load_a(1, 0)
         load_a(1, 1)
 
@@ -123,8 +127,8 @@ def tile_moe_bdx_mlp_relu2_kernel(
         def gather_on_scalar(e, sn, t, c0=0, n=C):
             nc.scalar.activation(g[e, sn][:, t, c0 : c0 + n], dy_t[sn][t][:].indirect(slots(c0, n, e)), COPY)
 
-        def gather_on_vector(e, sn, t):
-            nc.vector.tensor_copy(g[e, sn][:, t, :], dy_t[sn][t][:].indirect(slots(0, C, e)))
+        def gather_on_vector(e, sn, t, c0, n):
+            nc.vector.tensor_copy(g[e, sn][:, t, c0 : c0 + n], dy_t[sn][t][:].indirect(slots(c0, n, e)))
 
         def gather_gated(e, sn, t):
             nc.vector.tensor_tensor(g[e, sn][:, t, :], dy_t[sn][t][:].indirect(slots(0, C, e)), gate_t[e][:], ALU.mult)
@@ -151,7 +155,7 @@ def tile_moe_bdx_mlp_relu2_kernel(
         def permute_words(e, sn):
             nc.scalar.copy(
                 out=w2_t[e, sn][:].bitcast(U16).rearrange("p (s t m) -> p s t m", s=SI, t=PACK),
-                in_=w2_raw[e][:, sn, :].bitcast(U16).rearrange("p (s m t) -> p s t m", s=SI, t=PACK),
+                in_=w2_raw[e, sn][:].bitcast(U16).rearrange("p (s m t) -> p s t m", s=SI, t=PACK),
             )
 
         def permute_scales():
@@ -255,7 +259,8 @@ def tile_moe_bdx_mlp_relu2_kernel(
         quantize_g(0, 0)
         for t in range(PACK - 1):
             gather_on_scalar(0, 1, t)
-        gather_on_vector(0, 1, PACK - 1)
+        gather_on_vector(0, 1, PACK - 1, 0, HALF)
+        gather_on_scalar(0, 1, PACK - 1, HALF, HALF)
         for half in range(2):
             weave_gating(0, 1, half * HALF, (half + 1) * HALF)
         for half in range(2):
@@ -267,7 +272,7 @@ def tile_moe_bdx_mlp_relu2_kernel(
         order = [(si, 2 * pair + ql) for pair in range(2) for si in range(SI) for ql in range(2)]
         for x, (si, q) in enumerate(order[:3]):
             first_product(0, si, q, 0, x)
-        g[1, 1] = tile([P, PACK, C], F32, "w2raw0")[:]
+        g[1, 1] = tile([P, PACK, C], F32, "w2raw00")[:]
         for t in range(PACK):
             gather_on_scalar(1, 1, t)
         for sn in range(SN):
@@ -284,7 +289,7 @@ def tile_moe_bdx_mlp_relu2_kernel(
             derive(0, si, q)
             if x == 4:
                 quantize_da(0, 0)
-                dx = both_rows(0, 0, 256, 0, "w2raw1")
+                dx = both_rows(0, 0, 256, 0, "w2raw10")
                 for k in (1, 0):
                     scatter_on_scalar(dx[:, k, :], 0, 0, 256, k)
                 g_codes[1, 0] = heir([P, C], U32, "gc10", 0)
@@ -318,15 +323,20 @@ def tile_moe_bdx_mlp_relu2_kernel(
                 quantize_da(1, 0)
                 second = back_on_both(1, 0, HALF, (2, 3))
             if x == 6:
-                quantize_da(1, 256)
-                third = back_on_both(1, 256, 128, (4, 0))
+                last = [bank_tile([P, HALF], bank) for bank in (4, 0)]
+                quantize_da(1, HALF)
+                for k in range(KT):
+                    second_product(1, HALF, P, k, last[k][:, 0:P])
         dx = tile([P, C], F32, "g10")
         drain_on_vector(dx[:, 0:HALF], second)
-        quantize_da(1, 384)
-        last = back_on_both(1, 384, 128, (6, 7))
+        quantize_da(1, 3 * P)
+        for k in range(KT):
+            second_product(1, 3 * P, P, k, last[k][:, P:HALF])
         scatter_on_vector(dx[:, 0:HALF], 1, 0, HALF, 1)
-        drain_on_vector(dx[:, HALF : 3 * P], third)
-        drain_on_vector(dx[:, 3 * P : C], last)
+        dx_0 = tile([P, HALF], F32, "dx_last")
+        nc.scalar.activation(dx_0[:], last[0][:], COPY, scale=2.0)
+        scatter_on_scalar(dx_0[:], 1, HALF, HALF, 0)
+        drain_on_vector(dx[:, HALF:C], last[1])
         scatter_on_vector(dx[:, HALF:C], 1, HALF, HALF, 1)
         for k in range(KT):
             nc.sync.dma_start(out[k * P : (k + 1) * P, :], windows[k][:])

@@ -1,6 +1,7 @@
 from contextlib import ExitStack
 
 import concourse.mybir as mybir
+from concourse.masks import make_identity
 
 K, T, E, C, H, N = 256, 1024, 2, 512, 1024, 1024
 P = 128
@@ -30,8 +31,8 @@ def tile_moe_bdx_mlp_relu2_kernel(
     STRIPE = 16
     ROWS = 4
     ALIGN = 64
-    PIECES = (((0, 256), (256, 256)), ((0, 256), (256, 128), (384, 128)))
     HALF = C // 2
+    KB = 1024
 
     with ExitStack() as ctx:
         held = ctx.enter_context(tc.tile_pool(name="held", bufs=1))
@@ -44,82 +45,94 @@ def tile_moe_bdx_mlp_relu2_kernel(
         def heir(shape, dtype, name, offset):
             return heirs.tile(shape, dtype, name=name, offset=offset, align_bytes=ALIGN)
 
+        def bank_tile(shape, bank):
+            return psum.tile(shape, F32, name=f"bank{bank}")
+
         groups = [(e, s) for e in range(E) for s in range(2)]
         offsets = held.tile([P, E * C // STRIPE], U16, name="offsets")
         dy_t = [[tile([P, T], F32, f"dy{sn}{t}") for t in range(PACK)] for sn in range(SN)]
-        gate_t = [tile([P, C], F32, f"gate{e}") for e in range(E)]
-        a_t = {x: tile([P, PACK, C], F32, f"a{x[0]}{x[1]}") for x in groups}
-        w2_raw = {x: tile([P, 2 * H], U8, f"w2raw{x[0]}{x[1]}") for x in groups}
-        w2s_raw = tile([P, SN, H], U8, "w2sraw")
-        w2_t = {x: tile([P, 2 * H], U8, f"w2{x[0]}{x[1]}") for x in groups}
-        w2s_t = [tile([P, SN, H], U8, f"w2s{e}") for e in range(E)]
+        a_t = {x: tile([P, SI, PACK, HALF], F32, f"a{x[0]}{x[1]}") for x in groups}
+        w2_raw = {x: tile([P, 2 * H], U8, f"w2raw{x[0]}{x[1]}") for x in groups if x != (0, 1)}
+        w2_raw[0, 1] = heir([P, 2 * H], U8, "w2raw01", 7 * KB)
+        w2s_raw = [heir([P, SN, H], U8, "w2sraw0", 18 * KB), tile([P, SN, H], U8, "w2sraw1")]
         w1_t = tile([P, E * SI, 2 * K], U8, "w1t")
         w1s_t = tile([P, E * SI, K], U8, "w1s")
+        gate_rows = tile([P, P], F32, "gate_rows")
+        gate_cols = tile([P, E * Q], F32, "gate_cols")
+        identity = tile([P, P], F32, "identity")
+        w2_t, w2s_t = {}, {}
 
         dy_v = dyT.rearrange("(s p t) c -> s t p c", p=P, t=PACK)
-        a_v = a.rearrange("(s p t) (e c) -> e s p t c", p=P, t=PACK, e=E)
+        a_v = a.rearrange("(s p t) (e h c) -> e h s p t c", p=P, t=PACK, e=E, h=2)
         w2_v = w2_words.bitcast(I32)
-        w2s_v = w2_scales.bitcast(I32).rearrange("e s (x r) i -> s x e r i", r=ROWS)
+        w2s_v = w2_scales.bitcast(I32).rearrange("e s (x r) i -> e r x s i", r=ROWS)
         w1_v = w1_words.bitcast(I32).rearrange("e s p b -> p (e s) b")
         w1s_v = w1_scales.bitcast(I32).rearrange("e s (x r) i -> r x (e s) i", r=ROWS)
 
         nc.sync.dma_start(offsets[:], offs)
-        nc.vector.memset(w2s_raw[:].bitcast(I32), 0)
+        nc.vector.memset(gate_rows[:], 0.0)
+        for e in range(E):
+            nc.vector.memset(w2s_raw[e][:].bitcast(I32), 0)
         nc.vector.memset(w1s_t[:].bitcast(I32), 0)
-        nc.vector.memset(w2s_t[1][:].bitcast(I32), 0)
+        make_identity(nc, identity[:])
 
         def load_dy(sn, t):
             nc.sync.dma_start(dy_t[sn][t][:], dy_v[sn, t])
 
-        def load_a(e, si):
-            nc.sync.dma_start(a_t[e, si][:], a_v[e, si])
+        def load_a(e, half, si):
+            nc.sync.dma_start(a_t[e, half][:, si], a_v[e, half, si])
 
-        def load_w2(e):
-            for sn in range(SN):
-                nc.sync.dma_start(w2_raw[e, sn][:].bitcast(I32), w2_v[e, sn])
+        def load_w2(e, sn):
+            nc.sync.dma_start(w2_raw[e, sn][:].bitcast(I32), w2_v[e, sn])
 
-        def load_scales(sn):
-            for x in (0, 2, 1, 3):
-                nc.sync.dma_start(w2s_raw[32 * x : 32 * x + E * ROWS, sn, :].bitcast(I32), w2s_v[sn, x])
+        def load_scales(e):
+            for row in range(ROWS):
+                nc.sync.dma_start(w2s_raw[e][row:P:32, :, :].bitcast(I32), w2s_v[e, row])
 
         load_dy(0, 0)
-        nc.sync.dma_start(gate_t[1][:], gate[0:P, C : 2 * C])
-        load_dy(0, 1)
-        load_dy(0, 2)
-        load_scales(0)
-        load_dy(0, 3)
-        load_scales(1)
-        load_dy(1, 0)
-        nc.sync.dma_start(gate_t[0][:], gate[0:P, 0:C])
+        nc.sync.dma_start(gate_rows[0 : E * Q, :], gate[0].rearrange("(j n) -> j n", n=P))
         for t in range(1, PACK):
+            load_dy(0, t)
+        load_w2(0, 0)
+        load_scales(0)
+        for t in range(PACK - 1):
             load_dy(1, t)
-        load_w2(0)
-        load_a(0, 0)
-        load_a(0, 1)
+        load_dy(1, PACK - 1)
+        load_w2(0, 1)
+        load_w2(1, 0)
+        load_a(0, 0, 0)
+        load_scales(1)
+        load_a(0, 0, 1)
         for row in range(ROWS):
             nc.sync.dma_start(w1s_t[row:P:32, :, :].bitcast(I32), w1s_v[row])
         nc.sync.dma_start(w1_t[:].bitcast(I32), w1_v)
-        load_w2(1)
-        load_a(1, 0)
-        load_a(1, 1)
+        load_w2(1, 1)
+        for e, half in groups[1:]:
+            for si in range(SI):
+                load_a(e, half, si)
 
-        g = {x: tile([P, PACK, C], F32, f"g{x[0]}{x[1]}")[:] for x in groups if x != (1, 1)}
-        g_woven = {(0, 0): tile([P, C * PACK], BF16, "gw00"), (0, 1): tile([P, C * PACK], BF16, "gw01")}
-        g_codes = {x: tile([P, C], U32, f"gc{x[0]}{x[1]}") for x in groups if x != (1, 0)}
-        g_scales = {x: tile([P, C], U8, f"gs{x[0]}{x[1]}") for x in groups}
-        da_woven, da_codes, da_scales = {}, {}, {}
+        turned = bank_tile([P, P], 0)
+        nc.tensor.transpose(turned[:], gate_rows[:], identity[:])
+        nc.vector.tensor_copy(gate_cols[:], turned[:, 0 : E * Q])
+        gate_t = [bank_tile([P, C], 6 + e) for e in range(E)]
         for e in range(E):
-            for c0, n in PIECES[e]:
-                if c0 != 0:
-                    da_woven[e, c0] = tile([P, SI, n * PACK], BF16, f"daw{e}{c0}")
-                da_codes[e, c0] = tile([P, SI, n], U32, f"dc{e}{c0}")
-                da_scales[e, c0] = tile([P, SI, n], U8, f"ds{e}{c0}")
-        da_woven[0, 0] = heir([P, SI, HALF * PACK], BF16, "daw_first", 0)
+            for q in range(Q):
+                j = e * Q + q
+                nc.tensor.transpose(gate_t[e][:, q * P : (q + 1) * P], gate_cols[:, j : j + 1].to_broadcast([P, P]), identity[:])
+
+        g = {x: tile([P, PACK, C], F32, f"g{x[0]}{x[1]}") for x in groups if x != (1, 1)}
+        g_woven = {(0, sn): tile([P, C * PACK], BF16, f"gw0{sn}") for sn in range(SN)}
+        g_codes = {x: tile([P, C], U32, f"gc{x[0]}{x[1]}") for x in groups if x[0] == 0}
+        g_scales = {x: tile([P, C], U8, f"gs{x[0]}{x[1]}") for x in groups}
+        piece = {(e, q): (q, 1) for e in range(E) for q in range(Q)}
+        firsts = [(e, q) for e in range(E) for q in range(Q) if piece[e, q][0] == q]
+        da_woven = {x: tile([P, SI, PASS], BF16, f"daw{x[0]}{x[1]}") for x in firsts if x[0] == 1 or x[1] == 3}
+        for q, at in enumerate((22, 13, 26)):
+            da_woven[0, q] = heir([P, SI, PASS], BF16, f"daw0{q}", at * KB)
+        da_codes = {x: tile([P, SI, P], U32, f"dc{x[0]}{x[1]}") for x in firsts if x != (0, 0)}
+        da_scales = {x: tile([P, SI, P], U8, f"ds{x[0]}{x[1]}") for x in firsts}
         windows = [tile([P, T], F32, f"window{k}") for k in range(KT)]
         dh_bank, rectified = {}, {}
-
-        def bank_tile(shape, bank):
-            return psum.tile(shape, F32, name=f"bank{bank}")
 
         def slots(c0, n, e):
             return offsets[:, (e * C + c0) // STRIPE : (e * C + c0 + n) // STRIPE]
@@ -127,13 +140,10 @@ def tile_moe_bdx_mlp_relu2_kernel(
         def gather_on_scalar(e, sn, t, c0=0, n=C):
             nc.scalar.activation(g[e, sn][:, t, c0 : c0 + n], dy_t[sn][t][:].indirect(slots(c0, n, e)), COPY)
 
-        def gather_on_vector(e, sn, t, c0, n):
+        def gather_on_vector(e, sn, t, c0=0, n=C):
             nc.vector.tensor_copy(g[e, sn][:, t, c0 : c0 + n], dy_t[sn][t][:].indirect(slots(c0, n, e)))
 
-        def gather_gated(e, sn, t):
-            nc.vector.tensor_tensor(g[e, sn][:, t, :], dy_t[sn][t][:].indirect(slots(0, C, e)), gate_t[e][:], ALU.mult)
-
-        def weave_gating(e, sn, c0=0, c1=C):
+        def weave(e, sn, c0=0, c1=C):
             nc.vector.tensor_tensor(
                 g_woven[e, sn][:, PACK * c0 : PACK * c1].rearrange("p (c v t) -> p c t v", v=2, t=PACK),
                 g[e, sn][:, :, c0:c1].rearrange("p t (c v) -> p c t v", v=2),
@@ -141,34 +151,32 @@ def tile_moe_bdx_mlp_relu2_kernel(
                 ALU.mult,
             )
 
-        def weave(e, sn):
-            nc.vector.tensor_copy(
-                g_woven[e, sn][:].rearrange("p (c v t) -> p c t v", v=4, t=PACK),
-                g[e, sn].rearrange("p t (c v) -> p c t v", v=4),
-            )
-
         def quantize_g(e, sn, c0=0, c1=C):
             nc.vector.quantize_mx(
                 out=g_codes[e, sn][:, c0:c1].bitcast(E5M2), scales=g_scales[e, sn][:, c0:c1], in_=g_woven[e, sn][:, PACK * c0 : PACK * c1]
             )
 
-        def permute_words(e, sn):
-            nc.scalar.copy(
-                out=w2_t[e, sn][:].bitcast(U16).rearrange("p (s t m) -> p s t m", s=SI, t=PACK),
+        def permute_words(move, e, sn, words):
+            w2_t[e, sn] = words
+            move(
+                out=words[:].bitcast(U16).rearrange("p (s t m) -> p s t m", s=SI, t=PACK),
                 in_=w2_raw[e, sn][:].bitcast(U16).rearrange("p (s m t) -> p s t m", s=SI, t=PACK),
             )
 
-        def permute_scales():
-            nc.vector.tensor_copy(
-                w2s_t[0][:].rearrange("p n (s t m) -> p (n s) t m", s=SI, t=PACK),
-                w2s_raw[:].rearrange("p n (s m t) -> p (n s) t m", s=SI, t=PACK),
+        def permute_scales(move, e, planes):
+            w2s_t[e] = planes
+            move(
+                out=planes[:].rearrange("p n (s t m) -> p (n s) t m", s=SI, t=PACK),
+                in_=w2s_raw[e][:].rearrange("p n (s m t) -> p (n s) t m", s=SI, t=PACK),
             )
-            for row in range(ROWS):
-                nc.gpsimd.dma_start(w2s_t[1][row:P:32, :, :].bitcast(I32), w2s_t[0][ROWS + row : P : 32, :, :].bitcast(I32))
 
-        def rectify(e, si, half, planes):
-            rectified[e, si, half] = planes
-            nc.gpsimd.tensor_scalar(planes, a_t[e, si][:, :, half * HALF : (half + 1) * HALF], F32_MAX, 0.0, ALU.min, ALU.max)
+        def slope_input(e, si, q):
+            return a_t[e, q // 2][:, si, :, q % 2 * P : (q % 2 + 1) * P]
+
+        def rectify(e, passes, q, planes):
+            for x, si in enumerate(range(SI)[passes]):
+                rectified[e, si, q] = planes[:, x]
+            nc.gpsimd.tensor_scalar(planes[:], slope_input(e, passes, q), F32_MAX, 0.0, ALU.min, ALU.max)
 
         def first_product(e, si, q, sn, bank=None):
             if sn == 0:
@@ -186,40 +194,40 @@ def tile_moe_bdx_mlp_relu2_kernel(
                 )
 
         def derive(e, si, q):
-            c0 = max(first for first, n in PIECES[e] if first <= q * P)
-            at = (q * P - c0) * PACK
-            if (e, si, q // 2) in rectified:
+            first = piece[e, q][0]
+            woven = da_woven[e, first][:, si, (q - first) * PASS : (q - first + 1) * PASS]
+            if (e, si, q) in rectified:
                 nc.vector.tensor_tensor(
-                    da_woven[e, c0][:, si, at : at + PASS].rearrange("p (c v t) -> p c t v", v=2, t=PACK),
-                    rectified[e, si, q // 2][:, :, q % 2 * P : (q % 2 + 1) * P].rearrange("p t (c v) -> p c t v", v=2),
+                    woven.rearrange("p (c v t) -> p c t v", v=2, t=PACK),
+                    rectified[e, si, q].rearrange("p t (c v) -> p c t v", v=2),
                     dh_bank[e, si, q][:].rearrange("p t (c v) -> p c t v", v=2),
                     ALU.mult,
                 )
                 return
             nc.vector.scalar_tensor_tensor(
-                da_woven[e, c0][:, si, at : at + PASS].rearrange("p (c t) -> p c t", t=PACK),
-                a_t[e, si][:, :, q * P : (q + 1) * P].rearrange("p t c -> p c t"),
+                woven.rearrange("p (c t) -> p c t", t=PACK),
+                slope_input(e, si, q).rearrange("p t c -> p c t"),
                 0.0,
                 dh_bank[e, si, q][:].rearrange("p t c -> p c t"),
                 ALU.max,
                 ALU.mult,
             )
 
-        def quantize_da(e, c0):
+        def quantize_da(e, q):
             nc.vector.quantize_mx(
-                out=da_codes[e, c0][:].rearrange("p s c -> p (s c)").bitcast(E5M2),
-                scales=da_scales[e, c0][:].rearrange("p s c -> p (s c)"),
-                in_=da_woven[e, c0][:].rearrange("p s c -> p (s c)"),
+                out=da_codes[e, q][:].rearrange("p s c -> p (s c)").bitcast(E5M2),
+                scales=da_scales[e, q][:].rearrange("p s c -> p (s c)"),
+                in_=da_woven[e, q][:].rearrange("p s c -> p (s c)"),
             )
 
-        def second_product(e, c0, n, k, dx_bank):
+        def second_product(e, q, k, dx_bank):
             for si in range(SI):
                 nc.tensor.matmul_mx(
                     out=dx_bank,
                     lhsT=w1_t[:, e * SI + si, 2 * k * P : 2 * (k + 1) * P].bitcast(E2M1),
                     lhsT_scale=w1s_t[:, e * SI + si, k * P : (k + 1) * P],
-                    rhs=da_codes[e, c0][:, si, :].bitcast(E5M2),
-                    rhs_scale=da_scales[e, c0][:, si, :],
+                    rhs=da_codes[e, q][:, si, :].bitcast(E5M2),
+                    rhs_scale=da_scales[e, q][:, si, :],
                     start=(si == 0),
                     stop=(si == SI - 1),
                 )
@@ -230,113 +238,122 @@ def tile_moe_bdx_mlp_relu2_kernel(
         def scatter_on_vector(dx, e, c0, n, k):
             nc.vector.tensor_copy(windows[k][:].indirect(slots(c0, n, e)), dx)
 
-        def both_rows(e, c0, n, bank, name):
-            dx_bank = bank_tile([P, KT, n], bank)
-            for k in range(KT):
-                second_product(e, c0, n, k, dx_bank[:, k, :])
+        def back_on_scalar(e, q, n, dx_bank, name):
             dx = tile([P, KT, n], F32, name)
             for k in (1, 0):
                 nc.scalar.activation(dx[:, k, :], dx_bank[:, k, :], COPY, scale=2.0)
-            return dx
+            for k in (1, 0):
+                scatter_on_scalar(dx[:, k, :], e, q * P, n, k)
 
-        def back_on_both(e, c0, n, banks):
-            dx_banks = [bank_tile([P, n], bank) for bank in banks]
+        def piece_on_scalar(e, q, bank, name):
+            dx_bank = bank_tile([P, KT, P], bank)
             for k in range(KT):
-                second_product(e, c0, n, k, dx_banks[k][:])
-            dx = tile([P, n], F32, f"dx{e}{c0}0")
-            nc.scalar.activation(dx[:], dx_banks[0][:], COPY, scale=2.0)
-            scatter_on_scalar(dx[:], e, c0, n, 0)
-            return dx_banks[1]
+                second_product(e, q, k, dx_bank[:, k, :])
+            back_on_scalar(e, q, P, dx_bank, name)
 
-        def drain_on_vector(dx, dx_bank):
-            nc.vector.tensor_scalar(dx, dx_bank[:], 2.0, None, ALU.mult)
-
-        for t in range(PACK):
+        for t in range(PACK - 1):
             gather_on_scalar(0, 0, t)
-            gather_gated(1, 0, t)
-        permute_scales()
-        weave_gating(0, 0)
-        quantize_g(0, 0)
+            gather_on_vector(1, 0, t)
+        gather_on_vector(0, 0, PACK - 1)
+        gather_on_scalar(1, 0, PACK - 1)
+        permute_words(nc.gpsimd.tensor_copy, 0, 0, tile([P, 2 * H], U8, "w200"))
+        for half in range(2):
+            weave(0, 0, half * HALF, (half + 1) * HALF)
+        quantize_g(0, 0, 0, HALF)
+        permute_scales(nc.vector.tensor_copy, 0, tile([P, SN, H], U8, "g00"))
+        quantize_g(0, 0, HALF, C)
+        g_woven[1, 0] = heir([P, C * PACK], BF16, "gw10", 18 * KB)
+        weave(1, 0)
+        order = [(si, q) for q in range(Q) for si in range(SI)]
+        for x, (si, q) in enumerate(order[:6]):
+            first_product(0, si, q, 0, x)
+        permute_words(nc.gpsimd.tensor_copy, 0, 1, tile([P, 2 * H], U8, "w201"))
+        permute_words(nc.gpsimd.tensor_copy, 1, 0, tile([P, 2 * H], U8, "w210"))
         for t in range(PACK - 1):
             gather_on_scalar(0, 1, t)
-        gather_on_vector(0, 1, PACK - 1, 0, HALF)
-        gather_on_scalar(0, 1, PACK - 1, HALF, HALF)
         for half in range(2):
-            weave_gating(0, 1, half * HALF, (half + 1) * HALF)
+            gather_on_scalar(0, 1, PACK - 1, half * HALF, HALF)
+        for half in range(2):
+            weave(0, 1, half * HALF, (half + 1) * HALF)
         for half in range(2):
             quantize_g(0, 1, half * HALF, (half + 1) * HALF)
-        g_woven[1, 0] = tile([P, C * PACK], BF16, "g01")
-        weave(1, 0)
-        for sn in range(SN):
-            permute_words(0, sn)
-        order = [(si, 2 * pair + ql) for pair in range(2) for si in range(SI) for ql in range(2)]
-        for x, (si, q) in enumerate(order[:3]):
-            first_product(0, si, q, 0, x)
-        g[1, 1] = tile([P, PACK, C], F32, "w2raw00")[:]
+        g_codes[1, 0] = tile([P, C], U32, "g01")
+        quantize_g(1, 0)
+        g[1, 1] = heir([P, PACK, C], F32, "g11", 0)
         for t in range(PACK):
             gather_on_scalar(1, 1, t)
-        for sn in range(SN):
-            permute_words(1, sn)
+        permute_words(nc.scalar.copy, 1, 1, tile([P, 2 * H], U8, "w211"))
+        permute_scales(nc.gpsimd.tensor_copy, 1, heir([P, SN, H], U8, "w2s1", 20 * KB))
+        both = slice(0, SI)
 
-        upper = tile([P, SI, PACK, HALF], F32, "g10")
-        for si in range(SI):
-            rectify(0, si, 1, upper[:, si])
-
-        for x, (si, q) in enumerate(order):
+        for si, q in order[:6]:
             first_product(0, si, q, 1)
-            if x < 5:
-                first_product(0, *order[x + 3], 0, x + 3)
+        for x, (si, q) in enumerate(order[:4]):
             derive(0, si, q)
-            if x == 4:
-                quantize_da(0, 0)
-                dx = both_rows(0, 0, 256, 0, "w2raw10")
-                for k in (1, 0):
-                    scatter_on_scalar(dx[:, k, :], 0, 0, 256, k)
-                g_codes[1, 0] = heir([P, C], U32, "gc10", 0)
-                g_woven[1, 1] = heir([P, C * PACK], BF16, "gw11", 4 * C)
-                weave_gating(1, 1, 0, HALF)
-                quantize_g(1, 0)
-                weave_gating(1, 1, HALF, C)
-                for half in range(2):
-                    quantize_g(1, 1, half * HALF, (half + 1) * HALF)
-                rectify(1, 0, 0, heir([P, PACK, HALF], F32, "lower", 4 * C)[:])
-                for y, bank in enumerate((1, 2, 3, 4, 0)):
-                    first_product(1, *order[y], 0, bank)
-        quantize_da(0, 256)
-        dx = both_rows(0, 256, 256, 5, "dx01")
-        for k in (1, 0):
-            scatter_on_scalar(dx[:, k, :], 0, 256, 256, k)
-        da_woven[1, 0] = tile([P, SI, HALF * PACK], BF16, "g10")
-        upper = tile([P, SI, PACK, HALF], F32, "daw0256")
-        for si in range(SI):
-            rectify(1, si, 1, upper[:, si])
-        order = order[:4] + [(si, q) for q in (2, 3) for si in range(SI)]
-        for y, bank in ((5, 6), (6, 7)):
+            if x < 2:
+                for sn in range(SN):
+                    first_product(0, *order[6 + x], sn, x)
+        da_codes[0, 0] = tile([P, SI, P], U32, "w2sraw1")
+        dx_bank = bank_tile([P, KT, HALF], 6)
+        for q in range(2):
+            quantize_da(0, q)
+            for k in range(KT):
+                second_product(0, q, k, dx_bank[:, k, q * P : (q + 1) * P])
+        back_on_scalar(0, 0, HALF, dx_bank, "w2raw11")
+        for q in (2, 3):
+            rectify(0, both, q, heir([P, SI, PACK, P], F32, f"upper0{q}", (2 + 4 * q) * KB))
+        for y, bank in ((0, 2), (1, 3)):
             first_product(1, *order[y], 0, bank)
+        g_woven[1, 1] = heir([P, C * PACK], BF16, "gw11", 22 * KB)
+        for half in range(2):
+            weave(1, 1, half * HALF, (half + 1) * HALF)
+        first_product(1, *order[4], 0, 7)
+        for x in (4, 5):
+            derive(0, *order[x])
+            first_product(1, *order[x - 2], 0, x)
+        g_codes[1, 1] = tile([P, C], U32, "a01")
+        for half in range(2):
+            quantize_g(1, 1, half * HALF, (half + 1) * HALF)
+        quantize_da(0, 2)
+        first_product(1, *order[0], 1)
+        piece_on_scalar(0, 2, 6, "dx02")
+        for si, q in order[1:5]:
+            first_product(1, si, q, 1)
+        rectify(1, both, 1, heir([P, SI, PACK, P], F32, "lower", 24 * KB))
+        for x in (6, 7):
+            derive(0, *order[x])
 
         for x, (si, q) in enumerate(order):
-            first_product(1, si, q, 1)
             derive(1, si, q)
             if x == 0:
-                first_product(1, *order[7], 0, 1)
-            if x == 4:
+                quantize_da(0, 3)
+                piece_on_scalar(0, 3, 6, "dx03")
+                rectify(1, slice(0, 1), 2, tile([P, 1, PACK, P], F32, "daw03"))
+                for y in (5, 6, 7):
+                    for sn in range(SN):
+                        first_product(1, *order[y], sn, y - 5)
+            if x == 2:
                 quantize_da(1, 0)
-                second = back_on_both(1, 0, HALF, (2, 3))
-            if x == 6:
-                last = [bank_tile([P, HALF], bank) for bank in (4, 0)]
-                quantize_da(1, HALF)
+                piece_on_scalar(1, 0, 3, "dx10")
+            if x in (4, 6):
+                q = x // 2 - 1
+                if q == 1:
+                    middle = [bank_tile([P, HALF], bank) for bank in (4, 5)]
+                quantize_da(1, q)
                 for k in range(KT):
-                    second_product(1, HALF, P, k, last[k][:, 0:P])
-        dx = tile([P, C], F32, "g10")
-        drain_on_vector(dx[:, 0:HALF], second)
-        quantize_da(1, 3 * P)
+                    second_product(1, q, k, middle[k][:, (q - 1) * P : q * P])
+            if x in (2, 4):
+                rectify(1, slice(1, 2), x // 2 + 1, tile([P, 1, PACK, P], F32, f"daw1{x // 2 - 1}"))
+        quantize_da(1, 3)
+        last = [bank_tile([P, P], bank) for bank in (7, 0)]
         for k in range(KT):
-            second_product(1, 3 * P, P, k, last[k][:, P:HALF])
-        scatter_on_vector(dx[:, 0:HALF], 1, 0, HALF, 1)
-        dx_0 = tile([P, HALF], F32, "dx_last")
-        nc.scalar.activation(dx_0[:], last[0][:], COPY, scale=2.0)
-        scatter_on_scalar(dx_0[:], 1, HALF, HALF, 0)
-        drain_on_vector(dx[:, HALF:C], last[1])
-        scatter_on_vector(dx[:, HALF:C], 1, HALF, HALF, 1)
-        for k in range(KT):
+            second_product(1, 3, k, last[k][:])
+        dx = [tile([P, 3 * P], F32, name) for name in ("dx_last", "daw11")]
+        for banks, c0, n in ((middle, P, HALF), (last, 3 * P, P)):
+            part = [dx[k][:, c0 - P : c0 - P + n] for k in range(KT)]
+            nc.scalar.activation(part[0], banks[0][:], COPY, scale=2.0)
+            scatter_on_scalar(part[0], 1, c0, n, 0)
+            nc.vector.tensor_scalar(part[1], banks[1][:], 2.0, None, ALU.mult)
+            scatter_on_vector(part[1], 1, c0, n, 1)
+        for k in (1, 0):
             nc.sync.dma_start(out[k * P : (k + 1) * P, :], windows[k][:])

@@ -33,6 +33,15 @@ def tile_moe_bdx_mlp_relu2_kernel(
     ALIGN = 64
     HALF = C // 2
     KB = 1024
+    PLACES = {
+        "gw10": 0, "w2s10": 0, "g11": 2,
+        "gw010": 10, "w2s11": 10, "rect011": 11,
+        "daw00": 16, "w210": 15,
+        "daw01": 36, "gw110": 35, "rect100": 37,
+        "daw02": 24, "rect110": 21, "gw111": 25, "rect102": 27,
+        "g01first": 32, "gw011": 32,
+    }
+    PIECES = (((0, 1), (1, 1), (2, 2)), ((0, 1), (1, 1), (2, 1), (3, 1)))
 
     with ExitStack() as ctx:
         held = ctx.enter_context(tc.tile_pool(name="held", bufs=1))
@@ -40,10 +49,9 @@ def tile_moe_bdx_mlp_relu2_kernel(
         psum = ctx.enter_context(tc.psum_pool(name="psum", bufs=1))
 
         def tile(shape, dtype, name):
+            if name in PLACES:
+                return heirs.tile(shape, dtype, name=name, offset=PLACES[name] * KB, align_bytes=ALIGN)
             return held.tile(shape, dtype, name=name, align_bytes=ALIGN)
-
-        def heir(shape, dtype, name, offset):
-            return heirs.tile(shape, dtype, name=name, offset=offset, align_bytes=ALIGN)
 
         def bank_tile(shape, bank):
             return psum.tile(shape, F32, name=f"bank{bank}")
@@ -51,10 +59,9 @@ def tile_moe_bdx_mlp_relu2_kernel(
         groups = [(e, s) for e in range(E) for s in range(2)]
         offsets = held.tile([P, E * C // STRIPE], U16, name="offsets")
         dy_t = [[tile([P, T], F32, f"dy{sn}{t}") for t in range(PACK)] for sn in range(SN)]
-        a_t = {x: tile([P, SI, PACK, HALF], F32, f"a{x[0]}{x[1]}") for x in groups}
-        w2_raw = {x: tile([P, 2 * H], U8, f"w2raw{x[0]}{x[1]}") for x in groups if x != (0, 1)}
-        w2_raw[0, 1] = heir([P, 2 * H], U8, "w2raw01", 7 * KB)
-        w2s_raw = [heir([P, SN, H], U8, "w2sraw0", 18 * KB), tile([P, SN, H], U8, "w2sraw1")]
+        a_t = {(e, half, si): tile([P, PACK, HALF], F32, f"a{e}{half}{si}") for e, half in groups for si in range(SI)}
+        w2_raw = {x: tile([P, 2 * H], U8, f"w2raw{x[0]}{x[1]}") for x in groups}
+        w2s_raw = [tile([P, SN, H], U8, f"w2sraw{e}") for e in range(E)]
         w1_t = tile([P, E * SI, 2 * K], U8, "w1t")
         w1s_t = tile([P, E * SI, K], U8, "w1s")
         gate_rows = tile([P, P], F32, "gate_rows")
@@ -66,7 +73,7 @@ def tile_moe_bdx_mlp_relu2_kernel(
         a_v = a.rearrange("(s p t) (e h c) -> e h s p t c", p=P, t=PACK, e=E, h=2)
         w2_v = w2_words.bitcast(I32)
         w2s_v = w2_scales.bitcast(I32).rearrange("e s (x r) i -> e r x s i", r=ROWS)
-        w1_v = w1_words.bitcast(I32).rearrange("e s p b -> p (e s) b")
+        w1_v = w1_words.bitcast(I32).rearrange("e s p b -> e p s b")
         w1s_v = w1_scales.bitcast(I32).rearrange("e s (x r) i -> r x (e s) i", r=ROWS)
 
         nc.sync.dma_start(offsets[:], offs)
@@ -80,7 +87,7 @@ def tile_moe_bdx_mlp_relu2_kernel(
             nc.sync.dma_start(dy_t[sn][t][:], dy_v[sn, t])
 
         def load_a(e, half, si):
-            nc.sync.dma_start(a_t[e, half][:, si], a_v[e, half, si])
+            nc.sync.dma_start(a_t[e, half, si][:], a_v[e, half, si])
 
         def load_w2(e, sn):
             nc.sync.dma_start(w2_raw[e, sn][:].bitcast(I32), w2_v[e, sn])
@@ -89,48 +96,47 @@ def tile_moe_bdx_mlp_relu2_kernel(
             for row in range(ROWS):
                 nc.sync.dma_start(w2s_raw[e][row:P:32, :, :].bitcast(I32), w2s_v[e, row])
 
+        def load_w1(e):
+            nc.sync.dma_start(w1_t[:, e * SI : (e + 1) * SI, :].bitcast(I32), w1_v[e])
+
         load_dy(0, 0)
         nc.sync.dma_start(gate_rows[0 : E * Q, :], gate[0].rearrange("(j n) -> j n", n=P))
-        for t in range(1, PACK):
-            load_dy(0, t)
-        load_w2(0, 0)
+        load_dy(0, 1)
         load_scales(0)
-        for t in range(PACK - 1):
-            load_dy(1, t)
-        load_dy(1, PACK - 1)
+        load_dy(0, 2)
+        load_dy(0, 3)
+        load_w2(0, 0)
         load_w2(0, 1)
-        load_w2(1, 0)
-        load_a(0, 0, 0)
+        for t in range(PACK):
+            load_dy(1, t)
         load_scales(1)
+        load_a(0, 0, 0)
         load_a(0, 0, 1)
         for row in range(ROWS):
             nc.sync.dma_start(w1s_t[row:P:32, :, :].bitcast(I32), w1s_v[row])
-        nc.sync.dma_start(w1_t[:].bitcast(I32), w1_v)
+        load_w1(0)
+        load_w2(1, 0)
+        load_a(0, 1, 0)
+        load_a(0, 1, 1)
         load_w2(1, 1)
-        for e, half in groups[1:]:
-            for si in range(SI):
-                load_a(e, half, si)
+        load_a(1, 0, 0)
+        load_a(1, 0, 1)
+        load_w1(1)
+        load_a(1, 1, 0)
+        load_a(1, 1, 1)
 
-        turned = bank_tile([P, P], 0)
-        nc.tensor.transpose(turned[:], gate_rows[:], identity[:])
-        nc.vector.tensor_copy(gate_cols[:], turned[:, 0 : E * Q])
-        gate_t = [bank_tile([P, C], 6 + e) for e in range(E)]
-        for e in range(E):
-            for q in range(Q):
-                j = e * Q + q
-                nc.tensor.transpose(gate_t[e][:, q * P : (q + 1) * P], gate_cols[:, j : j + 1].to_broadcast([P, P]), identity[:])
+        g = {(e, 0): tile([P, PACK, C], F32, f"g{e}0")[:] for e in range(E)}
+        g_first, g_rest = tile([P, PACK, P], F32, "g01first"), tile([P, PACK, C - P], F32, "g01rest")
 
-        g = {x: tile([P, PACK, C], F32, f"g{x[0]}{x[1]}") for x in groups if x != (1, 1)}
-        g_woven = {(0, sn): tile([P, C * PACK], BF16, f"gw0{sn}") for sn in range(SN)}
-        g_codes = {x: tile([P, C], U32, f"gc{x[0]}{x[1]}") for x in groups if x[0] == 0}
-        g_scales = {x: tile([P, C], U8, f"gs{x[0]}{x[1]}") for x in groups}
-        piece = {(e, q): (q, 1) for e in range(E) for q in range(Q)}
-        firsts = [(e, q) for e in range(E) for q in range(Q) if piece[e, q][0] == q]
-        da_woven = {x: tile([P, SI, PASS], BF16, f"daw{x[0]}{x[1]}") for x in firsts if x[0] == 1 or x[1] == 3}
-        for q, at in enumerate((22, 13, 26)):
-            da_woven[0, q] = heir([P, SI, PASS], BF16, f"daw0{q}", at * KB)
-        da_codes = {x: tile([P, SI, P], U32, f"dc{x[0]}{x[1]}") for x in firsts if x != (0, 0)}
-        da_scales = {x: tile([P, SI, P], U8, f"ds{x[0]}{x[1]}") for x in firsts}
+        def gathered(e, sn, c0, c1):
+            if (e, sn) != (0, 1):
+                return g[e, sn][:, :, c0:c1]
+            return g_first[:] if c0 == 0 else g_rest[:, :, c0 - P : c1 - P]
+
+        g_woven = {}
+        piece = {(e, first + x): (first, n) for e in range(E) for first, n in PIECES[e] for x in range(n)}
+        g_codes, g_scales = {}, {}
+        da_woven, da_codes, da_scales = {}, {}, {}
         windows = [tile([P, T], F32, f"window{k}") for k in range(KT)]
         dh_bank, rectified = {}, {}
 
@@ -138,23 +144,31 @@ def tile_moe_bdx_mlp_relu2_kernel(
             return offsets[:, (e * C + c0) // STRIPE : (e * C + c0 + n) // STRIPE]
 
         def gather_on_scalar(e, sn, t, c0=0, n=C):
-            nc.scalar.activation(g[e, sn][:, t, c0 : c0 + n], dy_t[sn][t][:].indirect(slots(c0, n, e)), COPY)
+            nc.scalar.activation(gathered(e, sn, c0, c0 + n)[:, t, :], dy_t[sn][t][:].indirect(slots(c0, n, e)), COPY)
 
         def gather_on_vector(e, sn, t, c0=0, n=C):
-            nc.vector.tensor_copy(g[e, sn][:, t, c0 : c0 + n], dy_t[sn][t][:].indirect(slots(c0, n, e)))
+            nc.vector.tensor_copy(gathered(e, sn, c0, c0 + n)[:, t, :], dy_t[sn][t][:].indirect(slots(c0, n, e)))
 
-        def weave(e, sn, c0=0, c1=C):
+        def weave(e, sn, c0, c1, name=None, n=None):
+            if name:
+                woven = tile([P, (n or c1 - c0) * PACK], BF16, name)
+                for q in range(c0 // P, (c0 + (n or c1 - c0)) // P):
+                    g_woven[e, sn, q] = (woven, c0)
+            woven, first = g_woven[e, sn, c0 // P]
             nc.vector.tensor_tensor(
-                g_woven[e, sn][:, PACK * c0 : PACK * c1].rearrange("p (c v t) -> p c t v", v=2, t=PACK),
-                g[e, sn][:, :, c0:c1].rearrange("p t (c v) -> p c t v", v=2),
+                woven[:, PACK * (c0 - first) : PACK * (c1 - first)].rearrange("p (c v t) -> p c t v", v=2, t=PACK),
+                gathered(e, sn, c0, c1).rearrange("p t (c v) -> p c t v", v=2),
                 gate_t[e][:, c0:c1].rearrange("p (c v) -> p c v", v=2).unsqueeze(2).to_broadcast([P, (c1 - c0) // 2, PACK, 2]),
                 ALU.mult,
             )
 
-        def quantize_g(e, sn, c0=0, c1=C):
-            nc.vector.quantize_mx(
-                out=g_codes[e, sn][:, c0:c1].bitcast(E5M2), scales=g_scales[e, sn][:, c0:c1], in_=g_woven[e, sn][:, PACK * c0 : PACK * c1]
-            )
+        def quantize_g(e, sn, c0, n, name):
+            woven, first = g_woven[e, sn, c0 // P]
+            codes, scales = tile([P, n], U32, name), tile([P, n], U8, f"gs{e}{sn}{c0}")
+            for q in range(c0 // P, (c0 + n) // P):
+                g_codes[e, sn, q] = codes[:, q * P - c0 : (q + 1) * P - c0]
+                g_scales[e, sn, q] = scales[:, q * P - c0 : (q + 1) * P - c0]
+            nc.vector.quantize_mx(out=codes[:].bitcast(E5M2), scales=scales[:], in_=woven[:, PACK * (c0 - first) : PACK * (c0 + n - first)])
 
         def permute_words(move, e, sn, words):
             w2_t[e, sn] = words
@@ -163,20 +177,23 @@ def tile_moe_bdx_mlp_relu2_kernel(
                 in_=w2_raw[e, sn][:].bitcast(U16).rearrange("p (s m t) -> p s t m", s=SI, t=PACK),
             )
 
-        def permute_scales(move, e, planes):
-            w2s_t[e] = planes
-            move(
+        def permute_scales(e, first, n, name):
+            planes = tile([P, n, H], U8, name)
+            for x in range(n):
+                w2s_t[e, first + x] = planes[:, x, :]
+            nc.gpsimd.tensor_copy(
                 out=planes[:].rearrange("p n (s t m) -> p (n s) t m", s=SI, t=PACK),
-                in_=w2s_raw[e][:].rearrange("p n (s m t) -> p (n s) t m", s=SI, t=PACK),
+                in_=w2s_raw[e][:, first : first + n, :].rearrange("p n (s m t) -> p (n s) t m", s=SI, t=PACK),
             )
 
         def slope_input(e, si, q):
-            return a_t[e, q // 2][:, si, :, q % 2 * P : (q % 2 + 1) * P]
+            return a_t[e, q // 2, si][:, :, q % 2 * P : (q % 2 + 1) * P]
 
-        def rectify(e, passes, q, planes):
-            for x, si in enumerate(range(SI)[passes]):
-                rectified[e, si, q] = planes[:, x]
-            nc.gpsimd.tensor_scalar(planes[:], slope_input(e, passes, q), F32_MAX, 0.0, ALU.min, ALU.max)
+        def rectify(e, si, q, n, name):
+            planes = tile([P, PACK, n * P], F32, name)
+            for x in range(n):
+                rectified[e, si, q + x] = planes[:, :, x * P : (x + 1) * P]
+            nc.gpsimd.tensor_scalar(planes[:], a_t[e, q // 2, si][:, :, q % 2 * P : (q % 2 + n) * P], F32_MAX, 0.0, ALU.min, ALU.max)
 
         def first_product(e, si, q, sn, bank=None):
             if sn == 0:
@@ -186,15 +203,17 @@ def tile_moe_bdx_mlp_relu2_kernel(
                 nc.tensor.matmul_mx(
                     out=dh_bank[e, si, q][:, t, :],
                     lhsT=w2_t[e, sn][:, 2 * col : 2 * (col + P)].bitcast(E2M1),
-                    lhsT_scale=w2s_t[e][:, sn, col : col + P],
-                    rhs=g_codes[e, sn][:, q * P : (q + 1) * P].bitcast(E5M2),
-                    rhs_scale=g_scales[e, sn][:, q * P : (q + 1) * P],
+                    lhsT_scale=w2s_t[e, sn][:, col : col + P],
+                    rhs=g_codes[e, sn, q].bitcast(E5M2),
+                    rhs_scale=g_scales[e, sn, q],
                     start=(sn == 0 and t == 0),
                     stop=(sn == SN - 1 and t == PACK - 1),
                 )
 
-        def derive(e, si, q):
-            first = piece[e, q][0]
+        def derive(e, si, q, name=None):
+            first, n = piece[e, q]
+            if (e, first) not in da_woven:
+                da_woven[e, first] = tile([P, SI, n * PASS], BF16, name or f"daw{e}{first}")
             woven = da_woven[e, first][:, si, (q - first) * PASS : (q - first + 1) * PASS]
             if (e, si, q) in rectified:
                 nc.vector.tensor_tensor(
@@ -213,7 +232,10 @@ def tile_moe_bdx_mlp_relu2_kernel(
                 ALU.mult,
             )
 
-        def quantize_da(e, q):
+        def quantize_da(e, q, name=None):
+            n = piece[e, q][1] * P
+            da_codes[e, q] = tile([P, SI, n], U32, name or f"dc{e}{q}")[:]
+            da_scales[e, q] = tile([P, SI, n], U8, f"ds{e}{q}")
             nc.vector.quantize_mx(
                 out=da_codes[e, q][:].rearrange("p s c -> p (s c)").bitcast(E5M2),
                 scales=da_scales[e, q][:].rearrange("p s c -> p (s c)"),
@@ -238,122 +260,150 @@ def tile_moe_bdx_mlp_relu2_kernel(
         def scatter_on_vector(dx, e, c0, n, k):
             nc.vector.tensor_copy(windows[k][:].indirect(slots(c0, n, e)), dx)
 
-        def back_on_scalar(e, q, n, dx_bank, name):
+        def products(e, q, bank):
+            dx_bank = bank_tile([P, KT, da_codes[e, q].shape[2]], bank)
+            for k in range(KT):
+                second_product(e, q, k, dx_bank[:, k, :])
+            return dx_bank
+
+        def back_on_scalar(e, q, bank, name):
+            dx_bank = products(e, q, bank)
+            n = da_codes[e, q].shape[2]
             dx = tile([P, KT, n], F32, name)
             for k in (1, 0):
                 nc.scalar.activation(dx[:, k, :], dx_bank[:, k, :], COPY, scale=2.0)
             for k in (1, 0):
                 scatter_on_scalar(dx[:, k, :], e, q * P, n, k)
 
-        def piece_on_scalar(e, q, bank, name):
-            dx_bank = bank_tile([P, KT, P], bank)
-            for k in range(KT):
-                second_product(e, q, k, dx_bank[:, k, :])
-            back_on_scalar(e, q, P, dx_bank, name)
+        def both_passes(e, si, q, bank):
+            for sn in range(SN):
+                first_product(e, si, q, sn, bank)
+
+        order = [(si, q) for q in range(Q) for si in range(SI)]
+
+        gather_on_scalar(0, 0, 0)
+        gather_on_vector(1, 0, 0)
+        turned = bank_tile([P, P], 0)
+        nc.tensor.transpose(turned[:], gate_rows[:], identity[:])
+        nc.vector.tensor_copy(gate_cols[:], turned[:, 0 : E * Q])
+        gate_t = [bank_tile([P, C], 6 + e) for e in range(E)]
+        for e in range(E):
+            for q in range(Q):
+                j = e * Q + q
+                nc.tensor.transpose(gate_t[e][:, q * P : (q + 1) * P], gate_cols[:, j : j + 1].to_broadcast([P, P]), identity[:])
+        gather_on_scalar(0, 0, 1)
+        gather_on_vector(1, 0, 1)
+        permute_scales(0, 0, SN, "w2s0")
+        gather_on_vector(0, 0, 2)
+        gather_on_scalar(1, 0, 2)
+        for q in range(2):
+            gather_on_vector(0, 0, 3, q * P, P)
+        gather_on_scalar(0, 0, 3, HALF, HALF)
+        for half in range(2):
+            gather_on_scalar(1, 0, 3, half * HALF, HALF)
+        for sn in range(SN):
+            permute_words(nc.gpsimd.tensor_copy, 0, sn, tile([P, 2 * H], U8, f"w20{sn}"))
+        weave(0, 0, 0, P, "gw00", C)
+        weave(0, 0, P, HALF)
+        weave(0, 0, HALF, C)
+        weave(1, 0, 0, HALF, "gw10", C)
+        weave(1, 0, HALF, C)
+        quantize_g(0, 0, 0, C, "gc00")
+        quantize_g(1, 0, 0, C, "gc10")
+        for x, (si, q) in enumerate(order[:4]):
+            first_product(0, si, q, 0, x)
 
         for t in range(PACK - 1):
-            gather_on_scalar(0, 0, t)
-            gather_on_vector(1, 0, t)
-        gather_on_vector(0, 0, PACK - 1)
-        gather_on_scalar(1, 0, PACK - 1)
-        permute_words(nc.gpsimd.tensor_copy, 0, 0, tile([P, 2 * H], U8, "w200"))
-        for half in range(2):
-            weave(0, 0, half * HALF, (half + 1) * HALF)
-        quantize_g(0, 0, 0, HALF)
-        permute_scales(nc.vector.tensor_copy, 0, tile([P, SN, H], U8, "g00"))
-        quantize_g(0, 0, HALF, C)
-        g_woven[1, 0] = heir([P, C * PACK], BF16, "gw10", 18 * KB)
-        weave(1, 0)
-        order = [(si, q) for q in range(Q) for si in range(SI)]
-        for x, (si, q) in enumerate(order[:6]):
-            first_product(0, si, q, 0, x)
-        permute_words(nc.gpsimd.tensor_copy, 0, 1, tile([P, 2 * H], U8, "w201"))
-        permute_words(nc.gpsimd.tensor_copy, 1, 0, tile([P, 2 * H], U8, "w210"))
-        for t in range(PACK - 1):
-            gather_on_scalar(0, 1, t)
-        for half in range(2):
-            gather_on_scalar(0, 1, PACK - 1, half * HALF, HALF)
-        for half in range(2):
-            weave(0, 1, half * HALF, (half + 1) * HALF)
-        for half in range(2):
-            quantize_g(0, 1, half * HALF, (half + 1) * HALF)
-        g_codes[1, 0] = tile([P, C], U32, "g01")
-        quantize_g(1, 0)
-        g[1, 1] = heir([P, PACK, C], F32, "g11", 0)
+            gather_on_scalar(0, 1, t, 0, P)
+            gather_on_scalar(0, 1, t, P, C - P)
+        for q in range(2):
+            gather_on_vector(0, 1, 3, q * P, P)
+        gather_on_scalar(0, 1, 3, HALF, HALF)
+        permute_scales(1, 0, 1, "w2s10")
+        weave(0, 1, 0, P, "gw010", HALF)
+        weave(0, 1, P, HALF)
+        weave(0, 1, HALF, 3 * P, "gw011", HALF)
+        quantize_g(0, 1, 0, HALF, "gc010")
+        g[1, 1] = tile([P, PACK, C], F32, "g11")[:]
         for t in range(PACK):
             gather_on_scalar(1, 1, t)
-        permute_words(nc.scalar.copy, 1, 1, tile([P, 2 * H], U8, "w211"))
-        permute_scales(nc.gpsimd.tensor_copy, 1, heir([P, SN, H], U8, "w2s1", 20 * KB))
-        both = slice(0, SI)
+        weave(0, 1, 3 * P, C)
+        permute_scales(1, 1, 1, "w2s11")
 
-        for si, q in order[:6]:
+        for si, q in order[:2]:
             first_product(0, si, q, 1)
-        for x, (si, q) in enumerate(order[:4]):
-            derive(0, si, q)
-            if x < 2:
-                for sn in range(SN):
-                    first_product(0, *order[6 + x], sn, x)
-        da_codes[0, 0] = tile([P, SI, P], U32, "w2sraw1")
-        dx_bank = bank_tile([P, KT, HALF], 6)
-        for q in range(2):
-            quantize_da(0, q)
-            for k in range(KT):
-                second_product(0, q, k, dx_bank[:, k, q * P : (q + 1) * P])
-        back_on_scalar(0, 0, HALF, dx_bank, "w2raw11")
-        for q in (2, 3):
-            rectify(0, both, q, heir([P, SI, PACK, P], F32, f"upper0{q}", (2 + 4 * q) * KB))
-        for y, bank in ((0, 2), (1, 3)):
-            first_product(1, *order[y], 0, bank)
-        g_woven[1, 1] = heir([P, C * PACK], BF16, "gw11", 22 * KB)
-        for half in range(2):
-            weave(1, 1, half * HALF, (half + 1) * HALF)
-        first_product(1, *order[4], 0, 7)
         for x in (4, 5):
+            first_product(0, *order[x], 0, x)
+        for si, q in order[2:4]:
+            first_product(0, si, q, 1)
+        rectify(0, 1, 1, 1, "rect011")
+        for x in (0, 1, 2):
             derive(0, *order[x])
-            first_product(1, *order[x - 2], 0, x)
-        g_codes[1, 1] = tile([P, C], U32, "a01")
-        for half in range(2):
-            quantize_g(1, 1, half * HALF, (half + 1) * HALF)
-        quantize_da(0, 2)
-        first_product(1, *order[0], 1)
-        piece_on_scalar(0, 2, 6, "dx02")
-        for si, q in order[1:5]:
-            first_product(1, si, q, 1)
-        rectify(1, both, 1, heir([P, SI, PACK, P], F32, "lower", 24 * KB))
         for x in (6, 7):
+            first_product(0, *order[x], 0, x - 6)
+        quantize_g(0, 1, HALF, HALF, "w2sraw1")
+        quantize_da(0, 0)
+        first_product(0, *order[4], 1)
+        back_on_scalar(0, 0, 6, "dx00")
+        for si, q in order[5:]:
+            first_product(0, si, q, 1)
+        permute_words(nc.gpsimd.tensor_copy, 1, 0, tile([P, 2 * H], U8, "w210"))
+        for x in (3, 4, 5, 6):
             derive(0, *order[x])
+        permute_words(nc.scalar.copy, 1, 1, tile([P, 2 * H], U8, "a010"))
+        for y in range(2):
+            first_product(1, *order[y], 0, y + 2)
+        quantize_da(0, 1, "w2raw10")
+        back_on_scalar(0, 1, 6, "dx01")
+        for y in range(2, 4):
+            first_product(1, *order[y], 0, y + 2)
+        rectify(1, 0, 0, 2, "rect100")
+        derive(0, *order[7])
+        weave(1, 1, 0, HALF, "gw110")
+        for y in (4, 5):
+            first_product(1, *order[y], 0, y - 4)
+        quantize_da(0, 2)
+        quantize_g(1, 1, 0, HALF, "gc110")
+        back_on_scalar(0, 2, 6, "dx02")
+        for y in range(4):
+            first_product(1, *order[y], 1)
+        rectify(1, 1, 0, 2, "rect110")
+        rectify(1, 0, 2, 2, "rect102")
 
-        for x, (si, q) in enumerate(order):
-            derive(1, si, q)
-            if x == 0:
-                quantize_da(0, 3)
-                piece_on_scalar(0, 3, 6, "dx03")
-                rectify(1, slice(0, 1), 2, tile([P, 1, PACK, P], F32, "daw03"))
-                for y in (5, 6, 7):
-                    for sn in range(SN):
-                        first_product(1, *order[y], sn, y - 5)
-            if x == 2:
-                quantize_da(1, 0)
-                piece_on_scalar(1, 0, 3, "dx10")
-            if x in (4, 6):
-                q = x // 2 - 1
-                if q == 1:
-                    middle = [bank_tile([P, HALF], bank) for bank in (4, 5)]
-                quantize_da(1, q)
-                for k in range(KT):
-                    second_product(1, q, k, middle[k][:, (q - 1) * P : q * P])
-            if x in (2, 4):
-                rectify(1, slice(1, 2), x // 2 + 1, tile([P, 1, PACK, P], F32, f"daw1{x // 2 - 1}"))
-        quantize_da(1, 3)
-        last = [bank_tile([P, P], bank) for bank in (7, 0)]
-        for k in range(KT):
-            second_product(1, 3, k, last[k][:])
-        dx = [tile([P, 3 * P], F32, name) for name in ("dx_last", "daw11")]
-        for banks, c0, n in ((middle, P, HALF), (last, 3 * P, P)):
-            part = [dx[k][:, c0 - P : c0 - P + n] for k in range(KT)]
-            nc.scalar.activation(part[0], banks[0][:], COPY, scale=2.0)
-            scatter_on_scalar(part[0], 1, c0, n, 0)
-            nc.vector.tensor_scalar(part[1], banks[1][:], 2.0, None, ALU.mult)
-            scatter_on_vector(part[1], 1, c0, n, 1)
+        weave(1, 1, HALF, C, "gw111")
+        for y in (0, 1, 2):
+            derive(1, *order[y])
+        first_product(1, *order[6], 0, 2)
+        quantize_da(1, 0)
+        quantize_g(1, 1, HALF, HALF, "a110")
+        back_on_scalar(1, 0, 6, "dx10")
+        for y in (4, 5):
+            first_product(1, *order[y], 1)
+        first_product(1, *order[7], 0, 3)
+        rectify(1, 1, 2, 1, "daw10")
+        for y in (3, 4):
+            derive(1, *order[y])
+        for y in (6, 7):
+            first_product(1, *order[y], 1)
+        quantize_da(1, 1)
+        back_on_scalar(1, 1, 7, "dx11")
+        rectify(1, 1, 3, 1, "daw11")
+        for y in (5, 6):
+            derive(1, *order[y])
+        last = [bank_tile([P, HALF], 5), bank_tile([P, P], 4), bank_tile([P, P], 0)]
+        dx = [tile([P, HALF], F32, name) for name in ("dx_last0", "dx_last1")]
+        part = {q: dx[1][:, (q - 2) * P : (q - 1) * P] for q in (2, 3)}
+        for q in (2, 3):
+            quantize_da(1, q)
+            second_product(1, q, 1, last[q - 1][:])
+            second_product(1, q, 0, last[0][:, (q - 2) * P : (q - 1) * P])
+            if q == 2:
+                derive(1, *order[7])
+                nc.vector.tensor_scalar(part[q], last[1][:], 2.0, None, ALU.mult)
+        nc.scalar.activation(dx[0][:], last[0][:], COPY, scale=2.0)
+        scatter_on_scalar(dx[0][:], 1, HALF, HALF, 0)
+        scatter_on_vector(part[2], 1, 2 * P, P, 1)
+        nc.vector.tensor_scalar(part[3], last[2][:], 2.0, None, ALU.mult)
+        scatter_on_vector(part[3], 1, 3 * P, P, 1)
         for k in (1, 0):
             nc.sync.dma_start(out[k * P : (k + 1) * P, :], windows[k][:])

@@ -32,16 +32,15 @@ def tile_moe_bdx_mlp_relu2_kernel(
     ROWS = 4
     ALIGN = 64
     HALF = C // 2
-    KB = 1024
+    UNIT = 512
     PLACES = {
-        "gw10": 0, "w2s10": 0, "g11": 2,
-        "gw010": 10, "w2s11": 10, "rect011": 11,
-        "daw00": 16, "w210": 15,
-        "daw01": 36, "gw110": 35, "rect100": 37,
-        "daw02": 24, "rect110": 21, "gw111": 25, "rect102": 27,
-        "g01first": 32, "gw011": 32,
+        "g01first": 94, "g11": 79, "gc001": 95, "gw011": 97, "rect003": 100,
+        "a000": 0, "gc011": 0, "w2s11": 2,
+        "gw010": 20, "w2s10": 20, "w211": 23,
+        "daw00": 40, "rect012": 34, "gw110": 42, "rect100": 46,
+        "gw111": 42, "rect102": 38, "daw02": 64, "rect110": 66,
     }
-    PIECES = (((0, 1), (1, 1), (2, 2)), ((0, 1), (1, 1), (2, 1), (3, 1)))
+    PIECES = (((0, 2), (2, 2)), ((0, 1), (1, 1), (2, 1), (3, 1)))
 
     with ExitStack() as ctx:
         held = ctx.enter_context(tc.tile_pool(name="held", bufs=1))
@@ -50,7 +49,7 @@ def tile_moe_bdx_mlp_relu2_kernel(
 
         def tile(shape, dtype, name):
             if name in PLACES:
-                return heirs.tile(shape, dtype, name=name, offset=PLACES[name] * KB, align_bytes=ALIGN)
+                return heirs.tile(shape, dtype, name=name, offset=PLACES[name] * UNIT, align_bytes=ALIGN)
             return held.tile(shape, dtype, name=name, align_bytes=ALIGN)
 
         def bank_tile(shape, bank):
@@ -101,24 +100,23 @@ def tile_moe_bdx_mlp_relu2_kernel(
 
         load_dy(0, 0)
         nc.sync.dma_start(gate_rows[0 : E * Q, :], gate[0].rearrange("(j n) -> j n", n=P))
-        load_dy(0, 1)
+        for t in range(1, PACK):
+            load_dy(0, t)
         load_scales(0)
-        load_dy(0, 2)
-        load_dy(0, 3)
         load_w2(0, 0)
         load_w2(0, 1)
         for t in range(PACK):
             load_dy(1, t)
-        load_scales(1)
         load_a(0, 0, 0)
         load_a(0, 0, 1)
+        load_scales(1)
+        load_w2(1, 1)
+        load_a(0, 1, 0)
         for row in range(ROWS):
             nc.sync.dma_start(w1s_t[row:P:32, :, :].bitcast(I32), w1s_v[row])
         load_w1(0)
         load_w2(1, 0)
-        load_a(0, 1, 0)
         load_a(0, 1, 1)
-        load_w2(1, 1)
         load_a(1, 0, 0)
         load_a(1, 0, 1)
         load_w1(1)
@@ -177,11 +175,11 @@ def tile_moe_bdx_mlp_relu2_kernel(
                 in_=w2_raw[e, sn][:].bitcast(U16).rearrange("p (s m t) -> p s t m", s=SI, t=PACK),
             )
 
-        def permute_scales(e, first, n, name):
+        def permute_scales(move, e, first, n, name):
             planes = tile([P, n, H], U8, name)
             for x in range(n):
                 w2s_t[e, first + x] = planes[:, x, :]
-            nc.gpsimd.tensor_copy(
+            move(
                 out=planes[:].rearrange("p n (s t m) -> p (n s) t m", s=SI, t=PACK),
                 in_=w2s_raw[e][:, first : first + n, :].rearrange("p n (s m t) -> p (n s) t m", s=SI, t=PACK),
             )
@@ -275,6 +273,12 @@ def tile_moe_bdx_mlp_relu2_kernel(
             for k in (1, 0):
                 scatter_on_scalar(dx[:, k, :], e, q * P, n, k)
 
+        def row_block_1_first(dx, q, bank):
+            dx_bank = products(1, q, bank)
+            for k in (1, 0):
+                nc.scalar.activation(dx[:, k, q * P : (q + 1) * P], dx_bank[:, k, :], COPY, scale=2.0)
+            scatter_on_scalar(dx[:, 1, q * P : (q + 1) * P], 1, q * P, P, 1)
+
         def both_passes(e, si, q, bank):
             for sn in range(SN):
                 first_product(e, si, q, sn, bank)
@@ -293,7 +297,6 @@ def tile_moe_bdx_mlp_relu2_kernel(
                 nc.tensor.transpose(gate_t[e][:, q * P : (q + 1) * P], gate_cols[:, j : j + 1].to_broadcast([P, P]), identity[:])
         gather_on_scalar(0, 0, 1)
         gather_on_vector(1, 0, 1)
-        permute_scales(0, 0, SN, "w2s0")
         gather_on_vector(0, 0, 2)
         gather_on_scalar(1, 0, 2)
         for q in range(2):
@@ -308,8 +311,10 @@ def tile_moe_bdx_mlp_relu2_kernel(
         weave(0, 0, HALF, C)
         weave(1, 0, 0, HALF, "gw10", C)
         weave(1, 0, HALF, C)
-        quantize_g(0, 0, 0, C, "gc00")
-        quantize_g(1, 0, 0, C, "gc10")
+        permute_scales(nc.vector.tensor_copy, 0, 0, SN, "w2raw00")
+        quantize_g(0, 0, 0, HALF, "gc000")
+        for half in range(2):
+            quantize_g(1, 0, half * HALF, HALF, f"gc10{half}")
         for x, (si, q) in enumerate(order[:4]):
             first_product(0, si, q, 0, x)
 
@@ -319,91 +324,88 @@ def tile_moe_bdx_mlp_relu2_kernel(
         for q in range(2):
             gather_on_vector(0, 1, 3, q * P, P)
         gather_on_scalar(0, 1, 3, HALF, HALF)
-        permute_scales(1, 0, 1, "w2s10")
         weave(0, 1, 0, P, "gw010", HALF)
         weave(0, 1, P, HALF)
-        weave(0, 1, HALF, 3 * P, "gw011", HALF)
+        quantize_g(0, 0, HALF, HALF, "gc001")
+        first_product(0, *order[4], 0, 4)
         quantize_g(0, 1, 0, HALF, "gc010")
         g[1, 1] = tile([P, PACK, C], F32, "g11")[:]
         for t in range(PACK):
             gather_on_scalar(1, 1, t)
-        weave(0, 1, 3 * P, C)
-        permute_scales(1, 1, 1, "w2s11")
+        weave(0, 1, HALF, C, "gw011")
+        permute_scales(nc.gpsimd.tensor_copy, 1, 0, 1, "w2s10")
 
-        for si, q in order[:2]:
-            first_product(0, si, q, 1)
-        for x in (4, 5):
-            first_product(0, *order[x], 0, x)
-        for si, q in order[2:4]:
-            first_product(0, si, q, 1)
-        rectify(0, 1, 1, 1, "rect011")
-        for x in (0, 1, 2):
+        across = (0, 2, 1, 3)
+        for x in across:
+            first_product(0, *order[x], 1)
+        first_product(0, *order[5], 0, 5)
+        for x in across[:3]:
             derive(0, *order[x])
-        for x in (6, 7):
-            first_product(0, *order[x], 0, x - 6)
-        quantize_g(0, 1, HALF, HALF, "w2sraw1")
-        quantize_da(0, 0)
+        quantize_g(0, 1, HALF, HALF, "gc011")
+        permute_scales(nc.vector.tensor_copy, 1, 1, 1, "w2s11")
+        for sn in (1, 0):
+            permute_words(nc.scalar.copy, 1, sn, tile([P, 2 * H], U8, f"w21{sn}"))
+        rectify(0, 0, 3, 1, "rect003")
+        first_product(0, *order[6], 0, 0)
         first_product(0, *order[4], 1)
-        back_on_scalar(0, 0, 6, "dx00")
-        for si, q in order[5:]:
-            first_product(0, si, q, 1)
-        permute_words(nc.gpsimd.tensor_copy, 1, 0, tile([P, 2 * H], U8, "w210"))
-        for x in (3, 4, 5, 6):
+        first_product(0, *order[7], 0, 2)
+        for x in (6, 5, 7):
+            first_product(0, *order[x], 1)
+        for x in (3, 4):
             derive(0, *order[x])
-        permute_words(nc.scalar.copy, 1, 1, tile([P, 2 * H], U8, "a010"))
-        for y in range(2):
-            first_product(1, *order[y], 0, y + 2)
-        quantize_da(0, 1, "w2raw10")
-        back_on_scalar(0, 1, 6, "dx01")
-        for y in range(2, 4):
-            first_product(1, *order[y], 0, y + 2)
+        quantize_da(0, 0, "w2sraw1")
+        back_on_scalar(0, 0, 6, "w2raw10")
+        for y, bank in ((0, 1), (2, 3), (1, 4)):
+            first_product(1, *order[y], 0, bank)
+        rectify(0, 1, 2, 2, "rect012")
         rectify(1, 0, 0, 2, "rect100")
-        derive(0, *order[7])
+        derive(0, *order[6])
+        first_product(1, *order[3], 0, 0)
         weave(1, 1, 0, HALF, "gw110")
-        for y in (4, 5):
-            first_product(1, *order[y], 0, y - 4)
+        for x in (5, 7):
+            derive(0, *order[x])
+        first_product(1, *order[4], 0, 5)
+        quantize_g(1, 1, 0, HALF, "a100")
+        first_product(1, *order[0], 1)
         quantize_da(0, 2)
-        quantize_g(1, 1, 0, HALF, "gc110")
-        back_on_scalar(0, 2, 6, "dx02")
-        for y in range(4):
+        back_on_scalar(0, 2, 2, "dx02")
+        for y in across[1:]:
             first_product(1, *order[y], 1)
+        first_product(1, *order[6], 0, 6)
         rectify(1, 1, 0, 2, "rect110")
-        rectify(1, 0, 2, 2, "rect102")
 
         weave(1, 1, HALF, C, "gw111")
-        for y in (0, 1, 2):
+        derive(1, *order[0])
+        quantize_g(1, 1, HALF, HALF, "a101")
+        rectify(1, 0, 2, 2, "rect102")
+        for y in (4, 6):
+            first_product(1, *order[y], 1)
+        both_passes(1, *order[5], 1)
+        for y in across[1:]:
             derive(1, *order[y])
-        first_product(1, *order[6], 0, 2)
         quantize_da(1, 0)
-        quantize_g(1, 1, HALF, HALF, "a110")
-        back_on_scalar(1, 0, 6, "dx10")
-        for y in (4, 5):
-            first_product(1, *order[y], 1)
-        first_product(1, *order[7], 0, 3)
-        rectify(1, 1, 2, 1, "daw10")
-        for y in (3, 4):
-            derive(1, *order[y])
-        for y in (6, 7):
-            first_product(1, *order[y], 1)
+        dx = tile([P, KT, HALF], F32, "dx10")
+        row_block_1_first(dx, 0, 2)
+        both_passes(1, *order[7], 3)
+        derive(1, *order[4])
         quantize_da(1, 1)
-        back_on_scalar(1, 1, 7, "dx11")
+        row_block_1_first(dx, 1, 7)
+        scatter_on_scalar(dx[:, 0, :], 1, 0, HALF, 0)
         rectify(1, 1, 3, 1, "daw11")
-        for y in (5, 6):
+        for y in (6, 5, 7):
             derive(1, *order[y])
-        last = [bank_tile([P, HALF], 5), bank_tile([P, P], 4), bank_tile([P, P], 0)]
-        dx = [tile([P, HALF], F32, name) for name in ("dx_last0", "dx_last1")]
-        part = {q: dx[1][:, (q - 2) * P : (q - 1) * P] for q in (2, 3)}
+        last = [bank_tile([P, HALF], 0), bank_tile([P, P], 4), bank_tile([P, P], 5)]
         for q in (2, 3):
             quantize_da(1, q)
             second_product(1, q, 1, last[q - 1][:])
             second_product(1, q, 0, last[0][:, (q - 2) * P : (q - 1) * P])
-            if q == 2:
-                derive(1, *order[7])
-                nc.vector.tensor_scalar(part[q], last[1][:], 2.0, None, ALU.mult)
-        nc.scalar.activation(dx[0][:], last[0][:], COPY, scale=2.0)
-        scatter_on_scalar(dx[0][:], 1, HALF, HALF, 0)
-        scatter_on_vector(part[2], 1, 2 * P, P, 1)
-        nc.vector.tensor_scalar(part[3], last[2][:], 2.0, None, ALU.mult)
-        scatter_on_vector(part[3], 1, 3 * P, P, 1)
+        dx_0 = tile([P, HALF], F32, "dx_last0")
+        nc.scalar.activation(dx_0[:], last[0][:], COPY, scale=2.0)
+        scatter_on_scalar(dx_0[:], 1, HALF, HALF, 0)
+        dx_1 = tile([P, HALF], F32, "daw13")
+        for q in (2, 3):
+            part = dx_1[:, (q - 2) * P : (q - 1) * P]
+            nc.vector.tensor_scalar(part, last[q - 1][:], 2.0, None, ALU.mult)
+            scatter_on_vector(part, 1, q * P, P, 1)
         for k in (1, 0):
             nc.sync.dma_start(out[k * P : (k + 1) * P, :], windows[k][:])

@@ -34,13 +34,12 @@ def tile_moe_bdx_mlp_relu2_kernel(
     HALF = C // 2
     UNIT = 512
     PLACES = {
-        "g01first": 94, "g11": 79, "gc001": 95, "gw011": 97, "rect003": 100,
-        "a000": 0, "gc011": 0, "w2s11": 2,
-        "gw010": 20, "w2s10": 20, "w211": 23,
-        "daw00": 40, "rect012": 34, "gw110": 42, "rect100": 46,
-        "gw111": 42, "rect102": 38, "daw02": 64, "rect110": 66,
+        "gw010": 26, "w2s1": 23, "w210": 29,
+        "daw00": 40, "rect012": 33, "w211": 47,
+        "a001": 56, "gw110": 63, "gw111": 64,
+        "daw02": 76, "rect110": 69, "rect102": 83,
     }
-    PIECES = (((0, 2), (2, 2)), ((0, 1), (1, 1), (2, 1), (3, 1)))
+    PIECES = (((0, 2), (2, 2)), ((0, 2), (2, 1), (3, 1)))
 
     with ExitStack() as ctx:
         held = ctx.enter_context(tc.tile_pool(name="held", bufs=1))
@@ -104,32 +103,32 @@ def tile_moe_bdx_mlp_relu2_kernel(
             load_dy(0, t)
         load_scales(0)
         load_w2(0, 0)
+        load_dy(1, 0)
         load_w2(0, 1)
-        for t in range(PACK):
+        for t in range(1, PACK):
             load_dy(1, t)
         load_a(0, 0, 0)
         load_a(0, 0, 1)
         load_scales(1)
-        load_w2(1, 1)
-        load_a(0, 1, 0)
         for row in range(ROWS):
             nc.sync.dma_start(w1s_t[row:P:32, :, :].bitcast(I32), w1s_v[row])
         load_w1(0)
         load_w2(1, 0)
+        load_a(0, 1, 0)
         load_a(0, 1, 1)
+        load_w2(1, 1)
         load_a(1, 0, 0)
         load_a(1, 0, 1)
         load_w1(1)
         load_a(1, 1, 0)
         load_a(1, 1, 1)
 
-        g = {(e, 0): tile([P, PACK, C], F32, f"g{e}0")[:] for e in range(E)}
-        g_first, g_rest = tile([P, PACK, P], F32, "g01first"), tile([P, PACK, C - P], F32, "g01rest")
+        g_both = tile([P, PACK, E * C], F32, "g0")
+        g = {(0, 0): g_both[:], (1, 0): g_both[:, :, C:]}
+        g[0, 1] = tile([P, PACK, C], F32, "g01")[:]
 
         def gathered(e, sn, c0, c1):
-            if (e, sn) != (0, 1):
-                return g[e, sn][:, :, c0:c1]
-            return g_first[:] if c0 == 0 else g_rest[:, :, c0 - P : c1 - P]
+            return g[e, sn][:, :, c0:c1]
 
         g_woven = {}
         piece = {(e, first + x): (first, n) for e in range(E) for first, n in PIECES[e] for x in range(n)}
@@ -273,20 +272,14 @@ def tile_moe_bdx_mlp_relu2_kernel(
             for k in (1, 0):
                 scatter_on_scalar(dx[:, k, :], e, q * P, n, k)
 
-        def row_block_1_first(dx, q, bank):
-            dx_bank = products(1, q, bank)
-            for k in (1, 0):
-                nc.scalar.activation(dx[:, k, q * P : (q + 1) * P], dx_bank[:, k, :], COPY, scale=2.0)
-            scatter_on_scalar(dx[:, 1, q * P : (q + 1) * P], 1, q * P, P, 1)
-
         def both_passes(e, si, q, bank):
             for sn in range(SN):
                 first_product(e, si, q, sn, bank)
 
         order = [(si, q) for q in range(Q) for si in range(SI)]
 
-        gather_on_scalar(0, 0, 0)
-        gather_on_vector(1, 0, 0)
+        gather_on_vector(0, 0, 0)
+        gather_on_scalar(0, 0, 0, C, C)
         turned = bank_tile([P, P], 0)
         nc.tensor.transpose(turned[:], gate_rows[:], identity[:])
         nc.vector.tensor_copy(gate_cols[:], turned[:, 0 : E * Q])
@@ -295,77 +288,62 @@ def tile_moe_bdx_mlp_relu2_kernel(
             for q in range(Q):
                 j = e * Q + q
                 nc.tensor.transpose(gate_t[e][:, q * P : (q + 1) * P], gate_cols[:, j : j + 1].to_broadcast([P, P]), identity[:])
-        gather_on_scalar(0, 0, 1)
-        gather_on_vector(1, 0, 1)
-        gather_on_vector(0, 0, 2)
-        gather_on_scalar(1, 0, 2)
-        for q in range(2):
-            gather_on_vector(0, 0, 3, q * P, P)
-        gather_on_scalar(0, 0, 3, HALF, HALF)
-        for half in range(2):
-            gather_on_scalar(1, 0, 3, half * HALF, HALF)
-        for sn in range(SN):
-            permute_words(nc.gpsimd.tensor_copy, 0, sn, tile([P, 2 * H], U8, f"w20{sn}"))
-        weave(0, 0, 0, P, "gw00", C)
-        weave(0, 0, P, HALF)
-        weave(0, 0, HALF, C)
-        weave(1, 0, 0, HALF, "gw10", C)
-        weave(1, 0, HALF, C)
-        permute_scales(nc.vector.tensor_copy, 0, 0, SN, "w2raw00")
-        quantize_g(0, 0, 0, HALF, "gc000")
-        for half in range(2):
-            quantize_g(1, 0, half * HALF, HALF, f"gc10{half}")
-        for x, (si, q) in enumerate(order[:4]):
+        for t in range(1, PACK - 1):
+            gather_on_vector(0, 0, t)
+            gather_on_scalar(0, 0, t, C, C)
+        gather_on_vector(0, 0, 3, 0, HALF)
+        gather_on_vector(0, 0, 3, HALF, P)
+        gather_on_scalar(0, 0, 3, 3 * P, C + P)
+        permute_scales(nc.gpsimd.tensor_copy, 0, 0, SN, "w2s0")
+        permute_words(nc.gpsimd.tensor_copy, 0, 0, tile([P, 2 * H], U8, "w200"))
+        weave(0, 0, 0, HALF, "gw00", C)
+        weave(0, 0, HALF, 3 * P)
+        weave(0, 0, 3 * P, C)
+        weave(1, 0, 0, C, "gw10")
+        for e in range(E):
+            quantize_g(e, 0, 0, C, f"gc{e}0")
+        permute_words(nc.gpsimd.tensor_copy, 0, 1, tile([P, 2 * H], U8, "gw10"))
+        for x, (si, q) in enumerate(order[:6]):
             first_product(0, si, q, 0, x)
 
         for t in range(PACK - 1):
-            gather_on_scalar(0, 1, t, 0, P)
-            gather_on_scalar(0, 1, t, P, C - P)
-        for q in range(2):
-            gather_on_vector(0, 1, 3, q * P, P)
+            gather_on_scalar(0, 1, t)
+        gather_on_vector(0, 1, 3, 0, HALF)
         gather_on_scalar(0, 1, 3, HALF, HALF)
-        weave(0, 1, 0, P, "gw010", HALF)
-        weave(0, 1, P, HALF)
-        quantize_g(0, 0, HALF, HALF, "gc001")
-        first_product(0, *order[4], 0, 4)
+        weave(0, 1, 0, HALF, "gw010")
+        weave(0, 1, HALF, 3 * P, "gw011", HALF)
         quantize_g(0, 1, 0, HALF, "gc010")
-        g[1, 1] = tile([P, PACK, C], F32, "g11")[:]
+        g[1, 1] = tile([P, PACK, C], F32, "w2raw01")[:]
         for t in range(PACK):
             gather_on_scalar(1, 1, t)
-        weave(0, 1, HALF, C, "gw011")
-        permute_scales(nc.gpsimd.tensor_copy, 1, 0, 1, "w2s10")
+        permute_words(nc.scalar.copy, 1, 0, tile([P, 2 * H], U8, "w210"))
+        weave(0, 1, 3 * P, C)
+        permute_scales(nc.gpsimd.tensor_copy, 1, 0, SN, "w2s1")
 
         across = (0, 2, 1, 3)
         for x in across:
             first_product(0, *order[x], 1)
-        first_product(0, *order[5], 0, 5)
-        for x in across[:3]:
+        for x in across:
             derive(0, *order[x])
-        quantize_g(0, 1, HALF, HALF, "gc011")
-        permute_scales(nc.vector.tensor_copy, 1, 1, 1, "w2s11")
-        for sn in (1, 0):
-            permute_words(nc.scalar.copy, 1, sn, tile([P, 2 * H], U8, f"w21{sn}"))
-        rectify(0, 0, 3, 1, "rect003")
-        first_product(0, *order[6], 0, 0)
-        first_product(0, *order[4], 1)
-        first_product(0, *order[7], 0, 2)
-        for x in (6, 5, 7):
+        for x in (6, 7):
+            first_product(0, *order[x], 0, 2 * (x - 6))
+        quantize_g(0, 1, HALF, HALF, "a000")
+        for x in (4, 6):
             first_product(0, *order[x], 1)
-        for x in (3, 4):
-            derive(0, *order[x])
-        quantize_da(0, 0, "w2sraw1")
+        quantize_da(0, 0)
         back_on_scalar(0, 0, 6, "w2raw10")
-        for y, bank in ((0, 1), (2, 3), (1, 4)):
-            first_product(1, *order[y], 0, bank)
-        rectify(0, 1, 2, 2, "rect012")
-        rectify(1, 0, 0, 2, "rect100")
-        derive(0, *order[6])
-        first_product(1, *order[3], 0, 0)
-        weave(1, 1, 0, HALF, "gw110")
         for x in (5, 7):
-            derive(0, *order[x])
-        first_product(1, *order[4], 0, 5)
-        quantize_g(1, 1, 0, HALF, "a100")
+            first_product(0, *order[x], 1)
+        rectify(0, 1, 2, 2, "rect012")
+        permute_words(nc.gpsimd.tensor_copy, 1, 1, tile([P, 2 * H], U8, "w211"))
+        weave(1, 1, 0, HALF, "gw110")
+        for y, bank in ((0, 1), (2, 3)):
+            first_product(1, *order[y], 0, bank)
+        for x in across:
+            derive(0, *order[4 + x])
+        for y, bank in ((1, 4), (3, 0), (4, 5)):
+            first_product(1, *order[y], 0, bank)
+        quantize_g(1, 1, 0, HALF, "a011")
         first_product(1, *order[0], 1)
         quantize_da(0, 2)
         back_on_scalar(0, 2, 2, "dx02")
@@ -374,38 +352,32 @@ def tile_moe_bdx_mlp_relu2_kernel(
         first_product(1, *order[6], 0, 6)
         rectify(1, 1, 0, 2, "rect110")
 
+        rectify(1, 0, 2, 1, "rect102")
+
         weave(1, 1, HALF, C, "gw111")
-        derive(1, *order[0])
+        for y in across:
+            derive(1, *order[y])
+        for y, bank in ((5, 1), (7, 3)):
+            first_product(1, *order[y], 0, bank)
         quantize_g(1, 1, HALF, HALF, "a101")
-        rectify(1, 0, 2, 2, "rect102")
         for y in (4, 6):
             first_product(1, *order[y], 1)
-        both_passes(1, *order[5], 1)
-        for y in across[1:]:
-            derive(1, *order[y])
         quantize_da(1, 0)
-        dx = tile([P, KT, HALF], F32, "dx10")
-        row_block_1_first(dx, 0, 2)
-        both_passes(1, *order[7], 3)
-        derive(1, *order[4])
-        quantize_da(1, 1)
-        row_block_1_first(dx, 1, 7)
-        scatter_on_scalar(dx[:, 0, :], 1, 0, HALF, 0)
-        rectify(1, 1, 3, 1, "daw11")
-        for y in (6, 5, 7):
-            derive(1, *order[y])
-        last = [bank_tile([P, HALF], 0), bank_tile([P, P], 4), bank_tile([P, P], 5)]
+        back_on_scalar(1, 0, 2, "dx10")
+        for y in (5, 7):
+            first_product(1, *order[y], 1)
+        rectify(1, 1, 3, 1, "daw10")
+        for y in across:
+            derive(1, *order[4 + y])
+        last = [bank_tile([P, HALF], bank) for bank in (0, 4)]
         for q in (2, 3):
             quantize_da(1, q)
-            second_product(1, q, 1, last[q - 1][:])
-            second_product(1, q, 0, last[0][:, (q - 2) * P : (q - 1) * P])
-        dx_0 = tile([P, HALF], F32, "dx_last0")
-        nc.scalar.activation(dx_0[:], last[0][:], COPY, scale=2.0)
-        scatter_on_scalar(dx_0[:], 1, HALF, HALF, 0)
-        dx_1 = tile([P, HALF], F32, "daw13")
-        for q in (2, 3):
-            part = dx_1[:, (q - 2) * P : (q - 1) * P]
-            nc.vector.tensor_scalar(part, last[q - 1][:], 2.0, None, ALU.mult)
-            scatter_on_vector(part, 1, q * P, P, 1)
+            for k in (1, 0):
+                second_product(1, q, k, last[k][:, (q - 2) * P : (q - 1) * P])
+        upper = [tile([P, HALF], F32, name) for name in ("dx_last0", "daw13")]
+        for k in (1, 0):
+            nc.vector.tensor_scalar(upper[k][:], last[k][:], 2.0, None, ALU.mult)
+        scatter_on_vector(upper[1][:], 1, HALF, HALF, 1)
+        scatter_on_scalar(upper[0][:], 1, HALF, HALF, 0)
         for k in (1, 0):
             nc.sync.dma_start(out[k * P : (k + 1) * P, :], windows[k][:])

@@ -101,12 +101,11 @@ def tile_moe_bdx_mlp_relu2_kernel(
         nc.sync.dma_start(gate_rows[0 : E * Q, :], gate[0].rearrange("(j n) -> j n", n=P))
         for t in range(1, PACK):
             load_dy(0, t)
-        load_scales(0)
         load_w2(0, 0)
-        load_dy(1, 0)
-        load_w2(0, 1)
-        for t in range(1, PACK):
+        load_scales(0)
+        for t in range(PACK):
             load_dy(1, t)
+        load_w2(0, 1)
         load_a(0, 0, 0)
         load_a(0, 0, 1)
         load_scales(1)
@@ -291,13 +290,11 @@ def tile_moe_bdx_mlp_relu2_kernel(
         for t in range(1, PACK - 1):
             gather_on_vector(0, 0, t)
             gather_on_scalar(0, 0, t, C, C)
-        gather_on_vector(0, 0, 3, 0, HALF)
-        gather_on_vector(0, 0, 3, HALF, P)
+        gather_on_vector(0, 0, 3, 0, 3 * P)
         gather_on_scalar(0, 0, 3, 3 * P, C + P)
-        permute_scales(nc.gpsimd.tensor_copy, 0, 0, SN, "w2s0")
         permute_words(nc.gpsimd.tensor_copy, 0, 0, tile([P, 2 * H], U8, "w200"))
-        weave(0, 0, 0, HALF, "gw00", C)
-        weave(0, 0, HALF, 3 * P)
+        permute_scales(nc.gpsimd.tensor_copy, 0, 0, SN, "w2s0")
+        weave(0, 0, 0, 3 * P, "gw00", C)
         weave(0, 0, 3 * P, C)
         weave(1, 0, 0, C, "gw10")
         for e in range(E):
@@ -308,8 +305,8 @@ def tile_moe_bdx_mlp_relu2_kernel(
 
         for t in range(PACK - 1):
             gather_on_scalar(0, 1, t)
-        gather_on_vector(0, 1, 3, 0, HALF)
-        gather_on_scalar(0, 1, 3, HALF, HALF)
+        for half in range(2):
+            gather_on_scalar(0, 1, 3, half * HALF, HALF)
         weave(0, 1, 0, HALF, "gw010")
         weave(0, 1, HALF, 3 * P, "gw011", HALF)
         quantize_g(0, 1, 0, HALF, "gc010")

from contextlib import ExitStack

import concourse.mybir as mybir
from concourse.masks import make_identity

K, T, E, C, H, N = 256, 1024, 2, 512, 1024, 1024
P = 128
PACK = 4
PASS = P * PACK
FLOPS = 2 * E * C * H * (N + K)
BYTES = 4 * (N * T + H * E * C + K * T + E * C) + E * N * H // 2 + E * H * K // 2 + E * N * H // 32 + E * H * K // 32 + 2 * E * C

F32 = mybir.dt.float32
BF16 = mybir.dt.bfloat16
I32 = mybir.dt.int32
U32 = mybir.dt.uint32
U16 = mybir.dt.uint16
U8 = mybir.dt.uint8
E5M2 = mybir.dt.float8_e5m2_x4
E2M1 = mybir.dt.float4_e2m1fn_x4
ALU = mybir.AluOpType
COPY = mybir.ActivationFunctionType.Copy
F32_MAX = 3.4028234663852886e38


def tile_moe_bdx_mlp_relu2_kernel(
    tc, dyT, a, w2_words, w2_scales, w1_words, w1_scales, gate, offs, out
):
    nc = tc.nc
    SN, SI, KT, Q = N // PASS, H // PASS, K // P, C // P
    STRIPE = 16
    ROWS = 4
    ALIGN = 64
    HALF = C // 2
    UNIT = 512
    PLACES = {
        "gw010": 26, "w2s1": 23, "w210": 29,
        "daw00": 40, "rect012": 33, "w211": 47,
        "a001": 56, "gw110": 63, "gw111": 64,
        "daw02": 76, "rect110": 69, "rect102": 83,
    }
    PIECES = (((0, 2), (2, 2)), ((0, 2), (2, 1), (3, 1)))

    with ExitStack() as ctx:
        held = ctx.enter_context(tc.tile_pool(name="held", bufs=1))
        heirs = ctx.enter_context(tc.tile_pool(name="heirs", bufs=1))
        psum = ctx.enter_context(tc.psum_pool(name="psum", bufs=1))

        def tile(shape, dtype, name):
            if name in PLACES:
                return heirs.tile(shape, dtype, name=name, offset=PLACES[name] * UNIT, align_bytes=ALIGN)
            return held.tile(shape, dtype, name=name, align_bytes=ALIGN)

        def bank_tile(shape, bank):
            return psum.tile(shape, F32, name=f"bank{bank}")

        groups = [(e, s) for e in range(E) for s in range(2)]
        offsets = held.tile([P, E * C // STRIPE], U16, name="offsets")
        dy_t = [[tile([P, T], F32, f"dy{sn}{t}") for t in range(PACK)] for sn in range(SN)]
        a_t = {(e, half, si): tile([P, PACK, HALF], F32, f"a{e}{half}{si}") for e, half in groups for si in range(SI)}
        w2_raw = {x: tile([P, 2 * H], U8, f"w2raw{x[0]}{x[1]}") for x in groups}
        w2s_raw = [tile([P, SN, H], U8, f"w2sraw{e}") for e in range(E)]
        w1_t = tile([P, E * SI, 2 * K], U8, "w1t")
        w1s_t = tile([P, E * SI, K], U8, "w1s")
        gate_rows = tile([P, P], F32, "gate_rows")
        gate_cols = tile([P, E * Q], F32, "gate_cols")
        identity = tile([P, P], F32, "identity")
        w2_t, w2s_t = {}, {}

        dy_v = dyT.rearrange("(s p t) c -> s t p c", p=P, t=PACK)
        a_v = a.rearrange("(s p t) (e h c) -> e h s p t c", p=P, t=PACK, e=E, h=2)
        w2_v = w2_words.bitcast(I32)
        w2s_v = w2_scales.bitcast(I32).rearrange("e s (x r) i -> e r x s i", r=ROWS)
        w1_v = w1_words.bitcast(I32).rearrange("e s p b -> e p s b")
        w1s_v = w1_scales.bitcast(I32).rearrange("e s (x r) i -> r x (e s) i", r=ROWS)

        nc.sync.dma_start(offsets[:], offs)
        nc.vector.memset(gate_rows[:], 0.0)
        for e in range(E):
            nc.vector.memset(w2s_raw[e][:].bitcast(I32), 0)
        nc.vector.memset(w1s_t[:].bitcast(I32), 0)
        make_identity(nc, identity[:])

        def load_dy(sn, t):
            nc.sync.dma_start(dy_t[sn][t][:], dy_v[sn, t])

        def load_a(e, half, si):
            nc.sync.dma_start(a_t[e, half, si][:], a_v[e, half, si])

        def load_w2(e, sn):
            nc.sync.dma_start(w2_raw[e, sn][:].bitcast(I32), w2_v[e, sn])

        def load_scales(e):
            for row in range(ROWS):
                nc.sync.dma_start(w2s_raw[e][row:P:32, :, :].bitcast(I32), w2s_v[e, row])

        def load_w1(e):
            nc.sync.dma_start(w1_t[:, e * SI : (e + 1) * SI, :].bitcast(I32), w1_v[e])

        load_dy(0, 0)
        nc.sync.dma_start(gate_rows[0 : E * Q, :], gate[0].rearrange("(j n) -> j n", n=P))
        for t in range(1, PACK):
            load_dy(0, t)
        load_w2(0, 0)
        load_scales(0)
        for t in range(PACK):
            load_dy(1, t)
        load_w2(0, 1)
        load_a(0, 0, 0)
        load_a(0, 0, 1)
        load_scales(1)
        for row in range(ROWS):
            nc.sync.dma_start(w1s_t[row:P:32, :, :].bitcast(I32), w1s_v[row])
        load_w1(0)
        load_w2(1, 0)
        load_a(0, 1, 0)
        load_a(0, 1, 1)
        load_w2(1, 1)
        load_a(1, 0, 0)
        load_a(1, 0, 1)
        load_w1(1)
        load_a(1, 1, 0)
        load_a(1, 1, 1)

        g_both = tile([P, PACK, E * C], F32, "g0")
        g = {(0, 0): g_both[:], (1, 0): g_both[:, :, C:]}
        g[0, 1] = tile([P, PACK, C], F32, "g01")[:]

        def gathered(e, sn, c0, c1):
            return g[e, sn][:, :, c0:c1]

        g_woven = {}
        piece = {(e, first + x): (first, n) for e in range(E) for first, n in PIECES[e] for x in range(n)}
        g_codes, g_scales = {}, {}
        da_woven, da_codes, da_scales = {}, {}, {}
        windows = [tile([P, T], F32, f"window{k}") for k in range(KT)]
        dh_bank, rectified = {}, {}

        def slots(c0, n, e):
            return offsets[:, (e * C + c0) // STRIPE : (e * C + c0 + n) // STRIPE]

        def gather_on_scalar(e, sn, t, c0=0, n=C):
            nc.scalar.activation(gathered(e, sn, c0, c0 + n)[:, t, :], dy_t[sn][t][:].indirect(slots(c0, n, e)), COPY)

        def gather_on_vector(e, sn, t, c0=0, n=C):
            nc.vector.tensor_copy(gathered(e, sn, c0, c0 + n)[:, t, :], dy_t[sn][t][:].indirect(slots(c0, n, e)))

        def weave(e, sn, c0, c1, name=None, n=None):
            if name:
                woven = tile([P, (n or c1 - c0) * PACK], BF16, name)
                for q in range(c0 // P, (c0 + (n or c1 - c0)) // P):
                    g_woven[e, sn, q] = (woven, c0)
            woven, first = g_woven[e, sn, c0 // P]
            nc.vector.tensor_tensor(
                woven[:, PACK * (c0 - first) : PACK * (c1 - first)].rearrange("p (c v t) -> p c t v", v=2, t=PACK),
                gathered(e, sn, c0, c1).rearrange("p t (c v) -> p c t v", v=2),
                gate_t[e][:, c0:c1].rearrange("p (c v) -> p c v", v=2).unsqueeze(2).to_broadcast([P, (c1 - c0) // 2, PACK, 2]),
                ALU.mult,
            )

        def quantize_g(e, sn, c0, n, name):
            woven, first = g_woven[e, sn, c0 // P]
            codes, scales = tile([P, n], U32, name), tile([P, n], U8, f"gs{e}{sn}{c0}")
            for q in range(c0 // P, (c0 + n) // P):
                g_codes[e, sn, q] = codes[:, q * P - c0 : (q + 1) * P - c0]
                g_scales[e, sn, q] = scales[:, q * P - c0 : (q + 1) * P - c0]
            nc.vector.quantize_mx(out=codes[:].bitcast(E5M2), scales=scales[:], in_=woven[:, PACK * (c0 - first) : PACK * (c0 + n - first)])

        def permute_words(move, e, sn, words):
            w2_t[e, sn] = words
            move(
                out=words[:].bitcast(U16).rearrange("p (s t m) -> p s t m", s=SI, t=PACK),
                in_=w2_raw[e, sn][:].bitcast(U16).rearrange("p (s m t) -> p s t m", s=SI, t=PACK),
            )

        def permute_scales(move, e, first, n, name):
            planes = tile([P, n, H], U8, name)
            for x in range(n):
                w2s_t[e, first + x] = planes[:, x, :]
            move(
                out=planes[:].rearrange("p n (s t m) -> p (n s) t m", s=SI, t=PACK),
                in_=w2s_raw[e][:, first : first + n, :].rearrange("p n (s m t) -> p (n s) t m", s=SI, t=PACK),
            )

        def slope_input(e, si, q):
            return a_t[e, q // 2, si][:, :, q % 2 * P : (q % 2 + 1) * P]

        def rectify(e, si, q, n, name):
            planes = tile([P, PACK, n * P], F32, name)
            for x in range(n):
                rectified[e, si, q + x] = planes[:, :, x * P : (x + 1) * P]
            nc.gpsimd.tensor_scalar(planes[:], a_t[e, q // 2, si][:, :, q % 2 * P : (q % 2 + n) * P], F32_MAX, 0.0, ALU.min, ALU.max)

        def first_product(e, si, q, sn, bank=None):
            if sn == 0:
                dh_bank[e, si, q] = bank_tile([P, PACK, P], bank)
            for t in range(PACK):
                col = si * PASS + t * P
                nc.tensor.matmul_mx(
                    out=dh_bank[e, si, q][:, t, :],
                    lhsT=w2_t[e, sn][:, 2 * col : 2 * (col + P)].bitcast(E2M1),
                    lhsT_scale=w2s_t[e, sn][:, col : col + P],
                    rhs=g_codes[e, sn, q].bitcast(E5M2),
                    rhs_scale=g_scales[e, sn, q],
                    start=(sn == 0 and t == 0),
                    stop=(sn == SN - 1 and t == PACK - 1),
                )

        def derive(e, si, q, name=None):
            first, n = piece[e, q]
            if (e, first) not in da_woven:
                da_woven[e, first] = tile([P, SI, n * PASS], BF16, name or f"daw{e}{first}")
            woven = da_woven[e, first][:, si, (q - first) * PASS : (q - first + 1) * PASS]
            if (e, si, q) in rectified:
                nc.vector.tensor_tensor(
                    woven.rearrange("p (c v t) -> p c t v", v=2, t=PACK),
                    rectified[e, si, q].rearrange("p t (c v) -> p c t v", v=2),
                    dh_bank[e, si, q][:].rearrange("p t (c v) -> p c t v", v=2),
                    ALU.mult,
                )
                return
            nc.vector.scalar_tensor_tensor(
                woven.rearrange("p (c t) -> p c t", t=PACK),
                slope_input(e, si, q).rearrange("p t c -> p c t"),
                0.0,
                dh_bank[e, si, q][:].rearrange("p t c -> p c t"),
                ALU.max,
                ALU.mult,
            )

        def quantize_da(e, q, name=None):
            n = piece[e, q][1] * P
            da_codes[e, q] = tile([P, SI, n], U32, name or f"dc{e}{q}")[:]
            da_scales[e, q] = tile([P, SI, n], U8, f"ds{e}{q}")
            nc.vector.quantize_mx(
                out=da_codes[e, q][:].rearrange("p s c -> p (s c)").bitcast(E5M2),
                scales=da_scales[e, q][:].rearrange("p s c -> p (s c)"),
                in_=da_woven[e, q][:].rearrange("p s c -> p (s c)"),
            )

        def second_product(e, q, k, dx_bank):
            for si in range(SI):
                nc.tensor.matmul_mx(
                    out=dx_bank,
                    lhsT=w1_t[:, e * SI + si, 2 * k * P : 2 * (k + 1) * P].bitcast(E2M1),
                    lhsT_scale=w1s_t[:, e * SI + si, k * P : (k + 1) * P],
                    rhs=da_codes[e, q][:, si, :].bitcast(E5M2),
                    rhs_scale=da_scales[e, q][:, si, :],
                    start=(si == 0),
                    stop=(si == SI - 1),
                )

        def scatter_on_scalar(dx, e, c0, n, k):
            nc.scalar.activation(windows[k][:].indirect(slots(c0, n, e)), dx, COPY)

        def scatter_on_vector(dx, e, c0, n, k):
            nc.vector.tensor_copy(windows[k][:].indirect(slots(c0, n, e)), dx)

        def products(e, q, bank):
            dx_bank = bank_tile([P, KT, da_codes[e, q].shape[2]], bank)
            for k in range(KT):
                second_product(e, q, k, dx_bank[:, k, :])
            return dx_bank

        def back_on_scalar(e, q, bank, name):
            dx_bank = products(e, q, bank)
            n = da_codes[e, q].shape[2]
            dx = tile([P, KT, n], F32, name)
            for k in (1, 0):
                nc.scalar.activation(dx[:, k, :], dx_bank[:, k, :], COPY, scale=2.0)
            for k in (1, 0):
                scatter_on_scalar(dx[:, k, :], e, q * P, n, k)

        def both_passes(e, si, q, bank):
            for sn in range(SN):
                first_product(e, si, q, sn, bank)

        order = [(si, q) for q in range(Q) for si in range(SI)]

        gather_on_vector(0, 0, 0)
        gather_on_scalar(0, 0, 0, C, C)
        turned = bank_tile([P, P], 0)
        nc.tensor.transpose(turned[:], gate_rows[:], identity[:])
        nc.vector.tensor_copy(gate_cols[:], turned[:, 0 : E * Q])
        gate_t = [bank_tile([P, C], 6 + e) for e in range(E)]
        for e in range(E):
            for q in range(Q):
                j = e * Q + q
                nc.tensor.transpose(gate_t[e][:, q * P : (q + 1) * P], gate_cols[:, j : j + 1].to_broadcast([P, P]), identity[:])
        for t in range(1, PACK - 1):
            gather_on_vector(0, 0, t)
            gather_on_scalar(0, 0, t, C, C)
        gather_on_vector(0, 0, 3, 0, 3 * P)
        gather_on_scalar(0, 0, 3, 3 * P, C + P)
        permute_words(nc.gpsimd.tensor_copy, 0, 0, tile([P, 2 * H], U8, "w200"))
        permute_scales(nc.gpsimd.tensor_copy, 0, 0, SN, "w2s0")
        weave(0, 0, 0, 3 * P, "gw00", C)
        weave(0, 0, 3 * P, C)
        weave(1, 0, 0, C, "gw10")
        for e in range(E):
            quantize_g(e, 0, 0, C, f"gc{e}0")
        permute_words(nc.gpsimd.tensor_copy, 0, 1, tile([P, 2 * H], U8, "gw10"))
        for x, (si, q) in enumerate(order[:6]):
            first_product(0, si, q, 0, x)

        for t in range(PACK - 1):
            gather_on_scalar(0, 1, t)
        for half in range(2):
            gather_on_scalar(0, 1, 3, half * HALF, HALF)
        weave(0, 1, 0, HALF, "gw010")
        weave(0, 1, HALF, 3 * P, "gw011", HALF)
        quantize_g(0, 1, 0, HALF, "gc010")
        g[1, 1] = tile([P, PACK, C], F32, "w2raw01")[:]
        for t in range(PACK):
            gather_on_scalar(1, 1, t)
        permute_words(nc.scalar.copy, 1, 0, tile([P, 2 * H], U8, "w210"))
        weave(0, 1, 3 * P, C)
        permute_scales(nc.gpsimd.tensor_copy, 1, 0, SN, "w2s1")

        across = (0, 2, 1, 3)
        for x in across:
            first_product(0, *order[x], 1)
        for x in across:
            derive(0, *order[x])
        for x in (6, 7):
            first_product(0, *order[x], 0, 2 * (x - 6))
        quantize_g(0, 1, HALF, HALF, "a000")
        for x in (4, 6):
            first_product(0, *order[x], 1)
        quantize_da(0, 0)
        back_on_scalar(0, 0, 6, "w2raw10")
        for x in (5, 7):
            first_product(0, *order[x], 1)
        rectify(0, 1, 2, 2, "rect012")
        permute_words(nc.gpsimd.tensor_copy, 1, 1, tile([P, 2 * H], U8, "w211"))
        weave(1, 1, 0, HALF, "gw110")
        for y, bank in ((0, 1), (2, 3)):
            first_product(1, *order[y], 0, bank)
        for x in across:
            derive(0, *order[4 + x])
        for y, bank in ((1, 4), (3, 0), (4, 5)):
            first_product(1, *order[y], 0, bank)
        quantize_g(1, 1, 0, HALF, "a011")
        first_product(1, *order[0], 1)
        quantize_da(0, 2)
        back_on_scalar(0, 2, 2, "dx02")
        for y in across[1:]:
            first_product(1, *order[y], 1)
        first_product(1, *order[6], 0, 6)
        rectify(1, 1, 0, 2, "rect110")

        rectify(1, 0, 2, 1, "rect102")

        weave(1, 1, HALF, C, "gw111")
        for y in across:
            derive(1, *order[y])
        for y, bank in ((5, 1), (7, 3)):
            first_product(1, *order[y], 0, bank)
        quantize_g(1, 1, HALF, HALF, "a101")
        for y in (4, 6):
            first_product(1, *order[y], 1)
        quantize_da(1, 0)
        back_on_scalar(1, 0, 2, "dx10")
        for y in (5, 7):
            first_product(1, *order[y], 1)
        rectify(1, 1, 3, 1, "daw10")
        for y in across:
            derive(1, *order[4 + y])
        last = [bank_tile([P, HALF], bank) for bank in (0, 4)]
        for q in (2, 3):
            quantize_da(1, q)
            for k in (1, 0):
                second_product(1, q, k, last[k][:, (q - 2) * P : (q - 1) * P])
        upper = [tile([P, HALF], F32, name) for name in ("dx_last0", "daw13")]
        for k in (1, 0):
            nc.vector.tensor_scalar(upper[k][:], last[k][:], 2.0, None, ALU.mult)
        scatter_on_vector(upper[1][:], 1, HALF, HALF, 1)
        scatter_on_scalar(upper[0][:], 1, HALF, HALF, 0)
        for k in (1, 0):
            nc.sync.dma_start(out[k * P : (k + 1) * P, :], windows[k][:])
